import numpy as np
import ml_dtypes


def mxq(x, axis, fmt="e4m3"):
    dtype, down = {"e4m3": (ml_dtypes.float8_e4m3fn, 7), "e5m2": (ml_dtypes.float8_e5m2, 14)}[fmt]
    v = np.moveaxis(np.asarray(x, np.float32).astype(ml_dtypes.bfloat16).astype(np.float64), axis, -1)
    blocks = v.reshape(v.shape[:-1] + (-1, 32))
    amax = np.abs(blocks).max(-1, keepdims=True)
    byte = np.maximum(np.where(amax > 0, np.frexp(amax)[1] - 1 + 127, 0) - down, 1)
    scale = np.exp2(byte - 127.0)
    codes = (blocks / scale).astype(np.float32).astype(dtype).astype(np.float64)
    return np.moveaxis((codes * scale).reshape(v.shape), -1, axis)


WIDE = False


def mx_kscale(k):
    if not WIDE:
        return np.ones(k)
    levels = np.array([10, -10, 5, -5, 0])
    if k % 512:
        return np.exp2(np.random.permutation(np.resize(levels, k // 32))).repeat(32)
    a = np.empty((k // 512, 16))
    for p in range(k // 512):
        a[p, :8] = np.random.permutation(np.resize(levels, 8))
        for g in range(8):
            far = levels[np.abs(levels - a[p, g]) >= 10]
            a[p, g + 8] = far[np.random.randint(len(far))]
    return np.exp2(a.ravel()).repeat(32)


def f64(x):
    return np.asarray(x).astype(np.float64)


def striped(idx):
    return np.tile(np.asarray(idx).reshape(-1, 16).T, (8, 1)).astype(np.uint16)


def unstriped(offs):
    return offs[:16].T.reshape(-1).astype(np.int64)


E2M1 = np.array([0.0, 0.5, 1.0, 1.5, 2.0, 3.0, 4.0, 6.0, -0.0, -0.5, -1.0, -1.5, -2.0, -3.0, -4.0, -6.0])


def pack_weight(w, fmt):
    k, n = w.shape
    w = f64(np.asarray(w, np.float32).astype(ml_dtypes.bfloat16)).reshape(k // 32, 32, n)
    amax = np.abs(w).max(1)
    if fmt == "e4m3":
        byte = np.frexp(amax)[1] - 1 + 127 - 7
    else:
        mant, ex = np.frexp(amax / 6.0)
        byte = np.where(mant > 0.5, ex, ex - 1) + 127
    byte = np.clip(np.where(amax > 0, byte, 1), 1, 254)
    scaled = (w * np.exp2(127.0 - byte)[:, None, :]).reshape(k, n).astype(np.float32)
    by_word = np.ascontiguousarray(scaled.reshape(k // 512, 128, 4, n).transpose(0, 1, 3, 2))
    if fmt == "e4m3":
        words = by_word.astype(ml_dtypes.float8_e4m3fn).view(np.uint8)
    else:
        c = by_word.astype(ml_dtypes.float4_e2m1fn).view(np.uint8) & 0xF
        words = (c[..., 0::2] | (c[..., 1::2] << 4)).reshape(k // 512, 128, 2 * n)
    return np.ascontiguousarray(words), np.ascontiguousarray(byte.astype(np.uint8).reshape(k // 512, 16, n))


def unpack_weight(words, scales, fmt):
    g, _, n = scales.shape
    words = np.ascontiguousarray(words).reshape(g, 128, n, -1)
    if fmt == "e4m3":
        vals = words.view(ml_dtypes.float8_e4m3fn).astype(np.float64)
    else:
        nib = np.empty((g, 128, n, 4), np.uint8)
        nib[..., 0::2] = words & 0xF
        nib[..., 1::2] = words >> 4
        vals = E2M1[nib]
    vals = vals * np.repeat(np.exp2(scales.astype(np.float64) - 127.0), 8, axis=1)[..., None]
    return vals.transpose(0, 1, 3, 2).reshape(g * 512, n)


B, N, T, D, DV, NQ = 1, 1024, 2048, 512, 256, 256


def setup_inputs():
    n = np.random.standard_normal
    idx = np.sort(np.random.permutation(T)[:B * N].reshape(B, N), axis=1).reshape(-1)
    s = mx_kscale(D)[:, None]
    u = np.ones(T)
    u[idx] = mx_kscale(B * N)
    r = np.random.uniform(0.5, 2.0, T)
    k = n((D, T)) / s
    v = n((DV, T)) / (u * r)
    kp = pack_weight(k, "e4m3")
    when = np.zeros(T)
    when[idx] = np.sort(np.random.permutation(2 * N)[:B * N])
    return {
        "qT": (n((B, D, NQ)) * s * (1.00 / np.sqrt(D))).astype(np.float32),
        "k_words": kp[0],
        "k_scales": kp[1],
        "vT": v.astype(np.float32),
        "vs": np.tile(u * r, (128, 1)).astype(np.float32),
        "pos": np.tile(when, (128, 1)).astype(np.float32),
        "slope": np.exp2(-np.random.randint(8, 13, (B, NQ, 1))).astype(np.float32),
        "og": n((B, NQ, DV)).astype(np.float32),
        "offs": striped(idx),
    }


def reference(qT, k_words, k_scales, vT, vs, pos, slope, og, offs):
    idx = unstriped(offs)
    k = unpack_weight(k_words, k_scales, "e4m3")
    v = f64(vT)
    pick = lambda x: x[:, idx].reshape(x.shape[0], B, N).transpose(1, 0, 2)
    q = f64(qT)
    score = mxq(q, 1, "e4m3").transpose(0, 2, 1) @ pick(k)
    score = score + f64(slope) * pick(f64(pos))[:, :1, :]
    m = score.max(-1, keepdims=True)
    p = np.exp(score - m)
    total = p.sum(-1, keepdims=True)
    w = p * pick(f64(vs))[:, :1, :]
    y = mxq(w, 2, "e4m3") @ mxq(pick(v).transpose(0, 2, 1), 1, "e4m3")
    y = y / total
    y = y / (1.0 + np.exp(-f64(og)))
    return y

@@ -1,0 +1,208 @@
+from contextlib import ExitStack
+
+import concourse.mybir as mybir
+from concourse.masks import make_identity
+
+N, T, D, DV, NQ = 1024, 2048, 512, 256, 256
+FLOPS = 2 * NQ * N * D + 2 * NQ * N * DV
+
+F32 = mybir.dt.float32
+BF16 = mybir.dt.bfloat16
+I32 = mybir.dt.int32
+U32 = mybir.dt.uint32
+U16 = mybir.dt.uint16
+U8 = mybir.dt.uint8
+FP8X4 = mybir.dt.float8_e4m3fn_x4
+ALU = mybir.AluOpType
+ACT = mybir.ActivationFunctionType
+AX = mybir.AxisListType
+
+P = 128
+PASS = 512
+BT_ENGINE = "gpsimd"
+V0_ON_SCALAR = True
+
+
+def tile_attend_soft_alibi_gate_srtq256n1024t2048_kernel(tc, qT, k_words, k_scales, vT, vs, pos, slope, og, offs, out):
+    nc = tc.nc
+    with ExitStack() as ctx:
+        keep = ctx.enter_context(tc.tile_pool(name="keep", bufs=1))
+        sbank = ctx.enter_context(tc.psum_pool(name="sbank", bufs=1))
+        work = ctx.enter_context(tc.psum_pool(name="work", bufs=4))
+
+        offsets = keep.tile([P, N // 16], U16, name="offsets")
+        q_raw = keep.tile([P, 4, NQ], F32, name="q_raw")
+        slope_col = keep.tile([P, 2], F32, name="slope_col")
+        pos_win = keep.tile([P, T], F32, name="pos_win")
+        vs_win = keep.tile([P, T], F32, name="vs_win")
+        ks_win = keep.tile([P, T], U8, name="ks_win")
+        late = ctx.enter_context(tc.tile_pool(name="late", bufs=1))
+        warm = late.tile([P, 3 * T + 2 * DV], F32, name="warm", offset=0)
+        kw_win = late.tile([P, T], I32, name="kw_win", offset=0)
+        v_win = [late.tile([P, T], F32, name=f"v_win{f}", offset=4 * T * (f + 1)) for f in range(2)]
+        og_sb = late.tile([P, 2, DV], F32, name="og_sb", offset=4 * T * 3)
+        ident = keep.tile([P, P], F32, name="ident")
+
+        nc.vector.memset(ks_win[:].bitcast(I32), 0)
+        nc.vector.memset(pos_win[:], 0.0)
+        nc.vector.memset(vs_win[:], 0.0)
+        make_identity(nc, ident[:])
+
+        nc.sync.dma_start(offsets[:], offs)
+        nc.sync.dma_start(out=slope_col[:], in_=slope[0].rearrange("(p h) o -> p (h o)", h=2))
+        nc.sync.dma_start(out=q_raw[:], in_=qT[0].rearrange("(p j) w -> p j w", j=4))
+        ks_hbm = k_scales[0].bitcast(I32)
+        for quad in range(4):
+            nc.scalar.dma_start(out=ks_win[32 * quad : 32 * quad + 4, :].bitcast(I32), in_=ks_hbm[4 * quad : 4 * quad + 4, :])
+        nc.scalar.dma_start(out=pos_win[0:1, :], in_=pos[0:1, :])
+        nc.scalar.activation(out=warm[32:64, 0:1], in_=pos_win[32:64, 0:1], func=ACT.Exp)
+        nc.scalar.dma_start(out=vs_win[0:1, :], in_=vs[0:1, :])
+        nc.sync.dma_start(out=kw_win[:], in_=k_words[0].rearrange("p t r -> p (t r)").bitcast(I32))
+        for half in range(2):
+            cols = slice(half * T // 2, (half + 1) * T // 2)
+            nc.sync.dma_start(out=v_win[0][:, cols], in_=vT[0:P, cols])
+        nc.sync.dma_start(out=v_win[1][:], in_=vT[P : 2 * P, :])
+        nc.sync.dma_start(out=og_sb[:], in_=og[0].rearrange("(h p) e -> p h e", p=P))
+
+        slope_ps = work.tile([P, 2, P], F32, name="slope_ps", tag="work")
+        for h in range(2):
+            nc.tensor.transpose(slope_ps[:, h, :], slope_col[:, h : h + 1].to_broadcast([P, P]), ident[:])
+        slope_row = keep.tile([P, P, 2], F32, name="slope_row")
+        nc.scalar.copy(out=slope_row[:], in_=slope_ps[:].rearrange("p h n -> p n h"))
+
+        pos_g = keep.tile([P, N], F32, name="pos_g")
+        for g in range(2):
+            nc.vector.tensor_copy(pos_g[:, g * PASS : (g + 1) * PASS], pos_win[:].indirect(offsets[:, 32 * g : 32 * (g + 1)]))
+        ks_g = keep.tile([P, N], U8, name="ks_g", align_bytes=64)
+        nc.vector.tensor_copy(ks_g[:], ks_win[:].indirect(offsets[:]))
+
+        q_bf = keep.tile([P, NQ, 4], BF16, name="q_bf", align_bytes=64)
+        nc.scalar.copy(out=q_bf[:], in_=q_raw[:].rearrange("p j w -> p w j"))
+        q_codes = keep.tile([P, NQ], U32, name="q_codes", align_bytes=64)
+        q_scales = keep.tile([P, NQ], U8, name="q_scales", align_bytes=64)
+        nc.vector.quantize_mx(out=q_codes[:].bitcast(FP8X4), scales=q_scales[:], in_=q_bf[:].rearrange("p w j -> p (w j)"))
+
+        pos_col = keep.tile([P, 8], F32, name="pos_col")
+        for g in range(2):
+            pos_ps = work.tile([P, 4, P], F32, name=f"pos_ps{g}", tag="work")
+            for c in range(4):
+                nc.tensor.transpose(pos_ps[:, c, :], pos_g[:, g * PASS + c * P : g * PASS + (c + 1) * P], ident[:])
+            nc.scalar.copy(out=pos_col[:, 4 * g : 4 * g + 4], in_=pos_ps[:, :, 0])
+
+        kw_g = keep.tile([P, N], U32, name="kw_g", align_bytes=64)
+        for g in range(2):
+            nc.vector.tensor_copy(kw_g[:, g * PASS : (g + 1) * PASS], kw_win[:].bitcast(U32).indirect(offsets[:, 32 * g : 32 * (g + 1)]))
+
+        bias_t = [keep.tile([P, NQ], F32, name=f"bias_t{c}") for c in range(8)]
+        slope_flat = slope_row[:].rearrange("p n h -> p (n h)")
+        for c in range(8):
+            if BT_ENGINE == "scalar":
+                nc.scalar.activation(out=bias_t[c][:], in_=slope_flat, func=ACT.Copy, scale=pos_col[:, c : c + 1])
+            elif BT_ENGINE == "gpsimd":
+                nc.gpsimd.tensor_scalar(bias_t[c][:], slope_flat, pos_col[:, c : c + 1], 0.0, ALU.mult, ALU.add)
+            else:
+                nc.vector.tensor_scalar(bias_t[c][:], slope_flat, pos_col[:, c : c + 1], None, ALU.mult)
+
+        s_ps = {}
+        for g in range(2):
+            for h in range(2):
+                s_ps[h, g] = sbank.tile([P, PASS], F32, name=f"s_ps{h}{g}", tag=f"s{h}{g}")
+                for c in range(4):
+                    nc.tensor.matmul(s_ps[h, g][:, c * P : (c + 1) * P], lhsT=bias_t[4 * g + c][:, h * P : (h + 1) * P], rhs=ident[:],
+                                     start=(c == 0), stop=False, is_transpose=True)
+
+        a_sb = {}
+        for g in range(2):
+            for h in range(2):
+                a_ps = work.tile([P, 4, P], F32, name=f"a_ps{h}{g}", tag="work")
+                for c in range(4):
+                    keys = slice(g * PASS + c * P, g * PASS + (c + 1) * P)
+                    qs = slice(h * P, (h + 1) * P)
+                    nc.tensor.matmul_mx(out=a_ps[:, c, :], lhsT=kw_g[:, keys].bitcast(FP8X4), lhsT_scale=ks_g[:, keys],
+                                        rhs=q_codes[:, qs].bitcast(FP8X4), rhs_scale=q_scales[:, qs], start=True, stop=True)
+                a_sb[h, g] = keep.tile([P, 4, P], F32, name=f"a_sb{h}{g}")
+                nc.scalar.copy(out=a_sb[h, g][:], in_=a_ps[:])
+        for g in range(2):
+            for h in range(2):
+                for c in range(4):
+                    nc.tensor.matmul(s_ps[h, g][:, c * P : (c + 1) * P], lhsT=a_sb[h, g][:, c, :], rhs=ident[:],
+                                     start=False, stop=(c == 3), is_transpose=True)
+
+        vs_g = keep.tile([P, N], F32, name="vs_g")
+        nc.vector.tensor_copy(vs_g[:], vs_win[:].indirect(offsets[:]))
+        vs_ps = work.tile([P, PASS], F32, name="vs_ps", tag="work")
+        for g in range(2):
+            for t in range(4):
+                c = 4 * g + t
+                nc.tensor.transpose(vs_ps[:, 2 * c : 2 * c + P], vs_g[:, g * PASS + t : (g + 1) * PASS : 4], ident[:])
+        vs_col = keep.tile([P, 2, 4], F32, name="vs_col")
+        nc.scalar.copy(out=vs_col[:].rearrange("p g t -> p (g t)"), in_=vs_ps[:, 0:16:2])
+
+        half_max = [keep.tile([P, 2], F32, name=f"half_max{h}") for h in range(2)]
+        neg_max = [keep.tile([P, 1], F32, name=f"neg_max{h}") for h in range(2)]
+        half_sum = [keep.tile([P, 2], F32, name=f"half_sum{h}") for h in range(2)]
+        p_sb = {}
+        for h in range(2):
+            for g in range(2):
+                nc.vector.tensor_reduce(out=half_max[h][:, g : g + 1], in_=s_ps[h, g][:], axis=AX.X, op=ALU.max)
+            nc.vector.tensor_scalar(neg_max[h][:], half_max[h][:, 0:1], half_max[h][:, 1:2], -1.0, ALU.max, ALU.mult)
+            for g in range(2):
+                p_sb[h, g] = keep.tile([P, 4, P], F32, name=f"p_sb{h}{g}")
+                nc.scalar.activation(out=p_sb[h, g][:].rearrange("p t s -> p s t"), in_=s_ps[h, g][:].rearrange("p (s t) -> p s t", t=4),
+                                     func=ACT.Exp, bias=neg_max[h][:], accum_out=half_sum[h][:, g : g + 1])
+
+        v_bf = keep.tile([P, 2, DV, 4], BF16, name="v_bf", align_bytes=64)
+        v_words = v_bf[:].rearrange("p g c t -> p (g c t)").bitcast(F32).rearrange("p (g c u) -> p g c u", g=2, u=2)
+        for f in (1, 0):
+            v_g = keep.tile([P, 2, 2 * P, 2], BF16, name=f"v_g{f}")
+            if f == 0 and V0_ON_SCALAR:
+                v_cast = keep.tile([P, T], BF16, name="v_cast")
+                for half in range(2):
+                    cols = slice(half * T // 2, (half + 1) * T // 2)
+                    nc.scalar.activation(out=v_cast[:, cols], in_=v_win[0][:, cols], func=ACT.Copy)
+                nc.scalar.activation(out=v_g[:].rearrange("p u s e -> p s u e"), in_=v_cast[:].indirect(offsets[:]), func=ACT.Copy)
+            else:
+                nc.vector.tensor_copy(v_g[:].rearrange("p u s e -> p s u e"), v_win[f][:].indirect(offsets[:]))
+            pairs = v_g[:].rearrange("p u s e -> p (u s e)").bitcast(F32)
+            vt_ps = work.tile([P, 2, 2, P], F32, name=f"vt_ps{f}", tag="work")
+            for g in range(2):
+                for u in range(2):
+                    nc.tensor.transpose(vt_ps[:, g, u, :], pairs[:, 2 * P * u + P * g : 2 * P * u + P * (g + 1)], ident[:])
+            nc.scalar.copy(out=v_words[:, :, f * P : (f + 1) * P, :], in_=vt_ps[:].rearrange("p g u c -> p g c u"))
+        v_codes = keep.tile([P, 2, DV], U32, name="v_codes", align_bytes=64)
+        v_scales = keep.tile([P, 2, DV], U8, name="v_scales", align_bytes=64)
+
+        gate = keep.tile([P, 2, DV], F32, name="gate")
+        nc.scalar.activation(out=gate[:], in_=og_sb[:], func=ACT.Tanh, scale=0.5)
+
+        w_codes, w_scales = {}, {}
+        for h in range(2):
+            for g in range(2):
+                pt_ps = work.tile([P, 4, P], F32, name=f"pt_ps{h}{g}", tag="work")
+                for t in range(4):
+                    nc.tensor.transpose(pt_ps[:, t, :], p_sb[h, g][:, t, :], ident[:])
+                w_bf = keep.tile([P, P, 4], BF16, name=f"w_bf{h}{g}", align_bytes=64)
+                nc.vector.tensor_tensor(w_bf[:], pt_ps[:].rearrange("p t q -> p q t"),
+                                        vs_col[:, g, :].unsqueeze(1).to_broadcast([P, P, 4]), ALU.mult)
+                w_codes[h, g] = keep.tile([P, P], U32, name=f"w_codes{h}{g}", align_bytes=64)
+                w_scales[h, g] = keep.tile([P, P], U8, name=f"w_scales{h}{g}", align_bytes=64)
+                nc.vector.quantize_mx(out=w_codes[h, g][:].bitcast(FP8X4), scales=w_scales[h, g][:], in_=w_bf[:].rearrange("p q t -> p (q t)"))
+            if h == 0:
+                for g in range(2):
+                    nc.vector.quantize_mx(out=v_codes[:, g, :].bitcast(FP8X4), scales=v_scales[:, g, :],
+                                          in_=v_bf[:, g, :, :].rearrange("p c t -> p (c t)"))
+
+            twice_sum = keep.tile([P, 1], F32, name=f"twice_sum{h}")
+            nc.vector.tensor_scalar(twice_sum[:], half_sum[h][:, 0:1], half_sum[h][:, 1:2], 2.0, ALU.add, ALU.mult)
+            inv = keep.tile([P, 1], F32, name=f"inv{h}")
+            nc.vector.reciprocal(inv[:], twice_sum[:])
+            factor = keep.tile([P, DV], F32, name=f"factor{h}")
+            nc.scalar.activation(out=factor[:], in_=gate[:, h, :], func=ACT.Identity, scale=inv[:], bias=inv[:])
+
+            y_ps = sbank.tile([P, DV], F32, name=f"y_ps{h}", tag=f"s{h}0")
+            for g in range(2):
+                nc.tensor.matmul_mx(out=y_ps[:], lhsT=w_codes[h, g][:].bitcast(FP8X4), lhsT_scale=w_scales[h, g][:],
+                                    rhs=v_codes[:, g, :].bitcast(FP8X4), rhs_scale=v_scales[:, g, :], start=(g == 0), stop=(g == 1))
+            res = keep.tile([P, DV], F32, name=f"res{h}")
+            nc.vector.tensor_tensor(res[:], y_ps[:], factor[:], ALU.mult)
+            nc.sync.dma_start(out=out[0, h * P : (h + 1) * P, :], in_=res[:])

@@ -19,29 +19,32 @@ AX = mybir.AxisListType
 
 P = 128
 PASS = 512
-BT_ENGINE = "gpsimd"
-V0_ON_SCALAR = True
 
 
 def tile_attend_soft_alibi_gate_srtq256n1024t2048_kernel(tc, qT, k_words, k_scales, vT, vs, pos, slope, og, offs, out):
     nc = tc.nc
     with ExitStack() as ctx:
         keep = ctx.enter_context(tc.tile_pool(name="keep", bufs=1))
-        sbank = ctx.enter_context(tc.psum_pool(name="sbank", bufs=1))
-        work = ctx.enter_context(tc.psum_pool(name="work", bufs=4))
+        late = ctx.enter_context(tc.tile_pool(name="late", bufs=1))
+        psum = ctx.enter_context(tc.psum_pool(name="psum", bufs=8))
 
         offsets = keep.tile([P, N // 16], U16, name="offsets")
         q_raw = keep.tile([P, 4, NQ], F32, name="q_raw")
-        slope_col = keep.tile([P, 2], F32, name="slope_col")
         pos_win = keep.tile([P, T], F32, name="pos_win")
-        vs_win = keep.tile([P, T], F32, name="vs_win")
         ks_win = keep.tile([P, T], U8, name="ks_win")
-        late = ctx.enter_context(tc.tile_pool(name="late", bufs=1))
-        warm = late.tile([P, 3 * T + 2 * DV], F32, name="warm", offset=0)
+        warm = late.tile([P, 3 * T + 2 * DV + 16], F32, name="warm", offset=0)
         kw_win = late.tile([P, T], I32, name="kw_win", offset=0)
         v_win = [late.tile([P, T], F32, name=f"v_win{f}", offset=4 * T * (f + 1)) for f in range(2)]
+        vs_win = keep.tile([P, T], F32, name="vs_win")
         og_sb = late.tile([P, 2, DV], F32, name="og_sb", offset=4 * T * 3)
+        slope_col = [late.tile([P, 1], F32, name=f"slope_col{h}", offset=4 * (3 * T + 2 * DV + 8 * h)) for h in range(2)]
         ident = keep.tile([P, P], F32, name="ident")
+
+        def half_list(g):
+            return offsets[:, 32 * g : 32 * (g + 1)]
+
+        def slots(g):
+            return slice(g * PASS, (g + 1) * PASS)
 
         nc.vector.memset(ks_win[:].bitcast(I32), 0)
         nc.vector.memset(pos_win[:], 0.0)
@@ -49,30 +52,25 @@ def tile_attend_soft_alibi_gate_srtq256n1024t2048_kernel(tc, qT, k_words, k_scal
         make_identity(nc, ident[:])
 
         nc.sync.dma_start(offsets[:], offs)
-        nc.sync.dma_start(out=slope_col[:], in_=slope[0].rearrange("(p h) o -> p (h o)", h=2))
         nc.sync.dma_start(out=q_raw[:], in_=qT[0].rearrange("(p j) w -> p j w", j=4))
         ks_hbm = k_scales[0].bitcast(I32)
         for quad in range(4):
             nc.scalar.dma_start(out=ks_win[32 * quad : 32 * quad + 4, :].bitcast(I32), in_=ks_hbm[4 * quad : 4 * quad + 4, :])
         nc.scalar.dma_start(out=pos_win[0:1, :], in_=pos[0:1, :])
         nc.scalar.activation(out=warm[32:64, 0:1], in_=pos_win[32:64, 0:1], func=ACT.Exp)
-        nc.scalar.dma_start(out=vs_win[0:1, :], in_=vs[0:1, :])
         nc.sync.dma_start(out=kw_win[:], in_=k_words[0].rearrange("p t r -> p (t r)").bitcast(I32))
+        for h in range(2):
+            nc.sync.dma_start(out=slope_col[h][:], in_=slope[0, h * P : (h + 1) * P, :])
         for half in range(2):
             cols = slice(half * T // 2, (half + 1) * T // 2)
             nc.sync.dma_start(out=v_win[0][:, cols], in_=vT[0:P, cols])
         nc.sync.dma_start(out=v_win[1][:], in_=vT[P : 2 * P, :])
         nc.sync.dma_start(out=og_sb[:], in_=og[0].rearrange("(h p) e -> p h e", p=P))
-
-        slope_ps = work.tile([P, 2, P], F32, name="slope_ps", tag="work")
-        for h in range(2):
-            nc.tensor.transpose(slope_ps[:, h, :], slope_col[:, h : h + 1].to_broadcast([P, P]), ident[:])
-        slope_row = keep.tile([P, P, 2], F32, name="slope_row")
-        nc.scalar.copy(out=slope_row[:], in_=slope_ps[:].rearrange("p h n -> p n h"))
+        nc.scalar.dma_start(out=vs_win[0:1, :], in_=vs[0:1, :])
 
         pos_g = keep.tile([P, N], F32, name="pos_g")
         for g in range(2):
-            nc.vector.tensor_copy(pos_g[:, g * PASS : (g + 1) * PASS], pos_win[:].indirect(offsets[:, 32 * g : 32 * (g + 1)]))
+            nc.vector.tensor_copy(pos_g[:, slots(g)], pos_win[:].indirect(half_list(g)))
         ks_g = keep.tile([P, N], U8, name="ks_g", align_bytes=64)
         nc.vector.tensor_copy(ks_g[:], ks_win[:].indirect(offsets[:]))
 
@@ -83,88 +81,80 @@ def tile_attend_soft_alibi_gate_srtq256n1024t2048_kernel(tc, qT, k_words, k_scal
         nc.vector.quantize_mx(out=q_codes[:].bitcast(FP8X4), scales=q_scales[:], in_=q_bf[:].rearrange("p w j -> p (w j)"))
 
         pos_col = keep.tile([P, 8], F32, name="pos_col")
+        pos_all = keep.tile([P, N], F32, name="pos_all")
         for g in range(2):
-            pos_ps = work.tile([P, 4, P], F32, name=f"pos_ps{g}", tag="work")
+            pos_ps = psum.tile([P, 4, P], F32, name=f"pos_ps{g}", tag="bank")
             for c in range(4):
                 nc.tensor.transpose(pos_ps[:, c, :], pos_g[:, g * PASS + c * P : g * PASS + (c + 1) * P], ident[:])
             nc.scalar.copy(out=pos_col[:, 4 * g : 4 * g + 4], in_=pos_ps[:, :, 0])
+        for g in range(2):
+            row_ps = psum.tile([P, 4, P], F32, name=f"row_ps{g}", tag="bank")
+            for c in range(4):
+                nc.tensor.transpose(row_ps[:, c, :], pos_col[:, 4 * g + c : 4 * g + c + 1].to_broadcast([P, P]), ident[:])
+            nc.scalar.copy(out=pos_all[:, slots(g)], in_=row_ps[:].rearrange("p c n -> p (c n)"))
 
         kw_g = keep.tile([P, N], U32, name="kw_g", align_bytes=64)
         for g in range(2):
-            nc.vector.tensor_copy(kw_g[:, g * PASS : (g + 1) * PASS], kw_win[:].bitcast(U32).indirect(offsets[:, 32 * g : 32 * (g + 1)]))
+            nc.vector.tensor_copy(kw_g[:, slots(g)], kw_win[:].bitcast(U32).indirect(half_list(g)))
 
-        bias_t = [keep.tile([P, NQ], F32, name=f"bias_t{c}") for c in range(8)]
-        slope_flat = slope_row[:].rearrange("p n h -> p (n h)")
-        for c in range(8):
-            if BT_ENGINE == "scalar":
-                nc.scalar.activation(out=bias_t[c][:], in_=slope_flat, func=ACT.Copy, scale=pos_col[:, c : c + 1])
-            elif BT_ENGINE == "gpsimd":
-                nc.gpsimd.tensor_scalar(bias_t[c][:], slope_flat, pos_col[:, c : c + 1], 0.0, ALU.mult, ALU.add)
-            else:
-                nc.vector.tensor_scalar(bias_t[c][:], slope_flat, pos_col[:, c : c + 1], None, ALU.mult)
-
-        s_ps = {}
+        a_ps = {}
         for g in range(2):
             for h in range(2):
-                s_ps[h, g] = sbank.tile([P, PASS], F32, name=f"s_ps{h}{g}", tag=f"s{h}{g}")
-                for c in range(4):
-                    nc.tensor.matmul(s_ps[h, g][:, c * P : (c + 1) * P], lhsT=bias_t[4 * g + c][:, h * P : (h + 1) * P], rhs=ident[:],
-                                     start=(c == 0), stop=False, is_transpose=True)
+                qs = slice(h * P, (h + 1) * P)
+                a_ps[h, g] = psum.tile([P, PASS], F32, name=f"a_ps{h}{g}", tag="bank")
+                nc.tensor.matmul_mx(out=a_ps[h, g][:], lhsT=q_codes[:, qs].bitcast(FP8X4), lhsT_scale=q_scales[:, qs],
+                                    rhs=kw_g[:, slots(g)].bitcast(FP8X4), rhs_scale=ks_g[:, slots(g)], start=True, stop=True)
 
-        a_sb = {}
-        for g in range(2):
-            for h in range(2):
-                a_ps = work.tile([P, 4, P], F32, name=f"a_ps{h}{g}", tag="work")
-                for c in range(4):
-                    keys = slice(g * PASS + c * P, g * PASS + (c + 1) * P)
-                    qs = slice(h * P, (h + 1) * P)
-                    nc.tensor.matmul_mx(out=a_ps[:, c, :], lhsT=kw_g[:, keys].bitcast(FP8X4), lhsT_scale=ks_g[:, keys],
-                                        rhs=q_codes[:, qs].bitcast(FP8X4), rhs_scale=q_scales[:, qs], start=True, stop=True)
-                a_sb[h, g] = keep.tile([P, 4, P], F32, name=f"a_sb{h}{g}")
-                nc.scalar.copy(out=a_sb[h, g][:], in_=a_ps[:])
-        for g in range(2):
-            for h in range(2):
-                for c in range(4):
-                    nc.tensor.matmul(s_ps[h, g][:, c * P : (c + 1) * P], lhsT=a_sb[h, g][:, c, :], rhs=ident[:],
-                                     start=False, stop=(c == 3), is_transpose=True)
-
-        vs_g = keep.tile([P, N], F32, name="vs_g")
-        nc.vector.tensor_copy(vs_g[:], vs_win[:].indirect(offsets[:]))
-        vs_ps = work.tile([P, PASS], F32, name="vs_ps", tag="work")
-        for g in range(2):
-            for t in range(4):
-                c = 4 * g + t
-                nc.tensor.transpose(vs_ps[:, 2 * c : 2 * c + P], vs_g[:, g * PASS + t : (g + 1) * PASS : 4], ident[:])
-        vs_col = keep.tile([P, 2, 4], F32, name="vs_col")
-        nc.scalar.copy(out=vs_col[:].rearrange("p g t -> p (g t)"), in_=vs_ps[:, 0:16:2])
-
-        half_max = [keep.tile([P, 2], F32, name=f"half_max{h}") for h in range(2)]
+        s_sb = [keep.tile([P, N], F32, name=f"s_sb{h}") for h in range(2)]
         neg_max = [keep.tile([P, 1], F32, name=f"neg_max{h}") for h in range(2)]
         half_sum = [keep.tile([P, 2], F32, name=f"half_sum{h}") for h in range(2)]
         p_sb = {}
-        for h in range(2):
-            for g in range(2):
-                nc.vector.tensor_reduce(out=half_max[h][:, g : g + 1], in_=s_ps[h, g][:], axis=AX.X, op=ALU.max)
-            nc.vector.tensor_scalar(neg_max[h][:], half_max[h][:, 0:1], half_max[h][:, 1:2], -1.0, ALU.max, ALU.mult)
+
+        def add_bias(h, g):
+            nc.vector.scalar_tensor_tensor(out=s_sb[h][:, slots(g)], in0=pos_all[:, slots(g)], scalar=slope_col[h][:],
+                                           in1=a_ps[h, g][:], op0=ALU.mult, op1=ALU.add)
+
+        def softmax(h):
+            nc.vector.tensor_reduce(out=neg_max[h][:], in_=s_sb[h][:], axis=AX.X, op=ALU.max, negate=True)
             for g in range(2):
                 p_sb[h, g] = keep.tile([P, 4, P], F32, name=f"p_sb{h}{g}")
-                nc.scalar.activation(out=p_sb[h, g][:].rearrange("p t s -> p s t"), in_=s_ps[h, g][:].rearrange("p (s t) -> p s t", t=4),
+                nc.scalar.activation(out=p_sb[h, g][:].rearrange("p t s -> p s t"), in_=s_sb[h][:, slots(g)].rearrange("p (s t) -> p s t", t=4),
                                      func=ACT.Exp, bias=neg_max[h][:], accum_out=half_sum[h][:, g : g + 1])
+
+        add_bias(0, 0)
+        add_bias(0, 1)
+        add_bias(1, 0)
+        softmax(0)
+        add_bias(1, 1)
+        vs_g = keep.tile([P, N], F32, name="vs_g")
+        nc.vector.tensor_copy(vs_g[:, slots(0)], vs_win[:].indirect(half_list(0)))
+        softmax(1)
+        nc.vector.tensor_copy(vs_g[:, slots(1)], vs_win[:].indirect(half_list(1)))
+
+        vs_col = keep.tile([P, 2, 4], F32, name="vs_col")
+        for g in range(2):
+            vs_ps = psum.tile([P, 4, P], F32, name=f"vs_ps{g}", tag="bank")
+            for t in range(4):
+                nc.tensor.transpose(vs_ps[:, t, :], vs_g[:, g * PASS + t : (g + 1) * PASS : 4], ident[:])
+            nc.scalar.copy(out=vs_col[:, g, :], in_=vs_ps[:, :, 0])
 
         v_bf = keep.tile([P, 2, DV, 4], BF16, name="v_bf", align_bytes=64)
         v_words = v_bf[:].rearrange("p g c t -> p (g c t)").bitcast(F32).rearrange("p (g c u) -> p g c u", g=2, u=2)
         for f in (1, 0):
             v_g = keep.tile([P, 2, 2 * P, 2], BF16, name=f"v_g{f}")
-            if f == 0 and V0_ON_SCALAR:
+            if f == 0:
                 v_cast = keep.tile([P, T], BF16, name="v_cast")
-                for half in range(2):
-                    cols = slice(half * T // 2, (half + 1) * T // 2)
+                for quarter in range(4):
+                    cols = slice(quarter * T // 4, (quarter + 1) * T // 4)
                     nc.scalar.activation(out=v_cast[:, cols], in_=v_win[0][:, cols], func=ACT.Copy)
-                nc.scalar.activation(out=v_g[:].rearrange("p u s e -> p s u e"), in_=v_cast[:].indirect(offsets[:]), func=ACT.Copy)
+                for g in range(2):
+                    nc.scalar.activation(out=v_g[:, :, g * P : (g + 1) * P, :].rearrange("p u s e -> p s u e"),
+                                         in_=v_cast[:].indirect(half_list(g)), func=ACT.Copy)
             else:
-                nc.vector.tensor_copy(v_g[:].rearrange("p u s e -> p s u e"), v_win[f][:].indirect(offsets[:]))
+                for g in range(2):
+                    nc.vector.tensor_copy(v_g[:, :, g * P : (g + 1) * P, :].rearrange("p u s e -> p s u e"), v_win[f][:].indirect(half_list(g)))
             pairs = v_g[:].rearrange("p u s e -> p (u s e)").bitcast(F32)
-            vt_ps = work.tile([P, 2, 2, P], F32, name=f"vt_ps{f}", tag="work")
+            vt_ps = psum.tile([P, 2, 2, P], F32, name=f"vt_ps{f}", tag="bank")
             for g in range(2):
                 for u in range(2):
                     nc.tensor.transpose(vt_ps[:, g, u, :], pairs[:, 2 * P * u + P * g : 2 * P * u + P * (g + 1)], ident[:])
@@ -175,34 +165,52 @@ def tile_attend_soft_alibi_gate_srtq256n1024t2048_kernel(tc, qT, k_words, k_scal
         gate = keep.tile([P, 2, DV], F32, name="gate")
         nc.scalar.activation(out=gate[:], in_=og_sb[:], func=ACT.Tanh, scale=0.5)
 
-        w_codes, w_scales = {}, {}
-        for h in range(2):
-            for g in range(2):
-                pt_ps = work.tile([P, 4, P], F32, name=f"pt_ps{h}{g}", tag="work")
-                for t in range(4):
-                    nc.tensor.transpose(pt_ps[:, t, :], p_sb[h, g][:, t, :], ident[:])
-                w_bf = keep.tile([P, P, 4], BF16, name=f"w_bf{h}{g}", align_bytes=64)
-                nc.vector.tensor_tensor(w_bf[:], pt_ps[:].rearrange("p t q -> p q t"),
-                                        vs_col[:, g, :].unsqueeze(1).to_broadcast([P, P, 4]), ALU.mult)
-                w_codes[h, g] = keep.tile([P, P], U32, name=f"w_codes{h}{g}", align_bytes=64)
-                w_scales[h, g] = keep.tile([P, P], U8, name=f"w_scales{h}{g}", align_bytes=64)
-                nc.vector.quantize_mx(out=w_codes[h, g][:].bitcast(FP8X4), scales=w_scales[h, g][:], in_=w_bf[:].rearrange("p q t -> p (q t)"))
-            if h == 0:
-                for g in range(2):
-                    nc.vector.quantize_mx(out=v_codes[:, g, :].bitcast(FP8X4), scales=v_scales[:, g, :],
-                                          in_=v_bf[:, g, :, :].rearrange("p c t -> p (c t)"))
+        w_bf, w_codes, w_scales = {}, {}, {}
 
+        def weigh(h, g):
+            pt_ps = psum.tile([P, 4, P], F32, name=f"pt_ps{h}{g}", tag="bank")
+            for t in range(4):
+                nc.tensor.transpose(pt_ps[:, t, :], p_sb[h, g][:, t, :], ident[:])
+            w_bf[h, g] = keep.tile([P, P, 4], BF16, name=f"w_bf{h}{g}", align_bytes=64)
+            nc.vector.tensor_tensor(w_bf[h, g][:], pt_ps[:].rearrange("p t q -> p q t"),
+                                    vs_col[:, g, :].unsqueeze(1).to_broadcast([P, P, 4]), ALU.mult)
+
+        def quantize_w(h, g):
+            w_codes[h, g] = keep.tile([P, P], U32, name=f"w_codes{h}{g}", align_bytes=64)
+            w_scales[h, g] = keep.tile([P, P], U8, name=f"w_scales{h}{g}", align_bytes=64)
+            nc.vector.quantize_mx(out=w_codes[h, g][:].bitcast(FP8X4), scales=w_scales[h, g][:], in_=w_bf[h, g][:].rearrange("p q t -> p (q t)"))
+
+        factor = {}
+
+        def make_factor(h):
             twice_sum = keep.tile([P, 1], F32, name=f"twice_sum{h}")
             nc.vector.tensor_scalar(twice_sum[:], half_sum[h][:, 0:1], half_sum[h][:, 1:2], 2.0, ALU.add, ALU.mult)
             inv = keep.tile([P, 1], F32, name=f"inv{h}")
             nc.vector.reciprocal(inv[:], twice_sum[:])
-            factor = keep.tile([P, DV], F32, name=f"factor{h}")
-            nc.scalar.activation(out=factor[:], in_=gate[:, h, :], func=ACT.Identity, scale=inv[:], bias=inv[:])
+            factor[h] = keep.tile([P, DV], F32, name=f"factor{h}")
+            nc.scalar.activation(out=factor[h][:], in_=gate[:, h, :], func=ACT.Identity, scale=inv[:], bias=inv[:])
 
-            y_ps = sbank.tile([P, DV], F32, name=f"y_ps{h}", tag=f"s{h}0")
+        def finish(h):
+            y_ps = psum.tile([P, DV], F32, name=f"y_ps{h}", tag="bank")
             for g in range(2):
                 nc.tensor.matmul_mx(out=y_ps[:], lhsT=w_codes[h, g][:].bitcast(FP8X4), lhsT_scale=w_scales[h, g][:],
                                     rhs=v_codes[:, g, :].bitcast(FP8X4), rhs_scale=v_scales[:, g, :], start=(g == 0), stop=(g == 1))
             res = keep.tile([P, DV], F32, name=f"res{h}")
-            nc.vector.tensor_tensor(res[:], y_ps[:], factor[:], ALU.mult)
+            nc.vector.tensor_tensor(res[:], y_ps[:], factor[h][:], ALU.mult)
             nc.sync.dma_start(out=out[0, h * P : (h + 1) * P, :], in_=res[:])
+
+        weigh(0, 0)
+        weigh(0, 1)
+        quantize_w(0, 0)
+        for g in range(2):
+            nc.vector.quantize_mx(out=v_codes[:, g, :].bitcast(FP8X4), scales=v_scales[:, g, :],
+                                  in_=v_bf[:, g, :, :].rearrange("p c t -> p (c t)"))
+        quantize_w(0, 1)
+        make_factor(0)
+        weigh(1, 0)
+        finish(0)
+        weigh(1, 1)
+        quantize_w(1, 0)
+        make_factor(1)
+        quantize_w(1, 1)
+        finish(1)

@@ -19,6 +19,7 @@ AX = mybir.AxisListType
 
 P = 128
 PASS = 512
+BANK_OF = {"pos_ps0":0,"pos_ps1":1,"row_ps0":2,"row_ps1":3,"a_ps00":4,"a_ps10":5,"a_ps01":2,"a_ps11":3,"vt_ps0":6,"vt_ps1":7,"vs_ps0":4,"vs_ps1":5,"pt_ps00":0,"pt_ps01":1,"pt_ps10":2,"pt_ps11":3,"y_ps0":4,"y_ps1":5}
 
 
 def tile_attend_soft_alibi_gate_srtq256n1024t2048_kernel(tc, qT, k_words, k_scales, vT, vs, pos, slope, og, offs, out):
@@ -26,25 +27,63 @@ def tile_attend_soft_alibi_gate_srtq256n1024t2048_kernel(tc, qT, k_words, k_scal
     with ExitStack() as ctx:
         keep = ctx.enter_context(tc.tile_pool(name="keep", bufs=1))
         late = ctx.enter_context(tc.tile_pool(name="late", bufs=1))
-        psum = ctx.enter_context(tc.psum_pool(name="psum", bufs=8))
+        psum = ctx.enter_context(tc.psum_pool(name="psum", bufs=1))
+        reuse = ctx.enter_context(tc.tile_pool(name="reuse", bufs=1))
 
         offsets = keep.tile([P, N // 16], U16, name="offsets")
         q_raw = keep.tile([P, 4, NQ], F32, name="q_raw")
         pos_win = keep.tile([P, T], F32, name="pos_win")
+        vs_win = keep.tile([P, T], F32, name="vs_win")
         ks_win = keep.tile([P, T], U8, name="ks_win")
         warm = late.tile([P, 3 * T + 2 * DV + 16], F32, name="warm", offset=0)
         kw_win = late.tile([P, T], I32, name="kw_win", offset=0)
         v_win = [late.tile([P, T], F32, name=f"v_win{f}", offset=4 * T * (f + 1)) for f in range(2)]
-        vs_win = keep.tile([P, T], F32, name="vs_win")
         og_sb = late.tile([P, 2, DV], F32, name="og_sb", offset=4 * T * 3)
         slope_col = [late.tile([P, 1], F32, name=f"slope_col{h}", offset=4 * (3 * T + 2 * DV + 8 * h)) for h in range(2)]
         ident = keep.tile([P, P], F32, name="ident")
+
+        pos_g = keep.tile([P, N], F32, name="pos_g")
+        vs_g = keep.tile([P, N], F32, name="vs_g")
+        ks_g = keep.tile([P, N], U8, name="ks_g", align_bytes=64)
+        kw_g = keep.tile([P, N], U32, name="kw_g", align_bytes=64)
+        q_bf = keep.tile([P, NQ, 4], BF16, name="q_bf", align_bytes=64)
+        q_codes = keep.tile([P, NQ], U32, name="q_codes", align_bytes=64)
+        q_scales = keep.tile([P, NQ], U8, name="q_scales", align_bytes=64)
+        pos_col = reuse.tile([P, 2, 4], F32, name="pos_col", offset=0)
+        pos_all = keep.tile([P, N], F32, name="pos_all")
+        vs_col = late.tile([P, 2, 4], F32, name="vs_col", offset=4 * T * 2)
+        s_sb = [keep.tile([P, N], F32, name=f"s_sb{h}") for h in range(2)]
+        neg_max = [keep.tile([P, 1], F32, name=f"neg_max{h}") for h in range(2)]
+        half_sum = [keep.tile([P, 2], F32, name=f"half_sum{h}") for h in range(2)]
+        p_sb = [reuse.tile([P, 2, 4, P], F32, name=f"p_sb{h}", offset=2 * T * (h + 1)) for h in range(2)]
+        v_cast = [reuse.tile([P, T], BF16, name=f"v_cast{f}", offset=2 * T * f) for f in range(2)]
+        v_g = [keep.tile([P, 2, 2 * P, 2], BF16, name=f"v_g{f}") for f in range(2)]
+        v_bf = keep.tile([P, 2, DV, 4], BF16, name="v_bf", align_bytes=64)
+        v_words = v_bf[:].rearrange("p g c t -> p (g c t)").bitcast(F32).rearrange("p (g c u) -> p g c u", g=2, u=2)
+        v_codes = keep.tile([P, 2, DV], U32, name="v_codes", align_bytes=64)
+        v_scales = keep.tile([P, 2, DV], U8, name="v_scales", align_bytes=64)
+        gate = keep.tile([P, 2, DV], F32, name="gate")
+        w_bf = [keep.tile([P, 2, P, 4], BF16, name=f"w_bf{h}", align_bytes=64) for h in range(2)]
+        w_codes = [keep.tile([P, 2, P], U32, name=f"w_codes{h}", align_bytes=64) for h in range(2)]
+        w_scales = [keep.tile([P, 2, P], U8, name=f"w_scales{h}", align_bytes=64) for h in range(2)]
+        twice_sum = [keep.tile([P, 1], F32, name=f"twice_sum{h}") for h in range(2)]
+        inv = [keep.tile([P, 1], F32, name=f"inv{h}") for h in range(2)]
+        factor = [keep.tile([P, DV], F32, name=f"factor{h}") for h in range(2)]
+        res = [keep.tile([P, DV], F32, name=f"res{h}") for h in range(2)]
+        bank = {}
+
+        def new_bank(key, shape):
+            bank[key] = psum.tile(shape, F32, name=key, tag=f"bank{BANK_OF[key]}")
+            return bank[key]
 
         def half_list(g):
             return offsets[:, 32 * g : 32 * (g + 1)]
 
         def slots(g):
             return slice(g * PASS, (g + 1) * PASS)
+
+        def tokens(half):
+            return slice(half * T // 2, (half + 1) * T // 2)
 
         nc.vector.memset(ks_win[:].bitcast(I32), 0)
         nc.vector.memset(pos_win[:], 0.0)
@@ -58,159 +97,211 @@ def tile_attend_soft_alibi_gate_srtq256n1024t2048_kernel(tc, qT, k_words, k_scal
             nc.scalar.dma_start(out=ks_win[32 * quad : 32 * quad + 4, :].bitcast(I32), in_=ks_hbm[4 * quad : 4 * quad + 4, :])
         nc.scalar.dma_start(out=pos_win[0:1, :], in_=pos[0:1, :])
         nc.scalar.activation(out=warm[32:64, 0:1], in_=pos_win[32:64, 0:1], func=ACT.Exp)
+        nc.scalar.dma_start(out=vs_win[0:1, :], in_=vs[0:1, :])
+        for half in range(2):
+            nc.sync.dma_start(out=v_win[0][:, tokens(half)], in_=vT[0:P, tokens(half)])
+        for half in range(2):
+            nc.sync.dma_start(out=v_win[1][:, tokens(half)], in_=vT[P : 2 * P, tokens(half)])
         nc.sync.dma_start(out=kw_win[:], in_=k_words[0].rearrange("p t r -> p (t r)").bitcast(I32))
         for h in range(2):
             nc.sync.dma_start(out=slope_col[h][:], in_=slope[0, h * P : (h + 1) * P, :])
-        for half in range(2):
-            cols = slice(half * T // 2, (half + 1) * T // 2)
-            nc.sync.dma_start(out=v_win[0][:, cols], in_=vT[0:P, cols])
-        nc.sync.dma_start(out=v_win[1][:], in_=vT[P : 2 * P, :])
         nc.sync.dma_start(out=og_sb[:], in_=og[0].rearrange("(h p) e -> p h e", p=P))
-        nc.scalar.dma_start(out=vs_win[0:1, :], in_=vs[0:1, :])
 
-        pos_g = keep.tile([P, N], F32, name="pos_g")
-        for g in range(2):
+        def gather_scales():
+            nc.vector.tensor_copy(ks_g[:], ks_win[:].indirect(offsets[:]))
+
+        def gather_pos(g):
             nc.vector.tensor_copy(pos_g[:, slots(g)], pos_win[:].indirect(half_list(g)))
-        ks_g = keep.tile([P, N], U8, name="ks_g", align_bytes=64)
-        nc.vector.tensor_copy(ks_g[:], ks_win[:].indirect(offsets[:]))
 
-        q_bf = keep.tile([P, NQ, 4], BF16, name="q_bf", align_bytes=64)
-        nc.scalar.copy(out=q_bf[:], in_=q_raw[:].rearrange("p j w -> p w j"))
-        q_codes = keep.tile([P, NQ], U32, name="q_codes", align_bytes=64)
-        q_scales = keep.tile([P, NQ], U8, name="q_scales", align_bytes=64)
-        nc.vector.quantize_mx(out=q_codes[:].bitcast(FP8X4), scales=q_scales[:], in_=q_bf[:].rearrange("p w j -> p (w j)"))
+        def gather_vs(g):
+            nc.vector.tensor_copy(vs_g[:, slots(g)], vs_win[:].indirect(half_list(g)))
 
-        pos_col = keep.tile([P, 8], F32, name="pos_col")
-        pos_all = keep.tile([P, N], F32, name="pos_all")
-        for g in range(2):
-            pos_ps = psum.tile([P, 4, P], F32, name=f"pos_ps{g}", tag="bank")
-            for c in range(4):
-                nc.tensor.transpose(pos_ps[:, c, :], pos_g[:, g * PASS + c * P : g * PASS + (c + 1) * P], ident[:])
-            nc.scalar.copy(out=pos_col[:, 4 * g : 4 * g + 4], in_=pos_ps[:, :, 0])
-        for g in range(2):
-            row_ps = psum.tile([P, 4, P], F32, name=f"row_ps{g}", tag="bank")
-            for c in range(4):
-                nc.tensor.transpose(row_ps[:, c, :], pos_col[:, 4 * g + c : 4 * g + c + 1].to_broadcast([P, P]), ident[:])
-            nc.scalar.copy(out=pos_all[:, slots(g)], in_=row_ps[:].rearrange("p c n -> p (c n)"))
+        def gather_pos_all():
+            nc.vector.tensor_copy(pos_g[:], pos_win[:].indirect(offsets[:]))
 
-        kw_g = keep.tile([P, N], U32, name="kw_g", align_bytes=64)
-        for g in range(2):
+        def gather_vs_all():
+            nc.vector.tensor_copy(vs_g[:], vs_win[:].indirect(offsets[:]))
+
+        def gather_keys(g):
             nc.vector.tensor_copy(kw_g[:, slots(g)], kw_win[:].bitcast(U32).indirect(half_list(g)))
 
-        a_ps = {}
-        for g in range(2):
-            for h in range(2):
-                qs = slice(h * P, (h + 1) * P)
-                a_ps[h, g] = psum.tile([P, PASS], F32, name=f"a_ps{h}{g}", tag="bank")
-                nc.tensor.matmul_mx(out=a_ps[h, g][:], lhsT=q_codes[:, qs].bitcast(FP8X4), lhsT_scale=q_scales[:, qs],
-                                    rhs=kw_g[:, slots(g)].bitcast(FP8X4), rhs_scale=ks_g[:, slots(g)], start=True, stop=True)
+        def cast_q():
+            nc.scalar.copy(out=q_bf[:], in_=q_raw[:].rearrange("p j w -> p w j"))
 
-        s_sb = [keep.tile([P, N], F32, name=f"s_sb{h}") for h in range(2)]
-        neg_max = [keep.tile([P, 1], F32, name=f"neg_max{h}") for h in range(2)]
-        half_sum = [keep.tile([P, 2], F32, name=f"half_sum{h}") for h in range(2)]
-        p_sb = {}
+        def quantize_q():
+            nc.vector.quantize_mx(out=q_codes[:].bitcast(FP8X4), scales=q_scales[:], in_=q_bf[:].rearrange("p w j -> p (w j)"))
+
+        def turn_pos(g):
+            ps = new_bank(f"pos_ps{g}", [P, 4, P])
+            for c in range(4):
+                nc.tensor.transpose(ps[:, c, :], pos_g[:, g * PASS + c * P : g * PASS + (c + 1) * P], ident[:])
+
+        def pick_pos(g):
+            nc.scalar.copy(out=pos_col[:, g, :], in_=bank[f"pos_ps{g}"][:, :, 0])
+
+        def spread_pos(g):
+            ps = new_bank(f"row_ps{g}", [P, 4, P])
+            for c in range(4):
+                nc.tensor.transpose(ps[:, c, :], pos_col[:, g, c : c + 1].to_broadcast([P, P]), ident[:])
+
+        def store_pos(g):
+            nc.scalar.copy(out=pos_all[:, slots(g)], in_=bank[f"row_ps{g}"][:].rearrange("p c n -> p (c n)"))
+
+        def scores(h, g):
+            qs = slice(h * P, (h + 1) * P)
+            ps = new_bank(f"a_ps{h}{g}", [P, PASS])
+            nc.tensor.matmul_mx(out=ps[:], lhsT=q_codes[:, qs].bitcast(FP8X4), lhsT_scale=q_scales[:, qs],
+                                rhs=kw_g[:, slots(g)].bitcast(FP8X4), rhs_scale=ks_g[:, slots(g)], start=True, stop=True)
 
         def add_bias(h, g):
             nc.vector.scalar_tensor_tensor(out=s_sb[h][:, slots(g)], in0=pos_all[:, slots(g)], scalar=slope_col[h][:],
-                                           in1=a_ps[h, g][:], op0=ALU.mult, op1=ALU.add)
+                                           in1=bank[f"a_ps{h}{g}"][:], op0=ALU.mult, op1=ALU.add)
 
-        def softmax(h):
+        def row_max(h):
             nc.vector.tensor_reduce(out=neg_max[h][:], in_=s_sb[h][:], axis=AX.X, op=ALU.max, negate=True)
-            for g in range(2):
-                p_sb[h, g] = keep.tile([P, 4, P], F32, name=f"p_sb{h}{g}")
-                nc.scalar.activation(out=p_sb[h, g][:].rearrange("p t s -> p s t"), in_=s_sb[h][:, slots(g)].rearrange("p (s t) -> p s t", t=4),
-                                     func=ACT.Exp, bias=neg_max[h][:], accum_out=half_sum[h][:, g : g + 1])
 
-        add_bias(0, 0)
-        add_bias(0, 1)
-        add_bias(1, 0)
-        softmax(0)
-        add_bias(1, 1)
-        vs_g = keep.tile([P, N], F32, name="vs_g")
-        nc.vector.tensor_copy(vs_g[:, slots(0)], vs_win[:].indirect(half_list(0)))
-        softmax(1)
-        nc.vector.tensor_copy(vs_g[:, slots(1)], vs_win[:].indirect(half_list(1)))
+        def exp(h, g):
+            nc.scalar.activation(out=p_sb[h][:, g, :, :].rearrange("p t s -> p s t"), in_=s_sb[h][:, slots(g)].rearrange("p (s t) -> p s t", t=4),
+                                 func=ACT.Exp, bias=neg_max[h][:], accum_out=half_sum[h][:, g : g + 1])
 
-        vs_col = keep.tile([P, 2, 4], F32, name="vs_col")
-        for g in range(2):
-            vs_ps = psum.tile([P, 4, P], F32, name=f"vs_ps{g}", tag="bank")
+        def turn_vs(g):
+            ps = new_bank(f"vs_ps{g}", [P, 4, P])
             for t in range(4):
-                nc.tensor.transpose(vs_ps[:, t, :], vs_g[:, g * PASS + t : (g + 1) * PASS : 4], ident[:])
-            nc.scalar.copy(out=vs_col[:, g, :], in_=vs_ps[:, :, 0])
+                nc.tensor.transpose(ps[:, t, :], vs_g[:, g * PASS + t : (g + 1) * PASS : 4], ident[:])
 
-        v_bf = keep.tile([P, 2, DV, 4], BF16, name="v_bf", align_bytes=64)
-        v_words = v_bf[:].rearrange("p g c t -> p (g c t)").bitcast(F32).rearrange("p (g c u) -> p g c u", g=2, u=2)
-        for f in (1, 0):
-            v_g = keep.tile([P, 2, 2 * P, 2], BF16, name=f"v_g{f}")
-            if f == 0:
-                v_cast = keep.tile([P, T], BF16, name="v_cast")
-                for quarter in range(4):
-                    cols = slice(quarter * T // 4, (quarter + 1) * T // 4)
-                    nc.scalar.activation(out=v_cast[:, cols], in_=v_win[0][:, cols], func=ACT.Copy)
-                for g in range(2):
-                    nc.scalar.activation(out=v_g[:, :, g * P : (g + 1) * P, :].rearrange("p u s e -> p s u e"),
-                                         in_=v_cast[:].indirect(half_list(g)), func=ACT.Copy)
-            else:
-                for g in range(2):
-                    nc.vector.tensor_copy(v_g[:, :, g * P : (g + 1) * P, :].rearrange("p u s e -> p s u e"), v_win[f][:].indirect(half_list(g)))
-            pairs = v_g[:].rearrange("p u s e -> p (u s e)").bitcast(F32)
-            vt_ps = psum.tile([P, 2, 2, P], F32, name=f"vt_ps{f}", tag="bank")
+        def pick_vs(g):
+            nc.scalar.copy(out=vs_col[:, g, :], in_=bank[f"vs_ps{g}"][:, :, 0])
+
+        def cast_v(f, half):
+            nc.scalar.activation(out=v_cast[f][:, tokens(half)], in_=v_win[f][:, tokens(half)], func=ACT.Copy)
+
+        def cast_v_vec(f, half):
+            nc.vector.tensor_copy(v_cast[f][:, tokens(half)], v_win[f][:, tokens(half)])
+
+        def gather_v(f, g):
+            nc.scalar.activation(out=v_g[f][:, :, g * P : (g + 1) * P, :].rearrange("p u s e -> p s u e"),
+                                 in_=v_cast[f][:].indirect(half_list(g)), func=ACT.Copy)
+
+        def gather_v_all(f):
+            nc.scalar.activation(out=v_g[f][:].rearrange("p u s e -> p s u e"), in_=v_cast[f][:].indirect(offsets[:]), func=ACT.Copy)
+
+        def gather_v_vec(f, g):
+            nc.vector.tensor_copy(v_g[f][:, :, g * P : (g + 1) * P, :].rearrange("p u s e -> p s u e"), v_win[f][:].indirect(half_list(g)))
+
+        def turn_v(f):
+            pairs = v_g[f][:].rearrange("p u s e -> p (u s e)").bitcast(F32)
+            ps = new_bank(f"vt_ps{f}", [P, 2, 2, P])
             for g in range(2):
                 for u in range(2):
-                    nc.tensor.transpose(vt_ps[:, g, u, :], pairs[:, 2 * P * u + P * g : 2 * P * u + P * (g + 1)], ident[:])
-            nc.scalar.copy(out=v_words[:, :, f * P : (f + 1) * P, :], in_=vt_ps[:].rearrange("p g u c -> p g c u"))
-        v_codes = keep.tile([P, 2, DV], U32, name="v_codes", align_bytes=64)
-        v_scales = keep.tile([P, 2, DV], U8, name="v_scales", align_bytes=64)
+                    nc.tensor.transpose(ps[:, g, u, :], pairs[:, 2 * P * u + P * g : 2 * P * u + P * (g + 1)], ident[:])
 
-        gate = keep.tile([P, 2, DV], F32, name="gate")
-        nc.scalar.activation(out=gate[:], in_=og_sb[:], func=ACT.Tanh, scale=0.5)
+        def store_v(f):
+            nc.scalar.copy(out=v_words[:, :, f * P : (f + 1) * P, :], in_=bank[f"vt_ps{f}"][:].rearrange("p g u c -> p g c u"))
 
-        w_bf, w_codes, w_scales = {}, {}, {}
+        def quantize_v():
+            nc.vector.quantize_mx(out=v_codes[:].rearrange("p g c -> p (g c)").bitcast(FP8X4), scales=v_scales[:].rearrange("p g c -> p (g c)"),
+                                  in_=v_bf[:].rearrange("p g c t -> p (g c t)"))
+
+        def tanh_gate():
+            nc.scalar.activation(out=gate[:], in_=og_sb[:], func=ACT.Tanh, scale=0.5)
+
+        def turn_p(h, g):
+            ps = new_bank(f"pt_ps{h}{g}", [P, 4, P])
+            for t in range(4):
+                nc.tensor.transpose(ps[:, t, :], p_sb[h][:, g, t, :], ident[:])
 
         def weigh(h, g):
-            pt_ps = psum.tile([P, 4, P], F32, name=f"pt_ps{h}{g}", tag="bank")
-            for t in range(4):
-                nc.tensor.transpose(pt_ps[:, t, :], p_sb[h, g][:, t, :], ident[:])
-            w_bf[h, g] = keep.tile([P, P, 4], BF16, name=f"w_bf{h}{g}", align_bytes=64)
-            nc.vector.tensor_tensor(w_bf[h, g][:], pt_ps[:].rearrange("p t q -> p q t"),
+            nc.vector.tensor_tensor(w_bf[h][:, g, :, :], bank[f"pt_ps{h}{g}"][:].rearrange("p t q -> p q t"),
                                     vs_col[:, g, :].unsqueeze(1).to_broadcast([P, P, 4]), ALU.mult)
 
-        def quantize_w(h, g):
-            w_codes[h, g] = keep.tile([P, P], U32, name=f"w_codes{h}{g}", align_bytes=64)
-            w_scales[h, g] = keep.tile([P, P], U8, name=f"w_scales{h}{g}", align_bytes=64)
-            nc.vector.quantize_mx(out=w_codes[h, g][:].bitcast(FP8X4), scales=w_scales[h, g][:], in_=w_bf[h, g][:].rearrange("p q t -> p (q t)"))
+        def quantize_w(h, first, last):
+            passes = slice(first, last + 1)
+            nc.vector.quantize_mx(out=w_codes[h][:, passes, :].rearrange("p g q -> p (g q)").bitcast(FP8X4),
+                                  scales=w_scales[h][:, passes, :].rearrange("p g q -> p (g q)"),
+                                  in_=w_bf[h][:, passes, :, :].rearrange("p g q t -> p (g q t)"))
 
-        factor = {}
+        def row_sum(h):
+            nc.vector.tensor_scalar(twice_sum[h][:], half_sum[h][:, 0:1], half_sum[h][:, 1:2], 2.0, ALU.add, ALU.mult)
+
+        def invert(h):
+            nc.vector.reciprocal(inv[h][:], twice_sum[h][:])
 
         def make_factor(h):
-            twice_sum = keep.tile([P, 1], F32, name=f"twice_sum{h}")
-            nc.vector.tensor_scalar(twice_sum[:], half_sum[h][:, 0:1], half_sum[h][:, 1:2], 2.0, ALU.add, ALU.mult)
-            inv = keep.tile([P, 1], F32, name=f"inv{h}")
-            nc.vector.reciprocal(inv[:], twice_sum[:])
-            factor[h] = keep.tile([P, DV], F32, name=f"factor{h}")
-            nc.scalar.activation(out=factor[h][:], in_=gate[:, h, :], func=ACT.Identity, scale=inv[:], bias=inv[:])
+            nc.scalar.activation(out=factor[h][:], in_=gate[:, h, :], func=ACT.Identity, scale=inv[h][:], bias=inv[h][:])
+
+        def product(h):
+            ps = new_bank(f"y_ps{h}", [P, DV])
+            for g in range(2):
+                nc.tensor.matmul_mx(out=ps[:], lhsT=w_codes[h][:, g, :].bitcast(FP8X4), lhsT_scale=w_scales[h][:, g, :],
+                                    rhs=v_codes[:, g, :].bitcast(FP8X4), rhs_scale=v_scales[:, g, :], start=(g == 0), stop=(g == 1))
 
         def finish(h):
-            y_ps = psum.tile([P, DV], F32, name=f"y_ps{h}", tag="bank")
-            for g in range(2):
-                nc.tensor.matmul_mx(out=y_ps[:], lhsT=w_codes[h, g][:].bitcast(FP8X4), lhsT_scale=w_scales[h, g][:],
-                                    rhs=v_codes[:, g, :].bitcast(FP8X4), rhs_scale=v_scales[:, g, :], start=(g == 0), stop=(g == 1))
-            res = keep.tile([P, DV], F32, name=f"res{h}")
-            nc.vector.tensor_tensor(res[:], y_ps[:], factor[h][:], ALU.mult)
-            nc.sync.dma_start(out=out[0, h * P : (h + 1) * P, :], in_=res[:])
+            nc.vector.tensor_tensor(res[h][:], bank[f"y_ps{h}"][:], factor[h][:], ALU.mult)
+            nc.sync.dma_start(out=out[0, h * P : (h + 1) * P, :], in_=res[h][:])
 
-        weigh(0, 0)
-        weigh(0, 1)
-        quantize_w(0, 0)
-        for g in range(2):
-            nc.vector.quantize_mx(out=v_codes[:, g, :].bitcast(FP8X4), scales=v_scales[:, g, :],
-                                  in_=v_bf[:, g, :, :].rearrange("p c t -> p (c t)"))
-        quantize_w(0, 1)
+        gather_scales()
+        cast_q()
+        cast_v(0,0)
+        cast_v(0,1)
+        gather_pos_all()
+        turn_pos(0)
+        turn_pos(1)
+        gather_v_all(0)
+        pick_pos(0)
+        pick_pos(1)
+        spread_pos(0)
+        spread_pos(1)
+        turn_v(0)
+        quantize_q()
+        gather_vs_all()
+        cast_v(1,0)
+        store_pos(0)
+        store_pos(1)
+        cast_v(1,1)
+        gather_v_all(1)
+        gather_keys(0)
+        scores(0,0)
+        scores(1,0)
+        gather_keys(1)
+        scores(0,1)
+        scores(1,1)
+        add_bias(0,0)
+        add_bias(1,0)
+        turn_vs(0)
+        turn_vs(1)
+        add_bias(0,1)
+        add_bias(1,1)
+        turn_v(1)
+        pick_vs(0)
+        pick_vs(1)
+        store_v(0)
+        row_max(0)
+        exp(0,0)
+        turn_p(0,0)
+        exp(0,1)
+        turn_p(0,1)
+        store_v(1)
+        row_max(1)
+        exp(1,0)
+        turn_p(1,0)
+        exp(1,1)
+        turn_p(1,1)
+        tanh_gate()
+        weigh(0,0)
+        row_sum(0)
+        weigh(0,1)
+        quantize_v()
+        invert(0)
+        quantize_w(0,0,1)
         make_factor(0)
-        weigh(1, 0)
-        finish(0)
-        weigh(1, 1)
-        quantize_w(1, 0)
+        product(0)
+        weigh(1,0)
+        row_sum(1)
+        weigh(1,1)
+        invert(1)
         make_factor(1)
-        quantize_w(1, 1)
+        quantize_w(1,0,0)
+        finish(0)
+        quantize_w(1,1,1)
+        product(1)
         finish(1)

@@ -33,9 +33,9 @@ def tile_attend_soft_alibi_gate_srtq256n1024t2048_kernel(tc, qT, k_words, k_scal
         offsets = keep.tile([P, N // 16], U16, name="offsets")
         q_raw = keep.tile([P, 4, NQ], F32, name="q_raw")
         pos_win = keep.tile([P, T], F32, name="pos_win")
-        vs_win = keep.tile([P, T], F32, name="vs_win")
         ks_win = keep.tile([P, T], U8, name="ks_win")
-        warm = late.tile([P, 3 * T + 2 * DV + 16], F32, name="warm", offset=0)
+        warm = late.tile([P, 4 * T + 2 * DV + 16], F32, name="warm", offset=0)
+        vs_win = late.tile([P, T], F32, name="vs_win", offset=4 * (3 * T + 2 * DV + 16))
         kw_win = late.tile([P, T], I32, name="kw_win", offset=0)
         v_win = [late.tile([P, T], F32, name=f"v_win{f}", offset=4 * T * (f + 1)) for f in range(2)]
         og_sb = late.tile([P, 2, DV], F32, name="og_sb", offset=4 * T * 3)
@@ -49,7 +49,7 @@ def tile_attend_soft_alibi_gate_srtq256n1024t2048_kernel(tc, qT, k_words, k_scal
         q_bf = keep.tile([P, NQ, 4], BF16, name="q_bf", align_bytes=64)
         q_codes = keep.tile([P, NQ], U32, name="q_codes", align_bytes=64)
         q_scales = keep.tile([P, NQ], U8, name="q_scales", align_bytes=64)
-        pos_col = reuse.tile([P, 2, 4], F32, name="pos_col", offset=0)
+        pos_col = late.tile([P, 2, 4], F32, name="pos_col", offset=4 * T)
         pos_all = keep.tile([P, N], F32, name="pos_all")
         vs_col = late.tile([P, 2, 4], F32, name="vs_col", offset=4 * T * 2)
         s_sb = [keep.tile([P, N], F32, name=f"s_sb{h}") for h in range(2)]
@@ -87,24 +87,23 @@ def tile_attend_soft_alibi_gate_srtq256n1024t2048_kernel(tc, qT, k_words, k_scal
 
         nc.vector.memset(ks_win[:].bitcast(I32), 0)
         nc.vector.memset(pos_win[:], 0.0)
-        nc.vector.memset(vs_win[:], 0.0)
         make_identity(nc, ident[:])
 
         nc.sync.dma_start(offsets[:], offs)
         nc.sync.dma_start(out=q_raw[:], in_=qT[0].rearrange("(p j) w -> p j w", j=4))
         ks_hbm = k_scales[0].bitcast(I32)
         for quad in range(4):
-            nc.scalar.dma_start(out=ks_win[32 * quad : 32 * quad + 4, :].bitcast(I32), in_=ks_hbm[4 * quad : 4 * quad + 4, :])
-        nc.scalar.dma_start(out=pos_win[0:1, :], in_=pos[0:1, :])
+            nc.sync.dma_start(out=ks_win[32 * quad : 32 * quad + 4, :].bitcast(I32), in_=ks_hbm[4 * quad : 4 * quad + 4, :])
+        nc.sync.dma_start(out=pos_win[0:1, :], in_=pos[0:1, :])
         nc.scalar.activation(out=warm[32:64, 0:1], in_=pos_win[32:64, 0:1], func=ACT.Exp)
-        nc.scalar.dma_start(out=vs_win[0:1, :], in_=vs[0:1, :])
         for half in range(2):
             nc.sync.dma_start(out=v_win[0][:, tokens(half)], in_=vT[0:P, tokens(half)])
+        nc.sync.dma_start(out=kw_win[:], in_=k_words[0].rearrange("p t r -> p (t r)").bitcast(I32))
         for half in range(2):
             nc.sync.dma_start(out=v_win[1][:, tokens(half)], in_=vT[P : 2 * P, tokens(half)])
-        nc.sync.dma_start(out=kw_win[:], in_=k_words[0].rearrange("p t r -> p (t r)").bitcast(I32))
         for h in range(2):
             nc.sync.dma_start(out=slope_col[h][:], in_=slope[0, h * P : (h + 1) * P, :])
+        nc.sync.dma_start(out=vs_win[:], in_=vs)
         nc.sync.dma_start(out=og_sb[:], in_=og[0].rearrange("(h p) e -> p h e", p=P))
 
         def gather_scales():
@@ -175,6 +174,10 @@ def tile_attend_soft_alibi_gate_srtq256n1024t2048_kernel(tc, qT, k_words, k_scal
         def cast_v(f, half):
             nc.scalar.activation(out=v_cast[f][:, tokens(half)], in_=v_win[f][:, tokens(half)], func=ACT.Copy)
 
+        def cast_v_quarter(f, quarter):
+            cols = slice(quarter * T // 4, (quarter + 1) * T // 4)
+            nc.scalar.activation(out=v_cast[f][:, cols], in_=v_win[f][:, cols], func=ACT.Copy)
+
         def cast_v_vec(f, half):
             nc.vector.tensor_copy(v_cast[f][:, tokens(half)], v_win[f][:, tokens(half)])
 
@@ -243,20 +246,22 @@ def tile_attend_soft_alibi_gate_srtq256n1024t2048_kernel(tc, qT, k_words, k_scal
         cast_q()
         cast_v(0,0)
         cast_v(0,1)
-        gather_pos_all()
+        gather_pos(0)
         turn_pos(0)
+        gather_pos(1)
         turn_pos(1)
-        gather_v_all(0)
+        gather_v(0,0)
         pick_pos(0)
-        pick_pos(1)
         spread_pos(0)
+        gather_v(0,1)
+        store_pos(0)
+        pick_pos(1)
         spread_pos(1)
         turn_v(0)
         quantize_q()
-        gather_vs_all()
-        cast_v(1,0)
-        store_pos(0)
+        cast_v_quarter(1,0)
         store_pos(1)
+        cast_v_quarter(1,1)
         cast_v(1,1)
         gather_v_all(1)
         gather_keys(0)
@@ -267,18 +272,20 @@ def tile_attend_soft_alibi_gate_srtq256n1024t2048_kernel(tc, qT, k_words, k_scal
         scores(1,1)
         add_bias(0,0)
         add_bias(1,0)
-        turn_vs(0)
-        turn_vs(1)
         add_bias(0,1)
         add_bias(1,1)
+        gather_vs(0)
+        turn_vs(0)
         turn_v(1)
         pick_vs(0)
-        pick_vs(1)
         store_v(0)
         row_max(0)
+        gather_vs(1)
         exp(0,0)
         turn_p(0,0)
+        turn_vs(1)
         exp(0,1)
+        pick_vs(1)
         turn_p(0,1)
         store_v(1)
         row_max(1)

@@ -19,7 +19,7 @@ AX = mybir.AxisListType
 
 P = 128
 PASS = 512
-BANK_OF = {"pos_ps0":0,"pos_ps1":1,"row_ps0":2,"row_ps1":3,"a_ps00":4,"a_ps10":5,"a_ps01":2,"a_ps11":3,"vt_ps0":6,"vt_ps1":7,"vs_ps0":4,"vs_ps1":5,"pt_ps00":0,"pt_ps01":1,"pt_ps10":2,"pt_ps11":3,"y_ps0":4,"y_ps1":5}
+BANK_OF = {"pos_ps0":0,"pos_ps1":1,"row_ps0":2,"row_ps1":3,"a_ps00":4,"a_ps10":5,"a_ps01":6,"a_ps11":7,"vt_ps0":6,"vt_ps1":7,"vs_ps0":4,"vs_ps1":2,"pt_ps00":0,"pt_ps01":1,"pt_ps10":3,"pt_ps11":4,"y_ps0":2,"y_ps1":5}
 
 
 def tile_attend_soft_alibi_gate_srtq256n1024t2048_kernel(tc, qT, k_words, k_scales, vT, vs, pos, slope, og, offs, out):
@@ -32,7 +32,7 @@ def tile_attend_soft_alibi_gate_srtq256n1024t2048_kernel(tc, qT, k_words, k_scal
 
         offsets = keep.tile([P, N // 16], U16, name="offsets")
         q_raw = keep.tile([P, 4, NQ], F32, name="q_raw")
-        pos_win = keep.tile([P, T], F32, name="pos_win")
+        pos_win = reuse.tile([P, T], F32, name="pos_win", offset=6 * T)
         ks_win = keep.tile([P, T], U8, name="ks_win")
         warm = late.tile([P, 4 * T + 2 * DV + 16], F32, name="warm", offset=0)
         vs_win = late.tile([P, T], F32, name="vs_win", offset=4 * (3 * T + 2 * DV + 16))
@@ -44,7 +44,7 @@ def tile_attend_soft_alibi_gate_srtq256n1024t2048_kernel(tc, qT, k_words, k_scal
 
         pos_g = keep.tile([P, N], F32, name="pos_g")
         vs_g = keep.tile([P, N], F32, name="vs_g")
-        ks_g = keep.tile([P, N], U8, name="ks_g", align_bytes=64)
+        ks_g = reuse.tile([P, N], U8, name="ks_g", align_bytes=64, offset=6 * T)
         kw_g = keep.tile([P, N], U32, name="kw_g", align_bytes=64)
         q_bf = keep.tile([P, NQ, 4], BF16, name="q_bf", align_bytes=64)
         q_codes = keep.tile([P, NQ], U32, name="q_codes", align_bytes=64)
@@ -52,9 +52,9 @@ def tile_attend_soft_alibi_gate_srtq256n1024t2048_kernel(tc, qT, k_words, k_scal
         pos_col = late.tile([P, 2, 4], F32, name="pos_col", offset=4 * T)
         pos_all = keep.tile([P, N], F32, name="pos_all")
         vs_col = late.tile([P, 2, 4], F32, name="vs_col", offset=4 * T * 2)
-        s_sb = [keep.tile([P, N], F32, name=f"s_sb{h}") for h in range(2)]
+        s_sb = [keep.tile([P, N], F32, name="s_sb0"), late.tile([P, N], F32, name="s_sb1", offset=4 * (3 * T + 2 * DV + 16))]
         neg_max = [keep.tile([P, 1], F32, name=f"neg_max{h}") for h in range(2)]
-        half_sum = [keep.tile([P, 2], F32, name=f"half_sum{h}") for h in range(2)]
+        half_sum = keep.tile([P, 2, 2], F32, name="half_sum")
         p_sb = [reuse.tile([P, 2, 4, P], F32, name=f"p_sb{h}", offset=2 * T * (h + 1)) for h in range(2)]
         v_cast = [reuse.tile([P, T], BF16, name=f"v_cast{f}", offset=2 * T * f) for f in range(2)]
         v_g = [keep.tile([P, 2, 2 * P, 2], BF16, name=f"v_g{f}") for f in range(2)]
@@ -66,8 +66,8 @@ def tile_attend_soft_alibi_gate_srtq256n1024t2048_kernel(tc, qT, k_words, k_scal
         w_bf = [keep.tile([P, 2, P, 4], BF16, name=f"w_bf{h}", align_bytes=64) for h in range(2)]
         w_codes = [keep.tile([P, 2, P], U32, name=f"w_codes{h}", align_bytes=64) for h in range(2)]
         w_scales = [keep.tile([P, 2, P], U8, name=f"w_scales{h}", align_bytes=64) for h in range(2)]
-        twice_sum = [keep.tile([P, 1], F32, name=f"twice_sum{h}") for h in range(2)]
-        inv = [keep.tile([P, 1], F32, name=f"inv{h}") for h in range(2)]
+        total = keep.tile([P, 2], F32, name="total")
+        inv = keep.tile([P, 2], F32, name="inv")
         factor = [keep.tile([P, DV], F32, name=f"factor{h}") for h in range(2)]
         res = [keep.tile([P, DV], F32, name=f"res{h}") for h in range(2)]
         bank = {}
@@ -99,10 +99,10 @@ def tile_attend_soft_alibi_gate_srtq256n1024t2048_kernel(tc, qT, k_words, k_scal
         for half in range(2):
             nc.sync.dma_start(out=v_win[0][:, tokens(half)], in_=vT[0:P, tokens(half)])
         nc.sync.dma_start(out=kw_win[:], in_=k_words[0].rearrange("p t r -> p (t r)").bitcast(I32))
-        for half in range(2):
-            nc.sync.dma_start(out=v_win[1][:, tokens(half)], in_=vT[P : 2 * P, tokens(half)])
         for h in range(2):
             nc.sync.dma_start(out=slope_col[h][:], in_=slope[0, h * P : (h + 1) * P, :])
+        for half in range(2):
+            nc.sync.dma_start(out=v_win[1][:, tokens(half)], in_=vT[P : 2 * P, tokens(half)])
         nc.sync.dma_start(out=vs_win[:], in_=vs)
         nc.sync.dma_start(out=og_sb[:], in_=og[0].rearrange("(h p) e -> p h e", p=P))
 
@@ -161,7 +161,7 @@ def tile_attend_soft_alibi_gate_srtq256n1024t2048_kernel(tc, qT, k_words, k_scal
 
         def exp(h, g):
             nc.scalar.activation(out=p_sb[h][:, g, :, :].rearrange("p t s -> p s t"), in_=s_sb[h][:, slots(g)].rearrange("p (s t) -> p s t", t=4),
-                                 func=ACT.Exp, bias=neg_max[h][:], accum_out=half_sum[h][:, g : g + 1])
+                                 func=ACT.Exp, bias=neg_max[h][:], accum_out=half_sum[:, h, g : g + 1])
 
         def turn_vs(g):
             ps = new_bank(f"vs_ps{g}", [P, 4, P])
@@ -223,14 +223,14 @@ def tile_attend_soft_alibi_gate_srtq256n1024t2048_kernel(tc, qT, k_words, k_scal
                                   scales=w_scales[h][:, passes, :].rearrange("p g q -> p (g q)"),
                                   in_=w_bf[h][:, passes, :, :].rearrange("p g q t -> p (g q t)"))
 
-        def row_sum(h):
-            nc.vector.tensor_scalar(twice_sum[h][:], half_sum[h][:, 0:1], half_sum[h][:, 1:2], 2.0, ALU.add, ALU.mult)
+        def row_sum():
+            nc.vector.tensor_reduce(out=total[:], in_=half_sum[:], axis=AX.X, op=ALU.add)
 
-        def invert(h):
-            nc.vector.reciprocal(inv[h][:], twice_sum[h][:])
+        def invert():
+            nc.vector.reciprocal(inv[:], total[:])
 
         def make_factor(h):
-            nc.scalar.activation(out=factor[h][:], in_=gate[:, h, :], func=ACT.Identity, scale=inv[h][:], bias=inv[h][:])
+            nc.scalar.activation(out=factor[h][:], in_=gate[:, h, :], func=ACT.Identity, scale=inv[:, h : h + 1], bias=inv[:, h : h + 1])
 
         def product(h):
             ps = new_bank(f"y_ps{h}", [P, DV])
@@ -239,29 +239,25 @@ def tile_attend_soft_alibi_gate_srtq256n1024t2048_kernel(tc, qT, k_words, k_scal
                                     rhs=v_codes[:, g, :].bitcast(FP8X4), rhs_scale=v_scales[:, g, :], start=(g == 0), stop=(g == 1))
 
         def finish(h):
-            nc.vector.tensor_tensor(res[h][:], bank[f"y_ps{h}"][:], factor[h][:], ALU.mult)
+            nc.vector.scalar_tensor_tensor(out=res[h][:], in0=bank[f"y_ps{h}"][:], scalar=0.5, in1=factor[h][:], op0=ALU.mult, op1=ALU.mult)
             nc.sync.dma_start(out=out[0, h * P : (h + 1) * P, :], in_=res[h][:])
 
+        gather_pos_all()
         gather_scales()
         cast_q()
         cast_v(0,0)
         cast_v(0,1)
-        gather_pos(0)
         turn_pos(0)
-        gather_pos(1)
         turn_pos(1)
-        gather_v(0,0)
         pick_pos(0)
-        spread_pos(0)
-        gather_v(0,1)
-        store_pos(0)
         pick_pos(1)
+        spread_pos(0)
         spread_pos(1)
-        turn_v(0)
-        quantize_q()
-        cast_v_quarter(1,0)
+        gather_v_all(0)
+        store_pos(0)
         store_pos(1)
-        cast_v_quarter(1,1)
+        quantize_q()
+        cast_v(1,0)
         cast_v(1,1)
         gather_v_all(1)
         gather_keys(0)
@@ -271,22 +267,22 @@ def tile_attend_soft_alibi_gate_srtq256n1024t2048_kernel(tc, qT, k_words, k_scal
         scores(0,1)
         scores(1,1)
         add_bias(0,0)
-        add_bias(1,0)
         add_bias(0,1)
-        add_bias(1,1)
-        gather_vs(0)
-        turn_vs(0)
-        turn_v(1)
-        pick_vs(0)
-        store_v(0)
+        turn_v(0)
         row_max(0)
-        gather_vs(1)
+        gather_vs_all()
+        turn_vs(0)
+        turn_vs(1)
+        add_bias(1,0)
+        add_bias(1,1)
         exp(0,0)
         turn_p(0,0)
-        turn_vs(1)
         exp(0,1)
-        pick_vs(1)
         turn_p(0,1)
+        pick_vs(0)
+        pick_vs(1)
+        turn_v(1)
+        store_v(0)
         store_v(1)
         row_max(1)
         exp(1,0)
@@ -295,20 +291,18 @@ def tile_attend_soft_alibi_gate_srtq256n1024t2048_kernel(tc, qT, k_words, k_scal
         turn_p(1,1)
         tanh_gate()
         weigh(0,0)
-        row_sum(0)
         weigh(0,1)
         quantize_v()
-        invert(0)
         quantize_w(0,0,1)
-        make_factor(0)
         product(0)
+        row_sum()
         weigh(1,0)
-        row_sum(1)
-        weigh(1,1)
-        invert(1)
+        invert()
+        make_factor(0)
         make_factor(1)
+        weigh(1,1)
         quantize_w(1,0,0)
-        finish(0)
         quantize_w(1,1,1)
         product(1)
+        finish(0)
         finish(1)

@@ -19,7 +19,8 @@ AX = mybir.AxisListType
 
 P = 128
 PASS = 512
-BANK_OF = {"pos_ps0":0,"pos_ps1":1,"row_ps0":2,"row_ps1":3,"a_ps00":4,"a_ps10":5,"a_ps01":6,"a_ps11":7,"vt_ps0":6,"vt_ps1":7,"vs_ps0":4,"vs_ps1":2,"pt_ps00":0,"pt_ps01":1,"pt_ps10":3,"pt_ps11":4,"y_ps0":2,"y_ps1":5}
+BANK_OF = {"pos_ps0":0,"pos_ps1":1,"row_ps0":2,"row_ps1":3,"a_ps00":4,"a_ps01":5,"a_ps10":6,"a_ps11":7,"vs_ps0":0,"vs_ps1":1,"vt_ps0":2,"vt_ps1":3,"pt_ps00":4,"pt_ps01":5,"pt_ps10":6,"pt_ps11":7,"y_ps0":0,"y_ps1":1}
+PREFIX = T - PASS
 
 
 def tile_attend_soft_alibi_gate_srtq256n1024t2048_kernel(tc, qT, k_words, k_scales, vT, vs, pos, slope, og, offs, out):
@@ -28,38 +29,46 @@ def tile_attend_soft_alibi_gate_srtq256n1024t2048_kernel(tc, qT, k_words, k_scal
         keep = ctx.enter_context(tc.tile_pool(name="keep", bufs=1))
         late = ctx.enter_context(tc.tile_pool(name="late", bufs=1))
         psum = ctx.enter_context(tc.psum_pool(name="psum", bufs=1))
-        reuse = ctx.enter_context(tc.tile_pool(name="reuse", bufs=1))
+
+        def slots(g):
+            return slice(g * PASS, (g + 1) * PASS)
 
         offsets = keep.tile([P, N // 16], U16, name="offsets")
-        q_raw = keep.tile([P, 4, NQ], F32, name="q_raw")
-        pos_win = reuse.tile([P, T], F32, name="pos_win", offset=6 * T)
         ks_win = keep.tile([P, T], U8, name="ks_win")
-        warm = late.tile([P, 4 * T + 2 * DV + 16], F32, name="warm", offset=0)
-        vs_win = late.tile([P, T], F32, name="vs_win", offset=4 * (3 * T + 2 * DV + 16))
-        kw_win = late.tile([P, T], I32, name="kw_win", offset=0)
-        v_win = [late.tile([P, T], F32, name=f"v_win{f}", offset=4 * T * (f + 1)) for f in range(2)]
-        og_sb = late.tile([P, 2, DV], F32, name="og_sb", offset=4 * T * 3)
-        slope_col = [late.tile([P, 1], F32, name=f"slope_col{h}", offset=4 * (3 * T + 2 * DV + 8 * h)) for h in range(2)]
+        v0_lo = keep.tile([P, T // 2], F32, name="v0_lo")
         ident = keep.tile([P, P], F32, name="ident")
-
+        KB = 1024
+        v0_hi = late.tile([P, T // 2], F32, name="v0_hi", offset=0)
+        warm = late.tile([P, 12 * KB], F32, name="warm", offset=0)
+        q_raw = late.tile([P, 4, NQ], F32, name="q_raw", offset=4 * KB)
+        kw_win = late.tile([P, T], I32, name="kw_win", offset=40 * KB)
+        vs_win = late.tile([P, T], F32, name="vs_win", offset=16 * KB)
+        v1_win = late.tile([P, T], F32, name="v1_win", offset=24 * KB)
+        og_sb = late.tile([P, 2, DV], F32, name="og_sb", offset=32 * KB)
+        slope_col = [late.tile([P, 1], F32, name=f"slope_col{h}", offset=34 * KB + 32 * h) for h in range(2)]
+        v_cast = [late.tile([P, T], BF16, name="v_cast0", offset=35 * KB), late.tile([P, PREFIX], BF16, name="v_cast1", offset=4 * KB + 32)]
+        pos_win = late.tile([P, T], F32, name="pos_win", offset=48 * KB)
+        kw_g = late.tile([P, N], U32, name="kw_g", align_bytes=64, offset=48 * KB)
+        vs_g = late.tile([P, N], F32, name="vs_g", offset=40 * KB)
+        s_sb = [late.tile([P, N], F32, name=f"s_sb{h}", offset=(16 + 4 * h) * KB) for h in range(2)]
+        gate_tanh = late.tile([P, 2, DV], F32, name="gate_tanh", offset=20 * KB)
+        pos_col = [late.tile([P, 4], F32, name=f"pos_col{g}", offset=4 * KB + 32 * g) for g in range(2)]
+        v_g0 = keep.tile([P, N], BF16, name="v_g0")
+        v_g10 = keep.tile([P, PASS], BF16, name="v_g10")
+        v_g11 = late.tile([P, PASS], BF16, name="v_g11", offset=56 * KB)
+        v_g = {(0, 0): v_g0[:, slots(0)], (0, 1): v_g0[:, slots(1)], (1, 0): v_g10[:], (1, 1): v_g11[:]}
         pos_g = keep.tile([P, N], F32, name="pos_g")
-        vs_g = keep.tile([P, N], F32, name="vs_g")
-        ks_g = reuse.tile([P, N], U8, name="ks_g", align_bytes=64, offset=6 * T)
-        kw_g = keep.tile([P, N], U32, name="kw_g", align_bytes=64)
-        q_bf = keep.tile([P, NQ, 4], BF16, name="q_bf", align_bytes=64)
-        q_codes = keep.tile([P, NQ], U32, name="q_codes", align_bytes=64)
+        ks_g = keep.tile([P, N], U8, name="ks_g", align_bytes=64)
+        q_bf = late.tile([P, NQ, 4], BF16, name="q_bf", align_bytes=64, offset=35 * KB)
+        q_codes = late.tile([P, NQ], U32, name="q_codes", align_bytes=64, offset=44 * KB)
         q_scales = keep.tile([P, NQ], U8, name="q_scales", align_bytes=64)
-        pos_col = late.tile([P, 2, 4], F32, name="pos_col", offset=4 * T)
-        pos_all = keep.tile([P, N], F32, name="pos_all")
-        vs_col = late.tile([P, 2, 4], F32, name="vs_col", offset=4 * T * 2)
-        s_sb = [keep.tile([P, N], F32, name="s_sb0"), late.tile([P, N], F32, name="s_sb1", offset=4 * (3 * T + 2 * DV + 16))]
+        pos_all = late.tile([P, N], F32, name="pos_all", offset=56 * KB)
+        vs_col = late.tile([P, 2, 4], F32, name="vs_col", offset=4 * KB + 64)
         neg_max = [keep.tile([P, 1], F32, name=f"neg_max{h}") for h in range(2)]
         half_sum = keep.tile([P, 2, 2], F32, name="half_sum")
-        p_sb = [reuse.tile([P, 2, 4, P], F32, name=f"p_sb{h}", offset=2 * T * (h + 1)) for h in range(2)]
-        v_cast = [reuse.tile([P, T], BF16, name=f"v_cast{f}", offset=2 * T * f) for f in range(2)]
-        v_g = [keep.tile([P, 2, 2 * P, 2], BF16, name=f"v_g{f}") for f in range(2)]
+        p_sb = [late.tile([P, 2, 4, P], F32, name="p_sb0", offset=5 * KB), keep.tile([P, 2, 4, P], F32, name="p_sb1")]
         v_bf = keep.tile([P, 2, DV, 4], BF16, name="v_bf", align_bytes=64)
-        v_words = v_bf[:].rearrange("p g c t -> p (g c t)").bitcast(F32).rearrange("p (g c u) -> p g c u", g=2, u=2)
+        v_words = v_bf[:].rearrange("p g c t -> p (g c t)").bitcast(F32).rearrange("p (g f c u) -> p g f c u", g=2, f=2, u=2)
         v_codes = keep.tile([P, 2, DV], U32, name="v_codes", align_bytes=64)
         v_scales = keep.tile([P, 2, DV], U8, name="v_scales", align_bytes=64)
         gate = keep.tile([P, 2, DV], F32, name="gate")
@@ -68,7 +77,6 @@ def tile_attend_soft_alibi_gate_srtq256n1024t2048_kernel(tc, qT, k_words, k_scal
         w_scales = [keep.tile([P, 2, P], U8, name=f"w_scales{h}", align_bytes=64) for h in range(2)]
         total = keep.tile([P, 2], F32, name="total")
         inv = keep.tile([P, 2], F32, name="inv")
-        factor = [keep.tile([P, DV], F32, name=f"factor{h}") for h in range(2)]
         res = [keep.tile([P, DV], F32, name=f"res{h}") for h in range(2)]
         bank = {}
 
@@ -79,9 +87,6 @@ def tile_attend_soft_alibi_gate_srtq256n1024t2048_kernel(tc, qT, k_words, k_scal
         def half_list(g):
             return offsets[:, 32 * g : 32 * (g + 1)]
 
-        def slots(g):
-            return slice(g * PASS, (g + 1) * PASS)
-
         def tokens(half):
             return slice(half * T // 2, (half + 1) * T // 2)
 
@@ -90,20 +95,20 @@ def tile_attend_soft_alibi_gate_srtq256n1024t2048_kernel(tc, qT, k_words, k_scal
         make_identity(nc, ident[:])
 
         nc.sync.dma_start(offsets[:], offs)
-        nc.sync.dma_start(out=q_raw[:], in_=qT[0].rearrange("(p j) w -> p j w", j=4))
+        nc.sync.dma_start(out=v0_lo[:], in_=vT[0:P, tokens(0)])
         ks_hbm = k_scales[0].bitcast(I32)
         for quad in range(4):
             nc.sync.dma_start(out=ks_win[32 * quad : 32 * quad + 4, :].bitcast(I32), in_=ks_hbm[4 * quad : 4 * quad + 4, :])
         nc.sync.dma_start(out=pos_win[0:1, :], in_=pos[0:1, :])
         nc.scalar.activation(out=warm[32:64, 0:1], in_=pos_win[32:64, 0:1], func=ACT.Exp)
-        for half in range(2):
-            nc.sync.dma_start(out=v_win[0][:, tokens(half)], in_=vT[0:P, tokens(half)])
+        nc.sync.dma_start(out=v0_hi[:], in_=vT[0:P, tokens(1)])
         nc.sync.dma_start(out=kw_win[:], in_=k_words[0].rearrange("p t r -> p (t r)").bitcast(I32))
-        for h in range(2):
-            nc.sync.dma_start(out=slope_col[h][:], in_=slope[0, h * P : (h + 1) * P, :])
-        for half in range(2):
-            nc.sync.dma_start(out=v_win[1][:, tokens(half)], in_=vT[P : 2 * P, tokens(half)])
+        nc.sync.dma_start(out=q_raw[:], in_=qT[0].rearrange("(p j) w -> p j w", j=4))
+        nc.sync.dma_start(out=slope_col[0][:], in_=slope[0, 0:P, :])
+        nc.sync.dma_start(out=slope_col[1][:], in_=slope[0, P : 2 * P, :])
         nc.sync.dma_start(out=vs_win[:], in_=vs)
+        nc.sync.dma_start(out=v1_win[:, 0:PREFIX], in_=vT[P : 2 * P, 0:PREFIX])
+        nc.sync.dma_start(out=v1_win[:, PREFIX:T], in_=vT[P : 2 * P, PREFIX:T])
         nc.sync.dma_start(out=og_sb[:], in_=og[0].rearrange("(h p) e -> p h e", p=P))
 
         def gather_scales():
@@ -111,12 +116,6 @@ def tile_attend_soft_alibi_gate_srtq256n1024t2048_kernel(tc, qT, k_words, k_scal
 
         def gather_pos(g):
             nc.vector.tensor_copy(pos_g[:, slots(g)], pos_win[:].indirect(half_list(g)))
-
-        def gather_vs(g):
-            nc.vector.tensor_copy(vs_g[:, slots(g)], vs_win[:].indirect(half_list(g)))
-
-        def gather_pos_all():
-            nc.vector.tensor_copy(pos_g[:], pos_win[:].indirect(offsets[:]))
 
         def gather_vs_all():
             nc.vector.tensor_copy(vs_g[:], vs_win[:].indirect(offsets[:]))
@@ -136,12 +135,12 @@ def tile_attend_soft_alibi_gate_srtq256n1024t2048_kernel(tc, qT, k_words, k_scal
                 nc.tensor.transpose(ps[:, c, :], pos_g[:, g * PASS + c * P : g * PASS + (c + 1) * P], ident[:])
 
         def pick_pos(g):
-            nc.scalar.copy(out=pos_col[:, g, :], in_=bank[f"pos_ps{g}"][:, :, 0])
+            nc.scalar.copy(out=pos_col[g][:], in_=bank[f"pos_ps{g}"][:, :, 0])
 
         def spread_pos(g):
             ps = new_bank(f"row_ps{g}", [P, 4, P])
             for c in range(4):
-                nc.tensor.transpose(ps[:, c, :], pos_col[:, g, c : c + 1].to_broadcast([P, P]), ident[:])
+                nc.tensor.transpose(ps[:, c, :], pos_col[g][:, c : c + 1].to_broadcast([P, P]), ident[:])
 
         def store_pos(g):
             nc.scalar.copy(out=pos_all[:, slots(g)], in_=bank[f"row_ps{g}"][:].rearrange("p c n -> p (c n)"))
@@ -171,42 +170,37 @@ def tile_attend_soft_alibi_gate_srtq256n1024t2048_kernel(tc, qT, k_words, k_scal
         def pick_vs(g):
             nc.scalar.copy(out=vs_col[:, g, :], in_=bank[f"vs_ps{g}"][:, :, 0])
 
-        def cast_v(f, half):
-            nc.scalar.activation(out=v_cast[f][:, tokens(half)], in_=v_win[f][:, tokens(half)], func=ACT.Copy)
+        def cast_v0(half):
+            nc.scalar.activation(out=v_cast[0][:, tokens(half)], in_=(v0_lo, v0_hi)[half][:], func=ACT.Copy)
 
-        def cast_v_quarter(f, quarter):
-            cols = slice(quarter * T // 4, (quarter + 1) * T // 4)
-            nc.scalar.activation(out=v_cast[f][:, cols], in_=v_win[f][:, cols], func=ACT.Copy)
-
-        def cast_v_vec(f, half):
-            nc.vector.tensor_copy(v_cast[f][:, tokens(half)], v_win[f][:, tokens(half)])
+        def cast_v1():
+            nc.scalar.activation(out=v_cast[1][:], in_=v1_win[:, 0:PREFIX], func=ACT.Copy)
 
         def gather_v(f, g):
-            nc.scalar.activation(out=v_g[f][:, :, g * P : (g + 1) * P, :].rearrange("p u s e -> p s u e"),
-                                 in_=v_cast[f][:].indirect(half_list(g)), func=ACT.Copy)
+            nc.scalar.activation(out=v_g[f, g], in_=v_cast[f][:].indirect(half_list(g)), func=ACT.Copy)
 
         def gather_v_all(f):
-            nc.scalar.activation(out=v_g[f][:].rearrange("p u s e -> p s u e"), in_=v_cast[f][:].indirect(offsets[:]), func=ACT.Copy)
+            nc.scalar.activation(out=v_g0[:], in_=v_cast[f][:].indirect(offsets[:]), func=ACT.Copy)
 
-        def gather_v_vec(f, g):
-            nc.vector.tensor_copy(v_g[f][:, :, g * P : (g + 1) * P, :].rearrange("p u s e -> p s u e"), v_win[f][:].indirect(half_list(g)))
+        def gather_v_vec():
+            nc.vector.tensor_copy(v_g[1, 1], v1_win[:].indirect(half_list(1)))
 
-        def turn_v(f):
-            pairs = v_g[f][:].rearrange("p u s e -> p (u s e)").bitcast(F32)
-            ps = new_bank(f"vt_ps{f}", [P, 2, 2, P])
-            for g in range(2):
-                for u in range(2):
-                    nc.tensor.transpose(ps[:, g, u, :], pairs[:, 2 * P * u + P * g : 2 * P * u + P * (g + 1)], ident[:])
+        def turn_v(f, g):
+            pairs = v_g[f, g].bitcast(F32)
+            ps = bank[f"vt_ps{g}"] if f else new_bank(f"vt_ps{g}", [P, 2, 2, P])
+            for u in range(2):
+                nc.tensor.transpose(ps[:, f, u, :], pairs[:, u : 2 * P : 2], ident[:])
 
-        def store_v(f):
-            nc.scalar.copy(out=v_words[:, :, f * P : (f + 1) * P, :], in_=bank[f"vt_ps{f}"][:].rearrange("p g u c -> p g c u"))
+        def store_v(g):
+            nc.scalar.copy(out=v_words[:, g, :, :, :], in_=bank[f"vt_ps{g}"][:].rearrange("p f u c -> p f c u"))
 
-        def quantize_v():
-            nc.vector.quantize_mx(out=v_codes[:].rearrange("p g c -> p (g c)").bitcast(FP8X4), scales=v_scales[:].rearrange("p g c -> p (g c)"),
-                                  in_=v_bf[:].rearrange("p g c t -> p (g c t)"))
+        def quantize_v(g):
+            nc.vector.quantize_mx(out=v_codes[:, g, :].bitcast(FP8X4), scales=v_scales[:, g, :],
+                                  in_=v_bf[:, g, :, :].rearrange("p c t -> p (c t)"))
 
-        def tanh_gate():
-            nc.scalar.activation(out=gate[:], in_=og_sb[:], func=ACT.Tanh, scale=0.5)
+        def make_gate():
+            nc.scalar.activation(out=gate_tanh[:], in_=og_sb[:], func=ACT.Tanh, scale=0.5)
+            nc.scalar.activation(out=gate[:], in_=gate_tanh[:], func=ACT.Copy, scale=0.5, bias=0.5)
 
         def turn_p(h, g):
             ps = new_bank(f"pt_ps{h}{g}", [P, 4, P])
@@ -229,9 +223,6 @@ def tile_attend_soft_alibi_gate_srtq256n1024t2048_kernel(tc, qT, k_words, k_scal
         def invert():
             nc.vector.reciprocal(inv[:], total[:])
 
-        def make_factor(h):
-            nc.scalar.activation(out=factor[h][:], in_=gate[:, h, :], func=ACT.Identity, scale=inv[:, h : h + 1], bias=inv[:, h : h + 1])
-
         def product(h):
             ps = new_bank(f"y_ps{h}", [P, DV])
             for g in range(2):
@@ -239,70 +230,72 @@ def tile_attend_soft_alibi_gate_srtq256n1024t2048_kernel(tc, qT, k_words, k_scal
                                     rhs=v_codes[:, g, :].bitcast(FP8X4), rhs_scale=v_scales[:, g, :], start=(g == 0), stop=(g == 1))
 
         def finish(h):
-            nc.vector.scalar_tensor_tensor(out=res[h][:], in0=bank[f"y_ps{h}"][:], scalar=0.5, in1=factor[h][:], op0=ALU.mult, op1=ALU.mult)
+            nc.vector.scalar_tensor_tensor(out=res[h][:], in0=bank[f"y_ps{h}"][:], scalar=inv[:, h : h + 1], in1=gate[:, h, :], op0=ALU.mult, op1=ALU.mult)
             nc.sync.dma_start(out=out[0, h * P : (h + 1) * P, :], in_=res[h][:])
 
-        gather_pos_all()
         gather_scales()
-        cast_q()
-        cast_v(0,0)
-        cast_v(0,1)
-        turn_pos(0)
-        turn_pos(1)
-        pick_pos(0)
-        pick_pos(1)
-        spread_pos(0)
-        spread_pos(1)
+        cast_v0(0)
+        cast_v0(1)
         gather_v_all(0)
+        cast_q()
+        gather_pos(0)
+        gather_pos(1)
+        turn_pos(0)
+        pick_pos(0)
+        spread_pos(0)
+        turn_pos(1)
+        pick_pos(1)
+        spread_pos(1)
         store_pos(0)
         store_pos(1)
-        quantize_q()
-        cast_v(1,0)
-        cast_v(1,1)
-        gather_v_all(1)
         gather_keys(0)
-        scores(0,0)
-        scores(1,0)
         gather_keys(1)
-        scores(0,1)
-        scores(1,1)
-        add_bias(0,0)
-        add_bias(0,1)
-        turn_v(0)
-        row_max(0)
+        quantize_q()
+        scores(0, 0)
+        scores(0, 1)
+        scores(1, 0)
+        scores(1, 1)
         gather_vs_all()
         turn_vs(0)
         turn_vs(1)
-        add_bias(1,0)
-        add_bias(1,1)
-        exp(0,0)
-        turn_p(0,0)
-        exp(0,1)
-        turn_p(0,1)
+        cast_v1()
+        gather_v(1, 0)
         pick_vs(0)
         pick_vs(1)
-        turn_v(1)
-        store_v(0)
-        store_v(1)
+        add_bias(0, 0)
+        add_bias(0, 1)
+        row_max(0)
+        add_bias(1, 0)
+        add_bias(1, 1)
         row_max(1)
-        exp(1,0)
-        turn_p(1,0)
-        exp(1,1)
-        turn_p(1,1)
-        tanh_gate()
-        weigh(0,0)
-        weigh(0,1)
-        quantize_v()
-        quantize_w(0,0,1)
-        product(0)
+        turn_v(0, 0)
+        turn_v(1, 0)
+        turn_v(0, 1)
+        exp(0, 0)
+        turn_p(0, 0)
+        exp(0, 1)
+        turn_p(0, 1)
+        store_v(0)
+        gather_v_vec()
+        exp(1, 0)
+        turn_p(1, 0)
+        turn_v(1, 1)
+        exp(1, 1)
+        turn_p(1, 1)
+        store_v(1)
+        make_gate()
+        weigh(0, 0)
+        weigh(0, 1)
+        quantize_v(0)
+        quantize_w(0, 0, 1)
         row_sum()
-        weigh(1,0)
+        weigh(1, 0)
         invert()
-        make_factor(0)
-        make_factor(1)
-        weigh(1,1)
-        quantize_w(1,0,0)
-        quantize_w(1,1,1)
+        weigh(1, 1)
+        quantize_v(1)
+        product(0)
+        quantize_w(1, 0, 0)
+        quantize_w(1, 1, 1)
         product(1)
         finish(0)
         finish(1)

@@ -20,6 +20,9 @@ AX = mybir.AxisListType
 P = 128
 PASS = 512
 BANK_OF = {"pos_ps0":0,"pos_ps1":1,"row_ps0":2,"row_ps1":3,"a_ps00":4,"a_ps01":5,"a_ps10":6,"a_ps11":7,"vs_ps0":0,"vs_ps1":1,"vt_ps0":2,"vt_ps1":3,"pt_ps00":4,"pt_ps01":5,"pt_ps10":6,"pt_ps11":7,"y_ps0":0,"y_ps1":1}
+KB = 1024
+FIRST = 512
+HEAD = T - N + FIRST
 PREFIX = T - PASS
 
 
@@ -34,47 +37,46 @@ def tile_attend_soft_alibi_gate_srtq256n1024t2048_kernel(tc, qT, k_words, k_scal
             return slice(g * PASS, (g + 1) * PASS)
 
         offsets = keep.tile([P, N // 16], U16, name="offsets")
-        ks_win = keep.tile([P, T], U8, name="ks_win")
         v0_lo = keep.tile([P, T // 2], F32, name="v0_lo")
         ident = keep.tile([P, P], F32, name="ident")
-        KB = 1024
-        v0_hi = late.tile([P, T // 2], F32, name="v0_hi", offset=0)
+        ks_win = keep.tile([P, T], U8, name="ks_win")
         warm = late.tile([P, 12 * KB], F32, name="warm", offset=0)
+        v0_hi = late.tile([P, T // 2], F32, name="v0_hi", offset=0)
+        og_sb = late.tile([P, 2, DV], F32, name="og_sb", offset=34 * KB)
         q_raw = late.tile([P, 4, NQ], F32, name="q_raw", offset=4 * KB)
-        kw_win = late.tile([P, T], I32, name="kw_win", offset=40 * KB)
+        vs_g = late.tile([P, N], F32, name="vs_g", offset=6 * KB)
+        pos_col = [late.tile([P, 4], F32, name=f"pos_col{g}", offset=4 * KB + 32 * g) for g in range(2)]
         vs_win = late.tile([P, T], F32, name="vs_win", offset=16 * KB)
         v1_win = late.tile([P, T], F32, name="v1_win", offset=24 * KB)
-        og_sb = late.tile([P, 2, DV], F32, name="og_sb", offset=32 * KB)
-        slope_col = [late.tile([P, 1], F32, name=f"slope_col{h}", offset=34 * KB + 32 * h) for h in range(2)]
-        v_cast = [late.tile([P, T], BF16, name="v_cast0", offset=35 * KB), late.tile([P, PREFIX], BF16, name="v_cast1", offset=4 * KB + 32)]
-        pos_win = late.tile([P, T], F32, name="pos_win", offset=48 * KB)
+        v_cast = [late.tile([P, T], BF16, name="v_cast0", offset=32 * KB), late.tile([P, PREFIX], BF16, name="v_cast1", offset=4 * KB + 64 - 2 * PREFIX)]
+        q_bf = keep.tile([P, NQ, 4], BF16, name="q_bf", align_bytes=64)
+        vs_col = late.tile([P, 2, 4], F32, name="vs_col", offset=18 * KB)
+        p_sb = [late.tile([P, 2, 4, P], F32, name="p_sb0", offset=0), keep.tile([P, 2, 4, P], F32, name="p_sb1")]
+        kw_win = late.tile([P, T], I32, name="kw_win", offset=8 * KB)
+        pos_win = keep.tile([P, T], F32, name="pos_win")
         kw_g = late.tile([P, N], U32, name="kw_g", align_bytes=64, offset=48 * KB)
-        vs_g = late.tile([P, N], F32, name="vs_g", offset=40 * KB)
+        slope_col = [late.tile([P, 1], F32, name=f"slope_col{h}", offset=(56 + 2 * h) * KB) for h in range(2)]
+        v_g11 = late.tile([P, PASS], BF16, name="v_g11", offset=56 * KB)
         s_sb = [late.tile([P, N], F32, name=f"s_sb{h}", offset=(16 + 4 * h) * KB) for h in range(2)]
         gate_tanh = late.tile([P, 2, DV], F32, name="gate_tanh", offset=20 * KB)
-        pos_col = [late.tile([P, 4], F32, name=f"pos_col{g}", offset=4 * KB + 32 * g) for g in range(2)]
-        v_g0 = keep.tile([P, N], BF16, name="v_g0")
-        v_g10 = keep.tile([P, PASS], BF16, name="v_g10")
-        v_g11 = late.tile([P, PASS], BF16, name="v_g11", offset=56 * KB)
-        v_g = {(0, 0): v_g0[:, slots(0)], (0, 1): v_g0[:, slots(1)], (1, 0): v_g10[:], (1, 1): v_g11[:]}
-        pos_g = keep.tile([P, N], F32, name="pos_g")
+        pos_g = [late.tile([P, PASS], F32, name="pos_g0", offset=48 * KB), keep.tile([P, PASS], F32, name="pos_g1")]
         ks_g = keep.tile([P, N], U8, name="ks_g", align_bytes=64)
-        q_bf = late.tile([P, NQ, 4], BF16, name="q_bf", align_bytes=64, offset=35 * KB)
-        q_codes = late.tile([P, NQ], U32, name="q_codes", align_bytes=64, offset=44 * KB)
+        q_codes = late.tile([P, NQ], U32, name="q_codes", align_bytes=64, offset=14 * KB)
+        pos_all = keep.tile([P, N], F32, name="pos_all")
+        v_g00 = keep.tile([P, PASS], BF16, name="v_g00")
+        v_g01 = late.tile([P, PASS], BF16, name="v_g01", offset=5 * KB)
+        v_g10 = keep.tile([P, PASS], BF16, name="v_g10")
+        v_g = {(0, 0): v_g00[:], (0, 1): v_g01[:], (1, 0): v_g10[:], (1, 1): v_g11[:]}
         q_scales = keep.tile([P, NQ], U8, name="q_scales", align_bytes=64)
-        pos_all = late.tile([P, N], F32, name="pos_all", offset=56 * KB)
-        vs_col = late.tile([P, 2, 4], F32, name="vs_col", offset=4 * KB + 64)
         neg_max = [keep.tile([P, 1], F32, name=f"neg_max{h}") for h in range(2)]
-        half_sum = keep.tile([P, 2, 2], F32, name="half_sum")
-        p_sb = [late.tile([P, 2, 4, P], F32, name="p_sb0", offset=5 * KB), keep.tile([P, 2, 4, P], F32, name="p_sb1")]
-        v_bf = keep.tile([P, 2, DV, 4], BF16, name="v_bf", align_bytes=64)
-        v_words = v_bf[:].rearrange("p g c t -> p (g c t)").bitcast(F32).rearrange("p (g f c u) -> p g f c u", g=2, f=2, u=2)
+        v_bf = [late.tile([P, DV, 4], BF16, name=f"v_bf{g}", align_bytes=64, offset=(16 + 6 * g) * KB) for g in range(2)]
         v_codes = keep.tile([P, 2, DV], U32, name="v_codes", align_bytes=64)
         v_scales = keep.tile([P, 2, DV], U8, name="v_scales", align_bytes=64)
         gate = keep.tile([P, 2, DV], F32, name="gate")
         w_bf = [keep.tile([P, 2, P, 4], BF16, name=f"w_bf{h}", align_bytes=64) for h in range(2)]
         w_codes = [keep.tile([P, 2, P], U32, name=f"w_codes{h}", align_bytes=64) for h in range(2)]
         w_scales = [keep.tile([P, 2, P], U8, name=f"w_scales{h}", align_bytes=64) for h in range(2)]
+        half_sum = keep.tile([P, 2], F32, name="half_sum")
         total = keep.tile([P, 2], F32, name="total")
         inv = keep.tile([P, 2], F32, name="inv")
         res = [keep.tile([P, DV], F32, name=f"res{h}") for h in range(2)]
@@ -92,9 +94,12 @@ def tile_attend_soft_alibi_gate_srtq256n1024t2048_kernel(tc, qT, k_words, k_scal
 
         nc.vector.memset(ks_win[:].bitcast(I32), 0)
         nc.vector.memset(pos_win[:], 0.0)
+        for h in range(2):
+            nc.gpsimd.dma_start(out=slope_col[h][:], in_=slope[0, h * P : (h + 1) * P, :])
         make_identity(nc, ident[:])
 
         nc.sync.dma_start(offsets[:], offs)
+        kw_hbm = k_words[0].rearrange("p t r -> p (t r)").bitcast(I32)
         nc.sync.dma_start(out=v0_lo[:], in_=vT[0:P, tokens(0)])
         ks_hbm = k_scales[0].bitcast(I32)
         for quad in range(4):
@@ -102,26 +107,28 @@ def tile_attend_soft_alibi_gate_srtq256n1024t2048_kernel(tc, qT, k_words, k_scal
         nc.sync.dma_start(out=pos_win[0:1, :], in_=pos[0:1, :])
         nc.scalar.activation(out=warm[32:64, 0:1], in_=pos_win[32:64, 0:1], func=ACT.Exp)
         nc.sync.dma_start(out=v0_hi[:], in_=vT[0:P, tokens(1)])
-        nc.sync.dma_start(out=kw_win[:], in_=k_words[0].rearrange("p t r -> p (t r)").bitcast(I32))
+        nc.sync.dma_start(out=kw_win[:, 0:HEAD], in_=kw_hbm[:, 0:HEAD])
         nc.sync.dma_start(out=q_raw[:], in_=qT[0].rearrange("(p j) w -> p j w", j=4))
-        nc.sync.dma_start(out=slope_col[0][:], in_=slope[0, 0:P, :])
-        nc.sync.dma_start(out=slope_col[1][:], in_=slope[0, P : 2 * P, :])
+        nc.sync.dma_start(out=kw_win[:, HEAD:T], in_=kw_hbm[:, HEAD:T])
         nc.sync.dma_start(out=vs_win[:], in_=vs)
         nc.sync.dma_start(out=v1_win[:, 0:PREFIX], in_=vT[P : 2 * P, 0:PREFIX])
         nc.sync.dma_start(out=v1_win[:, PREFIX:T], in_=vT[P : 2 * P, PREFIX:T])
-        nc.sync.dma_start(out=og_sb[:], in_=og[0].rearrange("(h p) e -> p h e", p=P))
 
         def gather_scales():
             nc.vector.tensor_copy(ks_g[:], ks_win[:].indirect(offsets[:]))
 
         def gather_pos(g):
-            nc.vector.tensor_copy(pos_g[:, slots(g)], pos_win[:].indirect(half_list(g)))
+            nc.vector.tensor_copy(pos_g[g][:], pos_win[:].indirect(half_list(g)))
 
         def gather_vs_all():
             nc.vector.tensor_copy(vs_g[:], vs_win[:].indirect(offsets[:]))
 
-        def gather_keys(g):
-            nc.vector.tensor_copy(kw_g[:, slots(g)], kw_win[:].bitcast(U32).indirect(half_list(g)))
+        def gather_keys():
+            nc.vector.tensor_copy(kw_g[:, 0:FIRST], kw_win[:, 0:HEAD].bitcast(U32).indirect(offsets[:, 0 : FIRST // 16]))
+            nc.vector.tensor_copy(kw_g[:, FIRST:N], kw_win[:].bitcast(U32).indirect(offsets[:, FIRST // 16 : N // 16]))
+
+        def load_og():
+            nc.sync.dma_start(out=og_sb[:], in_=og[0].rearrange("(h p) e -> p h e", p=P))
 
         def cast_q():
             nc.scalar.copy(out=q_bf[:], in_=q_raw[:].rearrange("p j w -> p w j"))
@@ -132,7 +139,7 @@ def tile_attend_soft_alibi_gate_srtq256n1024t2048_kernel(tc, qT, k_words, k_scal
         def turn_pos(g):
             ps = new_bank(f"pos_ps{g}", [P, 4, P])
             for c in range(4):
-                nc.tensor.transpose(ps[:, c, :], pos_g[:, g * PASS + c * P : g * PASS + (c + 1) * P], ident[:])
+                nc.tensor.transpose(ps[:, c, :], pos_g[g][:, c * P : (c + 1) * P], ident[:])
 
         def pick_pos(g):
             nc.scalar.copy(out=pos_col[g][:], in_=bank[f"pos_ps{g}"][:, :, 0])
@@ -158,9 +165,16 @@ def tile_attend_soft_alibi_gate_srtq256n1024t2048_kernel(tc, qT, k_words, k_scal
         def row_max(h):
             nc.vector.tensor_reduce(out=neg_max[h][:], in_=s_sb[h][:], axis=AX.X, op=ALU.max, negate=True)
 
-        def exp(h, g):
+        def exp(h):
+            nc.scalar.activation(out=p_sb[h][:].rearrange("p g t s -> p g s t"), in_=s_sb[h][:].rearrange("p (g s t) -> p g s t", g=2, t=4),
+                                 func=ACT.Exp, bias=neg_max[h][:], accum_out=total[:, h : h + 1])
+
+        def exp_half(h, g):
             nc.scalar.activation(out=p_sb[h][:, g, :, :].rearrange("p t s -> p s t"), in_=s_sb[h][:, slots(g)].rearrange("p (s t) -> p s t", t=4),
-                                 func=ACT.Exp, bias=neg_max[h][:], accum_out=half_sum[:, h, g : g + 1])
+                                 func=ACT.Exp, bias=neg_max[h][:], accum_out=half_sum[:, g : g + 1])
+
+        def join_sums(h):
+            nc.scalar.activation(out=total[:, h : h + 1], in_=half_sum[:, 0:1], func=ACT.Identity, bias=half_sum[:, 1:2])
 
         def turn_vs(g):
             ps = new_bank(f"vs_ps{g}", [P, 4, P])
@@ -176,14 +190,11 @@ def tile_attend_soft_alibi_gate_srtq256n1024t2048_kernel(tc, qT, k_words, k_scal
         def cast_v1():
             nc.scalar.activation(out=v_cast[1][:], in_=v1_win[:, 0:PREFIX], func=ACT.Copy)
 
-        def gather_v(f, g):
-            nc.scalar.activation(out=v_g[f, g], in_=v_cast[f][:].indirect(half_list(g)), func=ACT.Copy)
-
-        def gather_v_all(f):
-            nc.scalar.activation(out=v_g0[:], in_=v_cast[f][:].indirect(offsets[:]), func=ACT.Copy)
-
         def gather_v_vec():
             nc.vector.tensor_copy(v_g[1, 1], v1_win[:].indirect(half_list(1)))
+
+        def gather_v(f, g):
+            nc.scalar.activation(out=v_g[f, g], in_=v_cast[f][:].indirect(half_list(g)), func=ACT.Copy)
 
         def turn_v(f, g):
             pairs = v_g[f, g].bitcast(F32)
@@ -192,11 +203,11 @@ def tile_attend_soft_alibi_gate_srtq256n1024t2048_kernel(tc, qT, k_words, k_scal
                 nc.tensor.transpose(ps[:, f, u, :], pairs[:, u : 2 * P : 2], ident[:])
 
         def store_v(g):
-            nc.scalar.copy(out=v_words[:, g, :, :, :], in_=bank[f"vt_ps{g}"][:].rearrange("p f u c -> p f c u"))
+            nc.scalar.copy(out=v_bf[g][:].rearrange("p c t -> p (c t)").bitcast(F32).rearrange("p (f c u) -> p f c u", f=2, u=2), in_=bank[f"vt_ps{g}"][:].rearrange("p f u c -> p f c u"))
 
         def quantize_v(g):
             nc.vector.quantize_mx(out=v_codes[:, g, :].bitcast(FP8X4), scales=v_scales[:, g, :],
-                                  in_=v_bf[:, g, :, :].rearrange("p c t -> p (c t)"))
+                                  in_=v_bf[g][:].rearrange("p c t -> p (c t)"))
 
         def make_gate():
             nc.scalar.activation(out=gate_tanh[:], in_=og_sb[:], func=ACT.Tanh, scale=0.5)
@@ -217,9 +228,6 @@ def tile_attend_soft_alibi_gate_srtq256n1024t2048_kernel(tc, qT, k_words, k_scal
                                   scales=w_scales[h][:, passes, :].rearrange("p g q -> p (g q)"),
                                   in_=w_bf[h][:, passes, :, :].rearrange("p g q t -> p (g q t)"))
 
-        def row_sum():
-            nc.vector.tensor_reduce(out=total[:], in_=half_sum[:], axis=AX.X, op=ALU.add)
-
         def invert():
             nc.vector.reciprocal(inv[:], total[:])
 
@@ -234,22 +242,23 @@ def tile_attend_soft_alibi_gate_srtq256n1024t2048_kernel(tc, qT, k_words, k_scal
             nc.sync.dma_start(out=out[0, h * P : (h + 1) * P, :], in_=res[h][:])
 
         gather_scales()
-        cast_v0(0)
-        cast_v0(1)
-        gather_v_all(0)
-        cast_q()
         gather_pos(0)
         gather_pos(1)
+        gather_keys()
+        cast_v0(0)
+        cast_v0(1)
+        gather_v(0, 0)
+        cast_q()
         turn_pos(0)
         pick_pos(0)
         spread_pos(0)
         turn_pos(1)
         pick_pos(1)
         spread_pos(1)
+        gather_v(0, 1)
+        load_og()
         store_pos(0)
         store_pos(1)
-        gather_keys(0)
-        gather_keys(1)
         quantize_q()
         scores(0, 0)
         scores(0, 1)
@@ -260,40 +269,39 @@ def tile_attend_soft_alibi_gate_srtq256n1024t2048_kernel(tc, qT, k_words, k_scal
         turn_vs(1)
         cast_v1()
         gather_v(1, 0)
-        pick_vs(0)
-        pick_vs(1)
         add_bias(0, 0)
         add_bias(0, 1)
         row_max(0)
         add_bias(1, 0)
         add_bias(1, 1)
+        gather_v_vec()
         row_max(1)
         turn_v(0, 0)
         turn_v(1, 0)
         turn_v(0, 1)
-        exp(0, 0)
+        exp(0)
         turn_p(0, 0)
-        exp(0, 1)
         turn_p(0, 1)
+        pick_vs(0)
+        pick_vs(1)
         store_v(0)
-        gather_v_vec()
-        exp(1, 0)
-        turn_p(1, 0)
         turn_v(1, 1)
-        exp(1, 1)
+        exp_half(1, 0)
+        turn_p(1, 0)
+        exp_half(1, 1)
         turn_p(1, 1)
         store_v(1)
+        join_sums(1)
         make_gate()
         weigh(0, 0)
         weigh(0, 1)
         quantize_v(0)
         quantize_w(0, 0, 1)
-        row_sum()
         weigh(1, 0)
-        invert()
-        weigh(1, 1)
         quantize_v(1)
+        invert()
         product(0)
+        weigh(1, 1)
         quantize_w(1, 0, 0)
         quantize_w(1, 1, 1)
         product(1)

@@ -19,7 +19,7 @@ AX = mybir.AxisListType
 
 P = 128
 PASS = 512
-BANK_OF = {"pos_ps0":0,"pos_ps1":1,"row_ps0":2,"row_ps1":3,"a_ps00":4,"a_ps01":5,"a_ps10":6,"a_ps11":7,"vs_ps0":0,"vs_ps1":1,"vt_ps0":2,"vt_ps1":3,"pt_ps00":4,"pt_ps01":5,"pt_ps10":6,"pt_ps11":7,"y_ps0":0,"y_ps1":1}
+BANK_OF = {"slope_ps":4,"vs_ps0":0,"vs_ps1":1,"a_ps00":2,"a_ps01":3,"a_ps10":6,"a_ps11":7,"vt_ps0":2,"vt_ps1":3,"pt_ps00":4,"pt_ps01":5,"pt_ps10":6,"pt_ps11":7,"y_ps0":0,"y_ps1":1}
 KB = 1024
 FIRST = 512
 HEAD = T - N + FIRST
@@ -37,39 +37,38 @@ def tile_attend_soft_alibi_gate_srtq256n1024t2048_kernel(tc, qT, k_words, k_scal
             return slice(g * PASS, (g + 1) * PASS)
 
         offsets = keep.tile([P, N // 16], U16, name="offsets")
-        v0_lo = keep.tile([P, T // 2], F32, name="v0_lo")
+        v0_lo = late.tile([P, T // 2], F32, name="v0_lo", offset=68 * KB)
         ident = keep.tile([P, P], F32, name="ident")
         ks_win = keep.tile([P, T], U8, name="ks_win")
+        slope_rows = keep.tile([P, P], F32, name="slope_rows")
+        vs_win = late.tile([P, T], F32, name="vs_win", offset=48 * KB)
         warm = late.tile([P, 12 * KB], F32, name="warm", offset=0)
         v0_hi = late.tile([P, T // 2], F32, name="v0_hi", offset=0)
-        og_sb = late.tile([P, 2, DV], F32, name="og_sb", offset=34 * KB)
         q_raw = late.tile([P, 4, NQ], F32, name="q_raw", offset=4 * KB)
-        vs_g = late.tile([P, N], F32, name="vs_g", offset=6 * KB)
-        pos_col = [late.tile([P, 4], F32, name=f"pos_col{g}", offset=4 * KB + 32 * g) for g in range(2)]
-        vs_win = late.tile([P, T], F32, name="vs_win", offset=16 * KB)
-        v1_win = late.tile([P, T], F32, name="v1_win", offset=24 * KB)
-        v_cast = [late.tile([P, T], BF16, name="v_cast0", offset=32 * KB), late.tile([P, PREFIX], BF16, name="v_cast1", offset=4 * KB + 64 - 2 * PREFIX)]
-        q_bf = keep.tile([P, NQ, 4], BF16, name="q_bf", align_bytes=64)
-        vs_col = late.tile([P, 2, 4], F32, name="vs_col", offset=18 * KB)
-        p_sb = [late.tile([P, 2, 4, P], F32, name="p_sb0", offset=0), keep.tile([P, 2, 4, P], F32, name="p_sb1")]
-        kw_win = late.tile([P, T], I32, name="kw_win", offset=8 * KB)
-        pos_win = keep.tile([P, T], F32, name="pos_win")
-        kw_g = late.tile([P, N], U32, name="kw_g", align_bytes=64, offset=48 * KB)
-        slope_col = [late.tile([P, 1], F32, name=f"slope_col{h}", offset=(56 + 2 * h) * KB) for h in range(2)]
-        v_g11 = late.tile([P, PASS], BF16, name="v_g11", offset=56 * KB)
-        s_sb = [late.tile([P, N], F32, name=f"s_sb{h}", offset=(16 + 4 * h) * KB) for h in range(2)]
-        gate_tanh = late.tile([P, 2, DV], F32, name="gate_tanh", offset=20 * KB)
-        pos_g = [late.tile([P, PASS], F32, name="pos_g0", offset=48 * KB), keep.tile([P, PASS], F32, name="pos_g1")]
-        ks_g = keep.tile([P, N], U8, name="ks_g", align_bytes=64)
-        q_codes = late.tile([P, NQ], U32, name="q_codes", align_bytes=64, offset=14 * KB)
-        pos_all = keep.tile([P, N], F32, name="pos_all")
         v_g00 = keep.tile([P, PASS], BF16, name="v_g00")
-        v_g01 = late.tile([P, PASS], BF16, name="v_g01", offset=5 * KB)
+        v_g01 = late.tile([P, PASS], BF16, name="v_g01", offset=4 * KB)
+        kw_win = late.tile([P, T], I32, name="kw_win", offset=40 * KB)
+        vs_g = [keep.tile([P, PASS], F32, name=f"vs_g{g}") for g in range(2)]
+        pos_g = late.tile([P, N], F32, name="pos_g", offset=44 * KB)
+        q_codes = late.tile([P, NQ], U32, name="q_codes", align_bytes=64, offset=43 * KB)
+        pos_win = late.tile([P, T], F32, name="pos_win", offset=16 * KB)
+        v1_win = late.tile([P, T], F32, name="v1_win", offset=24 * KB)
+        v_cast = [late.tile([P, T], BF16, name="v_cast0", offset=32 * KB), late.tile([P, T], BF16, name="v_cast1", offset=36 * KB - 64)]
+        og_sb = late.tile([P, 2, DV], F32, name="og_sb", offset=32 * KB)
+        p_sb = [late.tile([P, 2, 4, P], F32, name="p_sb0", offset=37 * KB), keep.tile([P, 2, 4, P], F32, name="p_sb1")]
+        slope_col = [late.tile([P, 1], F32, name=f"slope_col{h}", offset=68 * KB + 32 * h) for h in range(2)]
+        v_g11 = keep.tile([P, PASS], BF16, name="v_g11")
+        s_sb = [late.tile([P, N], F32, name=f"s_sb{h}", offset=(60 + 4 * h) * KB) for h in range(2)]
+        vs_col = late.tile([P, 2, 4], F32, name="vs_col", offset=6 * KB)
+        gate_tanh = late.tile([P, 2, DV], F32, name="gate_tanh", offset=64 * KB)
+        v_bf = [late.tile([P, DV, 4], BF16, name="v_bf0", align_bytes=64, offset=60 * KB), late.tile([P, DV, 4], BF16, name="v_bf1", align_bytes=64, offset=66 * KB)]
+        kw_g = late.tile([P, N], U32, name="kw_g", align_bytes=64, offset=48 * KB)
+        ks_g = keep.tile([P, N], U8, name="ks_g", align_bytes=64)
+        q_bf = keep.tile([P, NQ, 4], BF16, name="q_bf", align_bytes=64)
         v_g10 = keep.tile([P, PASS], BF16, name="v_g10")
         v_g = {(0, 0): v_g00[:], (0, 1): v_g01[:], (1, 0): v_g10[:], (1, 1): v_g11[:]}
         q_scales = keep.tile([P, NQ], U8, name="q_scales", align_bytes=64)
         neg_max = [keep.tile([P, 1], F32, name=f"neg_max{h}") for h in range(2)]
-        v_bf = [late.tile([P, DV, 4], BF16, name=f"v_bf{g}", align_bytes=64, offset=(16 + 6 * g) * KB) for g in range(2)]
         v_codes = keep.tile([P, 2, DV], U32, name="v_codes", align_bytes=64)
         v_scales = keep.tile([P, 2, DV], U8, name="v_scales", align_bytes=64)
         gate = keep.tile([P, 2, DV], F32, name="gate")
@@ -93,9 +92,8 @@ def tile_attend_soft_alibi_gate_srtq256n1024t2048_kernel(tc, qT, k_words, k_scal
             return slice(half * T // 2, (half + 1) * T // 2)
 
         nc.vector.memset(ks_win[:].bitcast(I32), 0)
-        nc.vector.memset(pos_win[:], 0.0)
-        for h in range(2):
-            nc.gpsimd.dma_start(out=slope_col[h][:], in_=slope[0, h * P : (h + 1) * P, :])
+        nc.vector.memset(slope_rows[:], 0.0)
+        nc.vector.memset(vs_win[:], 0.0)
         make_identity(nc, ident[:])
 
         nc.sync.dma_start(offsets[:], offs)
@@ -104,24 +102,24 @@ def tile_attend_soft_alibi_gate_srtq256n1024t2048_kernel(tc, qT, k_words, k_scal
         ks_hbm = k_scales[0].bitcast(I32)
         for quad in range(4):
             nc.sync.dma_start(out=ks_win[32 * quad : 32 * quad + 4, :].bitcast(I32), in_=ks_hbm[4 * quad : 4 * quad + 4, :])
-        nc.sync.dma_start(out=pos_win[0:1, :], in_=pos[0:1, :])
-        nc.scalar.activation(out=warm[32:64, 0:1], in_=pos_win[32:64, 0:1], func=ACT.Exp)
+        nc.scalar.activation(out=warm[32:64, 0:1], in_=vs_win[32:64, 0:1], func=ACT.Exp)
+        nc.sync.dma_start(out=slope_rows[0:2, :], in_=slope[0].rearrange("(h p) o -> h (p o)", p=P))
+        nc.sync.dma_start(out=vs_win[0:1, :], in_=vs[0:1, :])
         nc.sync.dma_start(out=v0_hi[:], in_=vT[0:P, tokens(1)])
-        nc.sync.dma_start(out=kw_win[:, 0:HEAD], in_=kw_hbm[:, 0:HEAD])
+        nc.sync.dma_start(out=kw_win[:], in_=k_words[0].rearrange("p t r -> p (t r)").bitcast(I32))
         nc.sync.dma_start(out=q_raw[:], in_=qT[0].rearrange("(p j) w -> p j w", j=4))
-        nc.sync.dma_start(out=kw_win[:, HEAD:T], in_=kw_hbm[:, HEAD:T])
-        nc.sync.dma_start(out=vs_win[:], in_=vs)
-        nc.sync.dma_start(out=v1_win[:, 0:PREFIX], in_=vT[P : 2 * P, 0:PREFIX])
-        nc.sync.dma_start(out=v1_win[:, PREFIX:T], in_=vT[P : 2 * P, PREFIX:T])
+        nc.sync.dma_start(out=pos_win[:], in_=pos)
+        nc.sync.dma_start(out=v1_win[:, tokens(0)], in_=vT[P : 2 * P, tokens(0)])
+        nc.sync.dma_start(out=v1_win[:, tokens(1)], in_=vT[P : 2 * P, tokens(1)])
 
         def gather_scales():
             nc.vector.tensor_copy(ks_g[:], ks_win[:].indirect(offsets[:]))
 
         def gather_pos(g):
-            nc.vector.tensor_copy(pos_g[g][:], pos_win[:].indirect(half_list(g)))
+            nc.vector.tensor_copy(pos_g[:, slots(g)], pos_win[:, 0 : (PREFIX, T)[g]].indirect(half_list(g)))
 
-        def gather_vs_all():
-            nc.vector.tensor_copy(vs_g[:], vs_win[:].indirect(offsets[:]))
+        def gather_vs(g):
+            nc.vector.tensor_copy(vs_g[g][:], vs_win[:].indirect(half_list(g)))
 
         def gather_keys():
             nc.vector.tensor_copy(kw_g[:, 0:FIRST], kw_win[:, 0:HEAD].bitcast(U32).indirect(offsets[:, 0 : FIRST // 16]))
@@ -130,27 +128,17 @@ def tile_attend_soft_alibi_gate_srtq256n1024t2048_kernel(tc, qT, k_words, k_scal
         def load_og():
             nc.sync.dma_start(out=og_sb[:], in_=og[0].rearrange("(h p) e -> p h e", p=P))
 
+        def turn_slope():
+            ps = new_bank("slope_ps", [P, P])
+            nc.tensor.transpose(ps[:], slope_rows[:], ident[:])
+            for h in range(2):
+                nc.scalar.copy(out=slope_col[h][:], in_=ps[:, h : h + 1])
+
         def cast_q():
             nc.scalar.copy(out=q_bf[:], in_=q_raw[:].rearrange("p j w -> p w j"))
 
         def quantize_q():
             nc.vector.quantize_mx(out=q_codes[:].bitcast(FP8X4), scales=q_scales[:], in_=q_bf[:].rearrange("p w j -> p (w j)"))
-
-        def turn_pos(g):
-            ps = new_bank(f"pos_ps{g}", [P, 4, P])
-            for c in range(4):
-                nc.tensor.transpose(ps[:, c, :], pos_g[g][:, c * P : (c + 1) * P], ident[:])
-
-        def pick_pos(g):
-            nc.scalar.copy(out=pos_col[g][:], in_=bank[f"pos_ps{g}"][:, :, 0])
-
-        def spread_pos(g):
-            ps = new_bank(f"row_ps{g}", [P, 4, P])
-            for c in range(4):
-                nc.tensor.transpose(ps[:, c, :], pos_col[g][:, c : c + 1].to_broadcast([P, P]), ident[:])
-
-        def store_pos(g):
-            nc.scalar.copy(out=pos_all[:, slots(g)], in_=bank[f"row_ps{g}"][:].rearrange("p c n -> p (c n)"))
 
         def scores(h, g):
             qs = slice(h * P, (h + 1) * P)
@@ -159,7 +147,7 @@ def tile_attend_soft_alibi_gate_srtq256n1024t2048_kernel(tc, qT, k_words, k_scal
                                 rhs=kw_g[:, slots(g)].bitcast(FP8X4), rhs_scale=ks_g[:, slots(g)], start=True, stop=True)
 
         def add_bias(h, g):
-            nc.vector.scalar_tensor_tensor(out=s_sb[h][:, slots(g)], in0=pos_all[:, slots(g)], scalar=slope_col[h][:],
+            nc.vector.scalar_tensor_tensor(out=s_sb[h][:, slots(g)], in0=pos_g[:, slots(g)], scalar=slope_col[h][:],
                                            in1=bank[f"a_ps{h}{g}"][:], op0=ALU.mult, op1=ALU.add)
 
         def row_max(h):
@@ -179,7 +167,7 @@ def tile_attend_soft_alibi_gate_srtq256n1024t2048_kernel(tc, qT, k_words, k_scal
         def turn_vs(g):
             ps = new_bank(f"vs_ps{g}", [P, 4, P])
             for t in range(4):
-                nc.tensor.transpose(ps[:, t, :], vs_g[:, g * PASS + t : (g + 1) * PASS : 4], ident[:])
+                nc.tensor.transpose(ps[:, t, :], vs_g[g][:, t:PASS:4], ident[:])
 
         def pick_vs(g):
             nc.scalar.copy(out=vs_col[:, g, :], in_=bank[f"vs_ps{g}"][:, :, 0])
@@ -187,11 +175,8 @@ def tile_attend_soft_alibi_gate_srtq256n1024t2048_kernel(tc, qT, k_words, k_scal
         def cast_v0(half):
             nc.scalar.activation(out=v_cast[0][:, tokens(half)], in_=(v0_lo, v0_hi)[half][:], func=ACT.Copy)
 
-        def cast_v1():
-            nc.scalar.activation(out=v_cast[1][:], in_=v1_win[:, 0:PREFIX], func=ACT.Copy)
-
-        def gather_v_vec():
-            nc.vector.tensor_copy(v_g[1, 1], v1_win[:].indirect(half_list(1)))
+        def cast_v1(half):
+            nc.scalar.activation(out=v_cast[1][:, tokens(half)], in_=v1_win[:, tokens(half)], func=ACT.Copy)
 
         def gather_v(f, g):
             nc.scalar.activation(out=v_g[f, g], in_=v_cast[f][:].indirect(half_list(g)), func=ACT.Copy)
@@ -242,66 +227,61 @@ def tile_attend_soft_alibi_gate_srtq256n1024t2048_kernel(tc, qT, k_words, k_scal
             nc.sync.dma_start(out=out[0, h * P : (h + 1) * P, :], in_=res[h][:])
 
         gather_scales()
-        gather_pos(0)
-        gather_pos(1)
+        gather_vs(0)
+        gather_vs(1)
         gather_keys()
+        turn_vs(0)
+        turn_vs(1)
         cast_v0(0)
+        turn_slope()
         cast_v0(1)
         gather_v(0, 0)
         cast_q()
-        turn_pos(0)
-        pick_pos(0)
-        spread_pos(0)
-        turn_pos(1)
-        pick_pos(1)
-        spread_pos(1)
+        pick_vs(0)
+        pick_vs(1)
         gather_v(0, 1)
         load_og()
-        store_pos(0)
-        store_pos(1)
         quantize_q()
+        gather_pos(0)
+        gather_pos(1)
         scores(0, 0)
         scores(0, 1)
         scores(1, 0)
         scores(1, 1)
-        gather_vs_all()
-        turn_vs(0)
-        turn_vs(1)
-        cast_v1()
+        cast_v1(0)
+        cast_v1(1)
         gather_v(1, 0)
+        gather_v(1, 1)
         add_bias(0, 0)
         add_bias(0, 1)
         row_max(0)
         add_bias(1, 0)
         add_bias(1, 1)
-        gather_v_vec()
         row_max(1)
         turn_v(0, 0)
         turn_v(1, 0)
         turn_v(0, 1)
+        turn_v(1, 1)
         exp(0)
         turn_p(0, 0)
         turn_p(0, 1)
-        pick_vs(0)
-        pick_vs(1)
         store_v(0)
-        turn_v(1, 1)
         exp_half(1, 0)
         turn_p(1, 0)
         exp_half(1, 1)
         turn_p(1, 1)
-        store_v(1)
         join_sums(1)
+        store_v(1)
         make_gate()
         weigh(0, 0)
         weigh(0, 1)
         quantize_v(0)
         quantize_w(0, 0, 1)
         weigh(1, 0)
+        weigh(1, 1)
         quantize_v(1)
         invert()
         product(0)
-        weigh(1, 1)
         quantize_w(1, 0, 0)
         quantize_w(1, 1, 1)
         product(1)

@@ -19,7 +19,7 @@ AX = mybir.AxisListType
 
 P = 128
 PASS = 512
-BANK_OF = {"slope_ps":4,"vs_ps0":0,"vs_ps1":1,"a_ps00":2,"a_ps01":3,"a_ps10":6,"a_ps11":7,"vt_ps0":2,"vt_ps1":3,"pt_ps00":4,"pt_ps01":5,"pt_ps10":6,"pt_ps11":7,"y_ps0":0,"y_ps1":1}
+BANK_OF = {"slope_ps":0,"vs_ps0":0,"vs_ps1":1,"a_ps00":2,"a_ps01":3,"a_ps10":6,"a_ps11":7,"vt_ps0":2,"vt_ps1":3,"pt_ps00":4,"pt_ps01":5,"pt_ps10":6,"pt_ps11":7,"y_ps0":0,"y_ps1":1}
 KB = 1024
 FIRST = 512
 HEAD = T - N + FIRST
@@ -40,7 +40,7 @@ def tile_attend_soft_alibi_gate_srtq256n1024t2048_kernel(tc, qT, k_words, k_scal
         v0_lo = late.tile([P, T // 2], F32, name="v0_lo", offset=68 * KB)
         ident = keep.tile([P, P], F32, name="ident")
         ks_win = keep.tile([P, T], U8, name="ks_win")
-        slope_rows = keep.tile([P, P], F32, name="slope_rows")
+        slope_rows = late.tile([P, P], F32, name="slope_rows", offset=8 * KB)
         vs_win = late.tile([P, T], F32, name="vs_win", offset=48 * KB)
         warm = late.tile([P, 12 * KB], F32, name="warm", offset=0)
         v0_hi = late.tile([P, T // 2], F32, name="v0_hi", offset=0)
@@ -56,7 +56,7 @@ def tile_attend_soft_alibi_gate_srtq256n1024t2048_kernel(tc, qT, k_words, k_scal
         v_cast = [late.tile([P, T], BF16, name="v_cast0", offset=32 * KB), late.tile([P, T], BF16, name="v_cast1", offset=36 * KB - 64)]
         og_sb = late.tile([P, 2, DV], F32, name="og_sb", offset=32 * KB)
         p_sb = [late.tile([P, 2, 4, P], F32, name="p_sb0", offset=37 * KB), keep.tile([P, 2, 4, P], F32, name="p_sb1")]
-        slope_col = [late.tile([P, 1], F32, name=f"slope_col{h}", offset=68 * KB + 32 * h) for h in range(2)]
+        slope_col = [late.tile([P, 1], F32, name=f"slope_col{h}", offset=7 * KB + 32 * h) for h in range(2)]
         v_g11 = keep.tile([P, PASS], BF16, name="v_g11")
         s_sb = [late.tile([P, N], F32, name=f"s_sb{h}", offset=(60 + 4 * h) * KB) for h in range(2)]
         vs_col = late.tile([P, 2, 4], F32, name="vs_col", offset=6 * KB)
@@ -75,7 +75,7 @@ def tile_attend_soft_alibi_gate_srtq256n1024t2048_kernel(tc, qT, k_words, k_scal
         w_bf = [keep.tile([P, 2, P, 4], BF16, name=f"w_bf{h}", align_bytes=64) for h in range(2)]
         w_codes = [keep.tile([P, 2, P], U32, name=f"w_codes{h}", align_bytes=64) for h in range(2)]
         w_scales = [keep.tile([P, 2, P], U8, name=f"w_scales{h}", align_bytes=64) for h in range(2)]
-        half_sum = keep.tile([P, 2], F32, name="half_sum")
+        half_sum = keep.tile([P, 2, 2], F32, name="half_sum")
         total = keep.tile([P, 2], F32, name="total")
         inv = keep.tile([P, 2], F32, name="inv")
         res = [keep.tile([P, DV], F32, name=f"res{h}") for h in range(2)]
@@ -92,7 +92,6 @@ def tile_attend_soft_alibi_gate_srtq256n1024t2048_kernel(tc, qT, k_words, k_scal
             return slice(half * T // 2, (half + 1) * T // 2)
 
         nc.vector.memset(ks_win[:].bitcast(I32), 0)
-        nc.vector.memset(slope_rows[:], 0.0)
         nc.vector.memset(vs_win[:], 0.0)
         make_identity(nc, ident[:])
 
@@ -103,10 +102,11 @@ def tile_attend_soft_alibi_gate_srtq256n1024t2048_kernel(tc, qT, k_words, k_scal
         for quad in range(4):
             nc.sync.dma_start(out=ks_win[32 * quad : 32 * quad + 4, :].bitcast(I32), in_=ks_hbm[4 * quad : 4 * quad + 4, :])
         nc.scalar.activation(out=warm[32:64, 0:1], in_=vs_win[32:64, 0:1], func=ACT.Exp)
-        nc.sync.dma_start(out=slope_rows[0:2, :], in_=slope[0].rearrange("(h p) o -> h (p o)", p=P))
         nc.sync.dma_start(out=vs_win[0:1, :], in_=vs[0:1, :])
+        nc.vector.memset(slope_rows[:], 0.0)
         nc.sync.dma_start(out=v0_hi[:], in_=vT[0:P, tokens(1)])
         nc.sync.dma_start(out=kw_win[:], in_=k_words[0].rearrange("p t r -> p (t r)").bitcast(I32))
+        nc.sync.dma_start(out=slope_rows[0:2, :], in_=slope[0].rearrange("(h p) o -> h (p o)", p=P))
         nc.sync.dma_start(out=q_raw[:], in_=qT[0].rearrange("(p j) w -> p j w", j=4))
         nc.sync.dma_start(out=pos_win[:], in_=pos)
         nc.sync.dma_start(out=v1_win[:, tokens(0)], in_=vT[P : 2 * P, tokens(0)])
@@ -153,16 +153,12 @@ def tile_attend_soft_alibi_gate_srtq256n1024t2048_kernel(tc, qT, k_words, k_scal
         def row_max(h):
             nc.vector.tensor_reduce(out=neg_max[h][:], in_=s_sb[h][:], axis=AX.X, op=ALU.max, negate=True)
 
-        def exp(h):
-            nc.scalar.activation(out=p_sb[h][:].rearrange("p g t s -> p g s t"), in_=s_sb[h][:].rearrange("p (g s t) -> p g s t", g=2, t=4),
-                                 func=ACT.Exp, bias=neg_max[h][:], accum_out=total[:, h : h + 1])
-
         def exp_half(h, g):
             nc.scalar.activation(out=p_sb[h][:, g, :, :].rearrange("p t s -> p s t"), in_=s_sb[h][:, slots(g)].rearrange("p (s t) -> p s t", t=4),
-                                 func=ACT.Exp, bias=neg_max[h][:], accum_out=half_sum[:, g : g + 1])
+                                 func=ACT.Exp, bias=neg_max[h][:], accum_out=half_sum[:, h, g : g + 1])
 
         def join_sums(h):
-            nc.scalar.activation(out=total[:, h : h + 1], in_=half_sum[:, 0:1], func=ACT.Identity, bias=half_sum[:, 1:2])
+            nc.scalar.activation(out=total[:, h : h + 1], in_=half_sum[:, h, 0:1], func=ACT.Identity, bias=half_sum[:, h, 1:2])
 
         def turn_vs(g):
             ps = new_bank(f"vs_ps{g}", [P, 4, P])
@@ -233,12 +229,12 @@ def tile_attend_soft_alibi_gate_srtq256n1024t2048_kernel(tc, qT, k_words, k_scal
         turn_vs(0)
         turn_vs(1)
         cast_v0(0)
-        turn_slope()
         cast_v0(1)
         gather_v(0, 0)
         cast_q()
         pick_vs(0)
         pick_vs(1)
+        turn_slope()
         gather_v(0, 1)
         load_og()
         quantize_q()
@@ -262,14 +258,16 @@ def tile_attend_soft_alibi_gate_srtq256n1024t2048_kernel(tc, qT, k_words, k_scal
         turn_v(1, 0)
         turn_v(0, 1)
         turn_v(1, 1)
-        exp(0)
+        exp_half(0, 0)
         turn_p(0, 0)
+        exp_half(0, 1)
         turn_p(0, 1)
         store_v(0)
         exp_half(1, 0)
         turn_p(1, 0)
         exp_half(1, 1)
         turn_p(1, 1)
+        join_sums(0)
         join_sums(1)
         store_v(1)
         make_gate()

@@ -21,6 +21,7 @@ P = 128
 PASS = 512
 BANK_OF = {"slope_ps":0,"vs_ps0":0,"vs_ps1":1,"a_ps00":2,"a_ps01":3,"a_ps10":6,"a_ps11":7,"vt_ps0":2,"vt_ps1":3,"pt_ps00":4,"pt_ps01":5,"pt_ps10":6,"pt_ps11":7,"y_ps0":0,"y_ps1":1}
 KB = 1024
+V1_CUTS = (0, 768, 1536, 2048)
 FIRST = 512
 HEAD = T - N + FIRST
 PREFIX = T - PASS
@@ -40,7 +41,7 @@ def tile_attend_soft_alibi_gate_srtq256n1024t2048_kernel(tc, qT, k_words, k_scal
         v0_lo = late.tile([P, T // 2], F32, name="v0_lo", offset=68 * KB)
         ident = keep.tile([P, P], F32, name="ident")
         ks_win = keep.tile([P, T], U8, name="ks_win")
-        slope_rows = late.tile([P, P], F32, name="slope_rows", offset=8 * KB)
+        slope_rows = late.tile([P, P], F32, name="slope_rows", offset=12 * KB)
         vs_win = late.tile([P, T], F32, name="vs_win", offset=48 * KB)
         warm = late.tile([P, 12 * KB], F32, name="warm", offset=0)
         v0_hi = late.tile([P, T // 2], F32, name="v0_hi", offset=0)
@@ -53,9 +54,9 @@ def tile_attend_soft_alibi_gate_srtq256n1024t2048_kernel(tc, qT, k_words, k_scal
         q_codes = late.tile([P, NQ], U32, name="q_codes", align_bytes=64, offset=43 * KB)
         pos_win = late.tile([P, T], F32, name="pos_win", offset=16 * KB)
         v1_win = late.tile([P, T], F32, name="v1_win", offset=24 * KB)
-        v_cast = [late.tile([P, T], BF16, name="v_cast0", offset=32 * KB), late.tile([P, T], BF16, name="v_cast1", offset=36 * KB - 64)]
+        v_cast = [late.tile([P, T], BF16, name="v_cast0", offset=32 * KB), late.tile([P, T], BF16, name="v_cast1", offset=7 * KB + 64)]
         og_sb = late.tile([P, 2, DV], F32, name="og_sb", offset=32 * KB)
-        p_sb = [late.tile([P, 2, 4, P], F32, name="p_sb0", offset=37 * KB), keep.tile([P, 2, 4, P], F32, name="p_sb1")]
+        p_sb = [late.tile([P, 2, 4, P], F32, name="p_sb0", offset=24 * KB), keep.tile([P, 2, 4, P], F32, name="p_sb1")]
         slope_col = [late.tile([P, 1], F32, name=f"slope_col{h}", offset=7 * KB + 32 * h) for h in range(2)]
         v_g11 = keep.tile([P, PASS], BF16, name="v_g11")
         s_sb = [late.tile([P, N], F32, name=f"s_sb{h}", offset=(60 + 4 * h) * KB) for h in range(2)]
@@ -109,14 +110,14 @@ def tile_attend_soft_alibi_gate_srtq256n1024t2048_kernel(tc, qT, k_words, k_scal
         nc.sync.dma_start(out=slope_rows[0:2, :], in_=slope[0].rearrange("(h p) o -> h (p o)", p=P))
         nc.sync.dma_start(out=q_raw[:], in_=qT[0].rearrange("(p j) w -> p j w", j=4))
         nc.sync.dma_start(out=pos_win[:], in_=pos)
-        nc.sync.dma_start(out=v1_win[:, tokens(0)], in_=vT[P : 2 * P, tokens(0)])
-        nc.sync.dma_start(out=v1_win[:, tokens(1)], in_=vT[P : 2 * P, tokens(1)])
+        for a, b in zip(V1_CUTS, V1_CUTS[1:]):
+            nc.sync.dma_start(out=v1_win[:, a:b], in_=vT[P : 2 * P, a:b])
 
         def gather_scales():
             nc.vector.tensor_copy(ks_g[:], ks_win[:].indirect(offsets[:]))
 
         def gather_pos(g):
-            nc.vector.tensor_copy(pos_g[:, slots(g)], pos_win[:, 0 : (PREFIX, T)[g]].indirect(half_list(g)))
+            nc.vector.tensor_copy(pos_g[:, slots(g)], pos_win[:].indirect(half_list(g)))
 
         def gather_vs(g):
             nc.vector.tensor_copy(vs_g[g][:], vs_win[:].indirect(half_list(g)))
@@ -171,8 +172,9 @@ def tile_attend_soft_alibi_gate_srtq256n1024t2048_kernel(tc, qT, k_words, k_scal
         def cast_v0(half):
             nc.scalar.activation(out=v_cast[0][:, tokens(half)], in_=(v0_lo, v0_hi)[half][:], func=ACT.Copy)
 
-        def cast_v1(half):
-            nc.scalar.activation(out=v_cast[1][:, tokens(half)], in_=v1_win[:, tokens(half)], func=ACT.Copy)
+        def cast_v1():
+            for a, b in zip(V1_CUTS, V1_CUTS[1:]):
+                nc.scalar.activation(out=v_cast[1][:, a:b], in_=v1_win[:, a:b], func=ACT.Copy)
 
         def gather_v(f, g):
             nc.scalar.activation(out=v_g[f, g], in_=v_cast[f][:].indirect(half_list(g)), func=ACT.Copy)
@@ -244,8 +246,7 @@ def tile_attend_soft_alibi_gate_srtq256n1024t2048_kernel(tc, qT, k_words, k_scal
         scores(0, 1)
         scores(1, 0)
         scores(1, 1)
-        cast_v1(0)
-        cast_v1(1)
+        cast_v1()
         gather_v(1, 0)
         gather_v(1, 1)
         add_bias(0, 0)

@@ -136,7 +136,7 @@ def tile_attend_soft_alibi_gate_srtq256n1024t2048_kernel(tc, qT, k_words, k_scal
                 nc.scalar.copy(out=slope_col[h][:], in_=ps[:, h : h + 1])
 
         def cast_q():
-            nc.scalar.copy(out=q_bf[:], in_=q_raw[:].rearrange("p j w -> p w j"))
+            nc.gpsimd.tensor_scalar(q_bf[:], q_raw[:].rearrange("p j w -> p w j"), 1.0, 0.0, ALU.mult, ALU.add)
 
         def quantize_q():
             nc.vector.quantize_mx(out=q_codes[:].bitcast(FP8X4), scales=q_scales[:], in_=q_bf[:].rearrange("p w j -> p (w j)"))

@@ -19,12 +19,12 @@ AX = mybir.AxisListType
 
 P = 128
 PASS = 512
-BANK_OF = {"slope_ps":0,"vs_ps0":0,"vs_ps1":1,"a_ps00":2,"a_ps01":3,"a_ps10":6,"a_ps11":7,"vt_ps0":2,"vt_ps1":3,"pt_ps00":4,"pt_ps01":5,"pt_ps10":6,"pt_ps11":7,"y_ps0":0,"y_ps1":1}
 KB = 1024
 V1_CUTS = (0, 768, 1536, 2048)
-FIRST = 512
-HEAD = T - N + FIRST
 PREFIX = T - PASS
+BANK_OF = {"slope_ps": 6, "pos_ps0": 0, "pos_ps1": 1, "wide_ps0": 4, "wide_ps1": 5, "vs_ps0": 0, "vs_ps1": 1,
+           "a_ps00": 2, "a_ps01": 3, "a_ps10": 6, "a_ps11": 7, "vt_ps0": 2, "vt_ps1": 3,
+           "pt_ps00": 4, "pt_ps01": 5, "pt_ps10": 6, "pt_ps11": 7, "y_ps0": 0, "y_ps1": 1}
 
 
 def tile_attend_soft_alibi_gate_srtq256n1024t2048_kernel(tc, qT, k_words, k_scales, vT, vs, pos, slope, og, offs, out):
@@ -37,49 +37,58 @@ def tile_attend_soft_alibi_gate_srtq256n1024t2048_kernel(tc, qT, k_words, k_scal
         def slots(g):
             return slice(g * PASS, (g + 1) * PASS)
 
-        offsets = keep.tile([P, N // 16], U16, name="offsets")
-        v0_lo = late.tile([P, T // 2], F32, name="v0_lo", offset=68 * KB)
-        ident = keep.tile([P, P], F32, name="ident")
-        ks_win = keep.tile([P, T], U8, name="ks_win")
-        slope_rows = late.tile([P, P], F32, name="slope_rows", offset=12 * KB)
-        vs_win = late.tile([P, T], F32, name="vs_win", offset=48 * KB)
-        warm = late.tile([P, 12 * KB], F32, name="warm", offset=0)
-        v0_hi = late.tile([P, T // 2], F32, name="v0_hi", offset=0)
-        q_raw = late.tile([P, 4, NQ], F32, name="q_raw", offset=4 * KB)
-        v_g00 = keep.tile([P, PASS], BF16, name="v_g00")
-        v_g01 = late.tile([P, PASS], BF16, name="v_g01", offset=4 * KB)
-        kw_win = late.tile([P, T], I32, name="kw_win", offset=40 * KB)
-        vs_g = [keep.tile([P, PASS], F32, name=f"vs_g{g}") for g in range(2)]
-        pos_g = late.tile([P, N], F32, name="pos_g", offset=44 * KB)
-        q_codes = late.tile([P, NQ], U32, name="q_codes", align_bytes=64, offset=43 * KB)
-        pos_win = late.tile([P, T], F32, name="pos_win", offset=16 * KB)
-        v1_win = late.tile([P, T], F32, name="v1_win", offset=24 * KB)
-        v_cast = [late.tile([P, T], BF16, name="v_cast0", offset=32 * KB), late.tile([P, T], BF16, name="v_cast1", offset=7 * KB + 64)]
-        og_sb = late.tile([P, 2, DV], F32, name="og_sb", offset=32 * KB)
-        p_sb = [late.tile([P, 2, 4, P], F32, name="p_sb0", offset=24 * KB), keep.tile([P, 2, 4, P], F32, name="p_sb1")]
-        slope_col = [late.tile([P, 1], F32, name=f"slope_col{h}", offset=7 * KB + 32 * h) for h in range(2)]
-        v_g11 = keep.tile([P, PASS], BF16, name="v_g11")
-        s_sb = [late.tile([P, N], F32, name=f"s_sb{h}", offset=(60 + 4 * h) * KB) for h in range(2)]
-        vs_col = late.tile([P, 2, 4], F32, name="vs_col", offset=6 * KB)
-        gate_tanh = late.tile([P, 2, DV], F32, name="gate_tanh", offset=64 * KB)
-        v_bf = [late.tile([P, DV, 4], BF16, name="v_bf0", align_bytes=64, offset=60 * KB), late.tile([P, DV, 4], BF16, name="v_bf1", align_bytes=64, offset=66 * KB)]
-        kw_g = late.tile([P, N], U32, name="kw_g", align_bytes=64, offset=48 * KB)
-        ks_g = keep.tile([P, N], U8, name="ks_g", align_bytes=64)
-        q_bf = keep.tile([P, NQ, 4], BF16, name="q_bf", align_bytes=64)
-        v_g10 = keep.tile([P, PASS], BF16, name="v_g10")
-        v_g = {(0, 0): v_g00[:], (0, 1): v_g01[:], (1, 0): v_g10[:], (1, 1): v_g11[:]}
-        q_scales = keep.tile([P, NQ], U8, name="q_scales", align_bytes=64)
-        neg_max = [keep.tile([P, 1], F32, name=f"neg_max{h}") for h in range(2)]
-        v_codes = keep.tile([P, 2, DV], U32, name="v_codes", align_bytes=64)
-        v_scales = keep.tile([P, 2, DV], U8, name="v_scales", align_bytes=64)
-        gate = keep.tile([P, 2, DV], F32, name="gate")
-        w_bf = [keep.tile([P, 2, P, 4], BF16, name=f"w_bf{h}", align_bytes=64) for h in range(2)]
-        w_codes = [keep.tile([P, 2, P], U32, name=f"w_codes{h}", align_bytes=64) for h in range(2)]
-        w_scales = [keep.tile([P, 2, P], U8, name=f"w_scales{h}", align_bytes=64) for h in range(2)]
-        half_sum = keep.tile([P, 2, 2], F32, name="half_sum")
-        total = keep.tile([P, 2], F32, name="total")
-        inv = keep.tile([P, 2], F32, name="inv")
-        res = [keep.tile([P, DV], F32, name=f"res{h}") for h in range(2)]
+        def kept(name, shape, dtype):
+            return keep.tile(shape, dtype, name=name, align_bytes=64)
+
+        def placed(name, shape, dtype, kib):
+            return late.tile(shape, dtype, name=name, align_bytes=64, offset=int(kib * KB))
+
+        offsets = kept("offsets", [P, N // 16], U16)
+        ident = kept("ident", [P, P], F32)
+        warm = placed("warm", [P, 4 * KB], F32, 0)
+        v0_hi = placed("v0_hi", [P, T // 2], F32, 0)
+        pos_col = [placed(f"pos_col{g}", [P, 4], F32, g / 16) for g in range(2)]
+        slope_col = placed("slope_col", [P, 2], F32, 2 / 16)
+        kw_win = placed("kw_win", [P, T], I32, 4)
+        q_raw = placed("q_raw", [P, 4, NQ], F32, 12)
+        ks_win = placed("ks_win", [P, T], U8, 50)
+        pos_win = placed("pos_win", [P, T], F32, 20)
+        v1_raw = [placed("v1_raw0", [P, 768], F32, 18), placed("v1_raw1", [P, 768], F32, 21), placed("v1_raw2", [P, 512], F32, 50)]
+        og_sb = placed("og_sb", [P, 2, DV], F32, 4)
+        pos_g = [placed("pos_g0", [P, PASS], F32, 30), placed("pos_g1", [P, PASS], F32, 46)]
+        ks_g = placed("ks_g", [P, N], U8, 30)
+        pos_wide = [placed("pos_wide0", [P, PASS], F32, 32), placed("pos_wide1", [P, PASS], F32, 34)]
+        vs_g = [placed("vs_g0", [P, PASS], F32, 32), placed("vs_g1", [P, PASS], F32, 34)]
+        s_sb = [placed(f"s_sb{h}", [P, N], F32, 36 + 4 * h) for h in range(2)]
+        v_bf = [placed(f"v_bf{g}", [P, DV, 4], BF16, 36 + 2 * g) for g in range(2)]
+        gate_tanh = placed("gate_tanh", [P, 2, DV], F32, 42)
+        p_sb = {(h, g): placed(f"p_sb{h}{g}", [P, 4, P], F32, 49 + 2 * g) for h in range(2) for g in range(2)}
+        v0_lo = kept("v0_lo", [P, T // 2], F32)
+        slope_rows = kept("slope_rows", [P, P], F32)
+        vs_win = kept("vs_win", [P, T], F32)
+        v_cast0 = kept("v_cast0", [P, T], BF16)
+        v_cast1 = kept("v_cast1", [P, T], BF16)
+        v_g00 = placed("v_g00", [P, PASS], BF16, 31)
+        v_g01 = placed("v_g01", [P, PASS], BF16, 46)
+        v_g10 = kept("v_g10", [P, PASS], BF16)
+        v_g11 = kept("v_g11", [P, PASS], BF16)
+        kw_g = kept("kw_g", [P, N], U32)
+        vs_col = [kept(f"vs_col{g}", [P, 4], F32) for g in range(2)]
+        q_bf = kept("q_bf", [P, NQ, 4], BF16)
+        q_codes = kept("q_codes", [P, NQ], U32)
+        q_scales = kept("q_scales", [P, NQ], U8)
+        neg_max = [kept(f"neg_max{h}", [P, 1], F32) for h in range(2)]
+        v_codes = kept("v_codes", [P, 2, DV], U32)
+        v_scales = kept("v_scales", [P, 2, DV], U8)
+        gate = kept("gate", [P, 2, DV], F32)
+        w_bf = [kept(f"w_bf{h}", [P, 2, P, 4], BF16) for h in range(2)]
+        w_codes = [kept(f"w_codes{h}", [P, 2, P], U32) for h in range(2)]
+        w_scales = [kept(f"w_scales{h}", [P, 2, P], U8) for h in range(2)]
+        half_sum = kept("half_sum", [P, 2, 2], F32)
+        total = kept("total", [P, 2], F32)
+        inv = kept("inv", [P, 2], F32)
+        res = [kept(f"res{h}", [P, DV], F32) for h in range(2)]
+        v_g = {(0, 0): v_g00, (0, 1): v_g01, (1, 0): v_g10, (1, 1): v_g11}
         bank = {}
 
         def new_bank(key, shape):
@@ -92,48 +101,52 @@ def tile_attend_soft_alibi_gate_srtq256n1024t2048_kernel(tc, qT, k_words, k_scal
         def tokens(half):
             return slice(half * T // 2, (half + 1) * T // 2)
 
-        nc.vector.memset(ks_win[:].bitcast(I32), 0)
-        nc.vector.memset(vs_win[:], 0.0)
-        make_identity(nc, ident[:])
+        def load_scales():
+            ks_hbm = k_scales[0].bitcast(I32)
+            for quad in range(4):
+                nc.sync.dma_start(out=ks_win[32 * quad : 32 * quad + 4, :].bitcast(I32), in_=ks_hbm[4 * quad : 4 * quad + 4, :])
 
-        nc.sync.dma_start(offsets[:], offs)
-        kw_hbm = k_words[0].rearrange("p t r -> p (t r)").bitcast(I32)
-        nc.sync.dma_start(out=v0_lo[:], in_=vT[0:P, tokens(0)])
-        ks_hbm = k_scales[0].bitcast(I32)
-        for quad in range(4):
-            nc.sync.dma_start(out=ks_win[32 * quad : 32 * quad + 4, :].bitcast(I32), in_=ks_hbm[4 * quad : 4 * quad + 4, :])
-        nc.scalar.activation(out=warm[32:64, 0:1], in_=vs_win[32:64, 0:1], func=ACT.Exp)
-        nc.sync.dma_start(out=vs_win[0:1, :], in_=vs[0:1, :])
-        nc.vector.memset(slope_rows[:], 0.0)
-        nc.sync.dma_start(out=v0_hi[:], in_=vT[0:P, tokens(1)])
-        nc.sync.dma_start(out=kw_win[:], in_=k_words[0].rearrange("p t r -> p (t r)").bitcast(I32))
-        nc.sync.dma_start(out=slope_rows[0:2, :], in_=slope[0].rearrange("(h p) o -> h (p o)", p=P))
-        nc.sync.dma_start(out=q_raw[:], in_=qT[0].rearrange("(p j) w -> p j w", j=4))
-        nc.sync.dma_start(out=pos_win[:], in_=pos)
-        for a, b in zip(V1_CUTS, V1_CUTS[1:]):
-            nc.sync.dma_start(out=v1_win[:, a:b], in_=vT[P : 2 * P, a:b])
+        def load_v1(part):
+            nc.sync.dma_start(out=v1_raw[part][:], in_=vT[P : 2 * P, V1_CUTS[part] : V1_CUTS[part + 1]])
+
+        def load_og():
+            nc.sync.dma_start(out=og_sb[:], in_=og[0].rearrange("(h p) e -> p h e", p=P))
 
         def gather_scales():
             nc.vector.tensor_copy(ks_g[:], ks_win[:].indirect(offsets[:]))
 
         def gather_pos(g):
-            nc.vector.tensor_copy(pos_g[:, slots(g)], pos_win[:].indirect(half_list(g)))
+            nc.vector.tensor_copy(pos_g[g][:], pos_win[:].indirect(half_list(g)))
 
         def gather_vs(g):
             nc.vector.tensor_copy(vs_g[g][:], vs_win[:].indirect(half_list(g)))
 
-        def gather_keys():
-            nc.vector.tensor_copy(kw_g[:, 0:FIRST], kw_win[:, 0:HEAD].bitcast(U32).indirect(offsets[:, 0 : FIRST // 16]))
-            nc.vector.tensor_copy(kw_g[:, FIRST:N], kw_win[:].bitcast(U32).indirect(offsets[:, FIRST // 16 : N // 16]))
-
-        def load_og():
-            nc.sync.dma_start(out=og_sb[:], in_=og[0].rearrange("(h p) e -> p h e", p=P))
+        def gather_keys(g):
+            window = kw_win[:, 0 : (PREFIX, T)[g]]
+            nc.vector.tensor_copy(kw_g[:, slots(g)], window.bitcast(U32).indirect(half_list(g)))
 
         def turn_slope():
             ps = new_bank("slope_ps", [P, P])
             nc.tensor.transpose(ps[:], slope_rows[:], ident[:])
-            for h in range(2):
-                nc.scalar.copy(out=slope_col[h][:], in_=ps[:, h : h + 1])
+
+        def pick_slope():
+            nc.scalar.copy(out=slope_col[:], in_=bank["slope_ps"][:, 0:2])
+
+        def turn_pos_only(g):
+            ps = new_bank(f"pos_ps{g}", [P, 4, P])
+            for j in range(4):
+                nc.tensor.transpose(ps[:, j, :], pos_g[g][:, j * P : (j + 1) * P], ident[:])
+
+        def pick_pos(g):
+            nc.scalar.copy(out=pos_col[g][:], in_=bank[f"pos_ps{g}"][:, :, 0])
+
+        def spread_pos(g):
+            ps = new_bank(f"wide_ps{g}", [P, 4, P])
+            for j in range(4):
+                nc.tensor.transpose(ps[:, j, :], pos_col[g][:, j : j + 1].to_broadcast([P, P]), ident[:])
+
+        def store_pos(g):
+            nc.scalar.copy(out=pos_wide[g][:], in_=bank[f"wide_ps{g}"][:].rearrange("p j s -> p (j s)"))
 
         def cast_q():
             nc.gpsimd.tensor_scalar(q_bf[:], q_raw[:].rearrange("p j w -> p w j"), 1.0, 0.0, ALU.mult, ALU.add)
@@ -148,39 +161,34 @@ def tile_attend_soft_alibi_gate_srtq256n1024t2048_kernel(tc, qT, k_words, k_scal
                                 rhs=kw_g[:, slots(g)].bitcast(FP8X4), rhs_scale=ks_g[:, slots(g)], start=True, stop=True)
 
         def add_bias(h, g):
-            nc.vector.scalar_tensor_tensor(out=s_sb[h][:, slots(g)], in0=pos_g[:, slots(g)], scalar=slope_col[h][:],
+            nc.vector.scalar_tensor_tensor(out=s_sb[h][:, slots(g)], in0=pos_wide[g][:], scalar=slope_col[:, h : h + 1],
                                            in1=bank[f"a_ps{h}{g}"][:], op0=ALU.mult, op1=ALU.add)
 
         def row_max(h):
             nc.vector.tensor_reduce(out=neg_max[h][:], in_=s_sb[h][:], axis=AX.X, op=ALU.max, negate=True)
 
         def exp_half(h, g):
-            nc.scalar.activation(out=p_sb[h][:, g, :, :].rearrange("p t s -> p s t"), in_=s_sb[h][:, slots(g)].rearrange("p (s t) -> p s t", t=4),
+            nc.scalar.activation(out=p_sb[h, g][:].rearrange("p t s -> p s t"), in_=s_sb[h][:, slots(g)].rearrange("p (s t) -> p s t", t=4),
                                  func=ACT.Exp, bias=neg_max[h][:], accum_out=half_sum[:, h, g : g + 1])
 
         def join_sums(h):
             nc.scalar.activation(out=total[:, h : h + 1], in_=half_sum[:, h, 0:1], func=ACT.Identity, bias=half_sum[:, h, 1:2])
 
-        def turn_vs(g):
-            ps = new_bank(f"vs_ps{g}", [P, 4, P])
-            for t in range(4):
-                nc.tensor.transpose(ps[:, t, :], vs_g[g][:, t:PASS:4], ident[:])
-
-        def pick_vs(g):
-            nc.scalar.copy(out=vs_col[:, g, :], in_=bank[f"vs_ps{g}"][:, :, 0])
+        def deal_vs(g):
+            nc.sync.dma_start(out=vs_col[g][:], in_=vs_g[g][0:1, :])
 
         def cast_v0(half):
-            nc.scalar.activation(out=v_cast[0][:, tokens(half)], in_=(v0_lo, v0_hi)[half][:], func=ACT.Copy)
+            nc.scalar.activation(out=v_cast0[:, tokens(half)], in_=(v0_lo, v0_hi)[half][:], func=ACT.Copy)
 
-        def cast_v1():
-            for a, b in zip(V1_CUTS, V1_CUTS[1:]):
-                nc.scalar.activation(out=v_cast[1][:, a:b], in_=v1_win[:, a:b], func=ACT.Copy)
+        def cast_v1(part):
+            a, b = V1_CUTS[part], V1_CUTS[part + 1]
+            nc.scalar.activation(out=v_cast1[:, a:b], in_=v1_raw[part][:], func=ACT.Copy)
 
         def gather_v(f, g):
-            nc.scalar.activation(out=v_g[f, g], in_=v_cast[f][:].indirect(half_list(g)), func=ACT.Copy)
+            nc.scalar.activation(out=v_g[f, g][:], in_=(v_cast0, v_cast1)[f][:].indirect(half_list(g)), func=ACT.Copy)
 
         def turn_v(f, g):
-            pairs = v_g[f, g].bitcast(F32)
+            pairs = v_g[f, g][:].bitcast(F32)
             ps = bank[f"vt_ps{g}"] if f else new_bank(f"vt_ps{g}", [P, 2, 2, P])
             for u in range(2):
                 nc.tensor.transpose(ps[:, f, u, :], pairs[:, u : 2 * P : 2], ident[:])
@@ -192,18 +200,20 @@ def tile_attend_soft_alibi_gate_srtq256n1024t2048_kernel(tc, qT, k_words, k_scal
             nc.vector.quantize_mx(out=v_codes[:, g, :].bitcast(FP8X4), scales=v_scales[:, g, :],
                                   in_=v_bf[g][:].rearrange("p c t -> p (c t)"))
 
-        def make_gate():
+        def make_tanh():
             nc.scalar.activation(out=gate_tanh[:], in_=og_sb[:], func=ACT.Tanh, scale=0.5)
+
+        def make_gate():
             nc.scalar.activation(out=gate[:], in_=gate_tanh[:], func=ACT.Copy, scale=0.5, bias=0.5)
 
         def turn_p(h, g):
             ps = new_bank(f"pt_ps{h}{g}", [P, 4, P])
             for t in range(4):
-                nc.tensor.transpose(ps[:, t, :], p_sb[h][:, g, t, :], ident[:])
+                nc.tensor.transpose(ps[:, t, :], p_sb[h, g][:, t, :], ident[:])
 
         def weigh(h, g):
             nc.vector.tensor_tensor(w_bf[h][:, g, :, :], bank[f"pt_ps{h}{g}"][:].rearrange("p t q -> p q t"),
-                                    vs_col[:, g, :].unsqueeze(1).to_broadcast([P, P, 4]), ALU.mult)
+                                    vs_col[g][:].unsqueeze(1).to_broadcast([P, P, 4]), ALU.mult)
 
         def quantize_w(h, first, last):
             passes = slice(first, last + 1)
@@ -224,61 +234,93 @@ def tile_attend_soft_alibi_gate_srtq256n1024t2048_kernel(tc, qT, k_words, k_scal
             nc.vector.scalar_tensor_tensor(out=res[h][:], in0=bank[f"y_ps{h}"][:], scalar=inv[:, h : h + 1], in1=gate[:, h, :], op0=ALU.mult, op1=ALU.mult)
             nc.sync.dma_start(out=out[0, h * P : (h + 1) * P, :], in_=res[h][:])
 
-        gather_scales()
-        gather_vs(0)
-        gather_vs(1)
-        gather_keys()
-        turn_vs(0)
-        turn_vs(1)
-        cast_v0(0)
-        cast_v0(1)
-        gather_v(0, 0)
-        cast_q()
-        pick_vs(0)
-        pick_vs(1)
-        turn_slope()
-        gather_v(0, 1)
-        load_og()
-        quantize_q()
+        nc.vector.memset(pos_win[:], 0.0)
+        nc.vector.memset(ks_win[:].bitcast(I32), 0)
+        nc.vector.memset(slope_rows[:], 0.0)
+        nc.vector.memset(vs_win[:], 0.0)
+        make_identity(nc, ident[:])
+
+        nc.sync.dma_start(offsets[:], offs)
+        nc.sync.dma_start(out=v0_lo[:], in_=vT[0:P, tokens(0)])
+        nc.sync.dma_start(out=pos_win[0:1, :], in_=pos[0:1, :])
+        load_scales()
+        nc.sync.dma_start(out=slope_rows[0:2, :], in_=slope[0].rearrange("(h p) o -> h (p o)", p=P))
+        nc.scalar.activation(out=warm[32:64, 0:1], in_=slope_rows[32:64, 0:1], func=ACT.Exp)
+        nc.sync.dma_start(out=v0_hi[:], in_=vT[0:P, tokens(1)])
+        nc.sync.dma_start(out=q_raw[:], in_=qT[0].rearrange("(p j) w -> p j w", j=4))
+        kw_hbm = k_words[0].rearrange("p t r -> p (t r)").bitcast(I32)
+        nc.sync.dma_start(out=kw_win[:, 0:PREFIX], in_=kw_hbm[:, 0:PREFIX])
+        nc.sync.dma_start(out=kw_win[:, PREFIX:T], in_=kw_hbm[:, PREFIX:T])
+        nc.sync.dma_start(out=vs_win[0:1, :], in_=vs[0:1, :])
         gather_pos(0)
         gather_pos(1)
+        load_v1(0)
+        load_v1(1)
+        cast_v0(0)
+        turn_slope()
+        turn_pos_only(0)
+        gather_scales()
+        load_v1(2)
+        gather_keys(0)
+        cast_q()
+        quantize_q()
+        gather_keys(1)
+        load_og()
+        turn_pos_only(1)
+        cast_v0(1)
+        pick_pos(0)
+        gather_v(0, 0)
+        pick_pos(1)
+        pick_slope()
+        spread_pos(0)
+        gather_v(0, 1)
+        spread_pos(1)
+        store_pos(0)
+        store_pos(1)
         scores(0, 0)
-        scores(0, 1)
         scores(1, 0)
+        scores(0, 1)
         scores(1, 1)
-        cast_v1()
+        cast_v1(0)
+        cast_v1(1)
+        cast_v1(2)
         gather_v(1, 0)
         gather_v(1, 1)
         add_bias(0, 0)
-        add_bias(0, 1)
-        row_max(0)
         add_bias(1, 0)
+        add_bias(0, 1)
         add_bias(1, 1)
+        row_max(0)
+        gather_vs(0)
+        deal_vs(0)
+        gather_vs(1)
+        deal_vs(1)
         row_max(1)
         turn_v(0, 0)
-        turn_v(1, 0)
         turn_v(0, 1)
+        turn_v(1, 0)
         turn_v(1, 1)
         exp_half(0, 0)
         turn_p(0, 0)
         exp_half(0, 1)
         turn_p(0, 1)
         store_v(0)
+        store_v(1)
         exp_half(1, 0)
         turn_p(1, 0)
         exp_half(1, 1)
         turn_p(1, 1)
         join_sums(0)
         join_sums(1)
-        store_v(1)
+        make_tanh()
         make_gate()
         weigh(0, 0)
         weigh(0, 1)
         quantize_v(0)
+        quantize_v(1)
         quantize_w(0, 0, 1)
         weigh(1, 0)
         weigh(1, 1)
-        quantize_v(1)
         invert()
         product(0)
         quantize_w(1, 0, 0)

@@ -51,25 +51,25 @@ def tile_attend_soft_alibi_gate_srtq256n1024t2048_kernel(tc, qT, k_words, k_scal
         slope_col = placed("slope_col", [P, 2], F32, 2 / 16)
         kw_win = placed("kw_win", [P, T], I32, 4)
         q_raw = placed("q_raw", [P, 4, NQ], F32, 12)
-        ks_win = placed("ks_win", [P, T], U8, 50)
+        ks_win = placed("ks_win", [P, T], U8, 49.5)
         pos_win = placed("pos_win", [P, T], F32, 20)
-        v1_raw = [placed("v1_raw0", [P, 768], F32, 18), placed("v1_raw1", [P, 768], F32, 21), placed("v1_raw2", [P, 512], F32, 50)]
+        v1_raw = [placed("v1_raw0", [P, 768], F32, 18), placed("v1_raw1", [P, 768], F32, 21), placed("v1_raw2", [P, 512], F32, 48)]
         og_sb = placed("og_sb", [P, 2, DV], F32, 4)
-        pos_g = [placed("pos_g0", [P, PASS], F32, 30), placed("pos_g1", [P, PASS], F32, 46)]
-        ks_g = placed("ks_g", [P, N], U8, 30)
+        pos_g = [placed("pos_g0", [P, PASS], F32, 30), kept("pos_g1", [P, PASS], F32)]
+        ks_g = [kept("ks_g0", [P, PASS], U8), placed("ks_g1", [P, PASS], U8, 30)]
         pos_wide = [placed("pos_wide0", [P, PASS], F32, 32), placed("pos_wide1", [P, PASS], F32, 34)]
         vs_g = [placed("vs_g0", [P, PASS], F32, 32), placed("vs_g1", [P, PASS], F32, 34)]
         s_sb = [placed(f"s_sb{h}", [P, N], F32, 36 + 4 * h) for h in range(2)]
         v_bf = [placed(f"v_bf{g}", [P, DV, 4], BF16, 36 + 2 * g) for g in range(2)]
         gate_tanh = placed("gate_tanh", [P, 2, DV], F32, 42)
-        p_sb = {(h, g): placed(f"p_sb{h}{g}", [P, 4, P], F32, 49 + 2 * g) for h in range(2) for g in range(2)}
+        p_sb = {(h, g): placed(f"p_sb{h}{g}", [P, 4, P], F32, 47 + 2 * g) for h in range(2) for g in range(2)}
         v0_lo = kept("v0_lo", [P, T // 2], F32)
         slope_rows = kept("slope_rows", [P, P], F32)
-        vs_win = kept("vs_win", [P, T], F32)
+        vs_win = placed("vs_win", [P, T], F32, 51)
         v_cast0 = kept("v_cast0", [P, T], BF16)
         v_cast1 = kept("v_cast1", [P, T], BF16)
-        v_g00 = placed("v_g00", [P, PASS], BF16, 31)
-        v_g01 = placed("v_g01", [P, PASS], BF16, 46)
+        v_g00 = kept("v_g00", [P, PASS], BF16)
+        v_g01 = kept("v_g01", [P, PASS], BF16)
         v_g10 = kept("v_g10", [P, PASS], BF16)
         v_g11 = kept("v_g11", [P, PASS], BF16)
         kw_g = kept("kw_g", [P, N], U32)
@@ -77,9 +77,9 @@ def tile_attend_soft_alibi_gate_srtq256n1024t2048_kernel(tc, qT, k_words, k_scal
         q_bf = kept("q_bf", [P, NQ, 4], BF16)
         q_codes = kept("q_codes", [P, NQ], U32)
         q_scales = kept("q_scales", [P, NQ], U8)
-        neg_max = [kept(f"neg_max{h}", [P, 1], F32) for h in range(2)]
-        v_codes = kept("v_codes", [P, 2, DV], U32)
-        v_scales = kept("v_scales", [P, 2, DV], U8)
+        neg_max = [kept("neg_max0", [P, 1], F32), placed("neg_max1", [P, 1], F32, 58)]
+        v_codes = [placed(f"v_codes{g}", [P, DV], U32, 32 + 2 * g) for g in range(2)]
+        v_scales = [kept(f"v_scales{g}", [P, DV], U8) for g in range(2)]
         gate = kept("gate", [P, 2, DV], F32)
         w_bf = [kept(f"w_bf{h}", [P, 2, P, 4], BF16) for h in range(2)]
         w_codes = [kept(f"w_codes{h}", [P, 2, P], U32) for h in range(2)]
@@ -109,17 +109,21 @@ def tile_attend_soft_alibi_gate_srtq256n1024t2048_kernel(tc, qT, k_words, k_scal
         def load_v1(part):
             nc.sync.dma_start(out=v1_raw[part][:], in_=vT[P : 2 * P, V1_CUTS[part] : V1_CUTS[part + 1]])
 
+        def load_vs():
+            nc.sync.dma_start(out=vs_win[:, 0:PREFIX], in_=vs[:, 0:PREFIX])
+            nc.sync.dma_start(out=vs_win[:, PREFIX:T], in_=vs[:, PREFIX:T])
+
         def load_og():
             nc.sync.dma_start(out=og_sb[:], in_=og[0].rearrange("(h p) e -> p h e", p=P))
 
-        def gather_scales():
-            nc.vector.tensor_copy(ks_g[:], ks_win[:].indirect(offsets[:]))
+        def gather_scales(g):
+            nc.vector.tensor_copy(ks_g[g][:], ks_win[:].indirect(half_list(g)))
 
         def gather_pos(g):
             nc.vector.tensor_copy(pos_g[g][:], pos_win[:].indirect(half_list(g)))
 
         def gather_vs(g):
-            nc.vector.tensor_copy(vs_g[g][:], vs_win[:].indirect(half_list(g)))
+            nc.vector.tensor_copy(vs_g[g][:], vs_win[:, 0 : (PREFIX, T)[g]].indirect(half_list(g)))
 
         def gather_keys(g):
             window = kw_win[:, 0 : (PREFIX, T)[g]]
@@ -158,7 +162,7 @@ def tile_attend_soft_alibi_gate_srtq256n1024t2048_kernel(tc, qT, k_words, k_scal
             qs = slice(h * P, (h + 1) * P)
             ps = new_bank(f"a_ps{h}{g}", [P, PASS])
             nc.tensor.matmul_mx(out=ps[:], lhsT=q_codes[:, qs].bitcast(FP8X4), lhsT_scale=q_scales[:, qs],
-                                rhs=kw_g[:, slots(g)].bitcast(FP8X4), rhs_scale=ks_g[:, slots(g)], start=True, stop=True)
+                                rhs=kw_g[:, slots(g)].bitcast(FP8X4), rhs_scale=ks_g[g][:], start=True, stop=True)
 
         def add_bias(h, g):
             nc.vector.scalar_tensor_tensor(out=s_sb[h][:, slots(g)], in0=pos_wide[g][:], scalar=slope_col[:, h : h + 1],
@@ -197,7 +201,7 @@ def tile_attend_soft_alibi_gate_srtq256n1024t2048_kernel(tc, qT, k_words, k_scal
             nc.scalar.copy(out=v_bf[g][:].rearrange("p c t -> p (c t)").bitcast(F32).rearrange("p (f c u) -> p f c u", f=2, u=2), in_=bank[f"vt_ps{g}"][:].rearrange("p f u c -> p f c u"))
 
         def quantize_v(g):
-            nc.vector.quantize_mx(out=v_codes[:, g, :].bitcast(FP8X4), scales=v_scales[:, g, :],
+            nc.vector.quantize_mx(out=v_codes[g][:].bitcast(FP8X4), scales=v_scales[g][:],
                                   in_=v_bf[g][:].rearrange("p c t -> p (c t)"))
 
         def make_tanh():
@@ -228,30 +232,29 @@ def tile_attend_soft_alibi_gate_srtq256n1024t2048_kernel(tc, qT, k_words, k_scal
             ps = new_bank(f"y_ps{h}", [P, DV])
             for g in range(2):
                 nc.tensor.matmul_mx(out=ps[:], lhsT=w_codes[h][:, g, :].bitcast(FP8X4), lhsT_scale=w_scales[h][:, g, :],
-                                    rhs=v_codes[:, g, :].bitcast(FP8X4), rhs_scale=v_scales[:, g, :], start=(g == 0), stop=(g == 1))
+                                    rhs=v_codes[g][:].bitcast(FP8X4), rhs_scale=v_scales[g][:], start=(g == 0), stop=(g == 1))
 
         def finish(h):
             nc.vector.scalar_tensor_tensor(out=res[h][:], in0=bank[f"y_ps{h}"][:], scalar=inv[:, h : h + 1], in1=gate[:, h, :], op0=ALU.mult, op1=ALU.mult)
             nc.sync.dma_start(out=out[0, h * P : (h + 1) * P, :], in_=res[h][:])
 
-        nc.vector.memset(pos_win[:], 0.0)
         nc.vector.memset(ks_win[:].bitcast(I32), 0)
         nc.vector.memset(slope_rows[:], 0.0)
-        nc.vector.memset(vs_win[:], 0.0)
+        nc.vector.memset(pos_win[:], 0.0)
         make_identity(nc, ident[:])
 
         nc.sync.dma_start(offsets[:], offs)
         nc.sync.dma_start(out=v0_lo[:], in_=vT[0:P, tokens(0)])
-        nc.sync.dma_start(out=pos_win[0:1, :], in_=pos[0:1, :])
         load_scales()
         nc.sync.dma_start(out=slope_rows[0:2, :], in_=slope[0].rearrange("(h p) o -> h (p o)", p=P))
-        nc.scalar.activation(out=warm[32:64, 0:1], in_=slope_rows[32:64, 0:1], func=ACT.Exp)
+        nc.scalar.activation(out=warm[32:64, 0:1], in_=pos_win[32:64, 0:1], func=ACT.Exp)
+        nc.sync.dma_start(out=pos_win[0:1, :], in_=pos[0:1, :])
         nc.sync.dma_start(out=v0_hi[:], in_=vT[0:P, tokens(1)])
         nc.sync.dma_start(out=q_raw[:], in_=qT[0].rearrange("(p j) w -> p j w", j=4))
         kw_hbm = k_words[0].rearrange("p t r -> p (t r)").bitcast(I32)
         nc.sync.dma_start(out=kw_win[:, 0:PREFIX], in_=kw_hbm[:, 0:PREFIX])
         nc.sync.dma_start(out=kw_win[:, PREFIX:T], in_=kw_hbm[:, PREFIX:T])
-        nc.sync.dma_start(out=vs_win[0:1, :], in_=vs[0:1, :])
+        gather_scales(0)
         gather_pos(0)
         gather_pos(1)
         load_v1(0)
@@ -259,22 +262,23 @@ def tile_attend_soft_alibi_gate_srtq256n1024t2048_kernel(tc, qT, k_words, k_scal
         cast_v0(0)
         turn_slope()
         turn_pos_only(0)
-        gather_scales()
+        gather_scales(1)
         load_v1(2)
-        gather_keys(0)
+        load_vs()
         cast_q()
         quantize_q()
+        gather_keys(0)
         gather_keys(1)
         load_og()
-        turn_pos_only(1)
         cast_v0(1)
-        pick_pos(0)
         gather_v(0, 0)
-        pick_pos(1)
+        pick_pos(0)
         pick_slope()
+        turn_pos_only(1)
+        pick_pos(1)
         spread_pos(0)
-        gather_v(0, 1)
         spread_pos(1)
+        gather_v(0, 1)
         store_pos(0)
         store_pos(1)
         scores(0, 0)
@@ -315,8 +319,8 @@ def tile_attend_soft_alibi_gate_srtq256n1024t2048_kernel(tc, qT, k_words, k_scal
         make_tanh()
         make_gate()
         weigh(0, 0)
-        weigh(0, 1)
         quantize_v(0)
+        weigh(0, 1)
         quantize_v(1)
         quantize_w(0, 0, 1)
         weigh(1, 0)

@@ -20,6 +20,7 @@ AX = mybir.AxisListType
 P = 128
 PASS = 512
 KB = 1024
+V0_CUTS = (0, 1024, 1536, 2048)
 V1_CUTS = (0, 768, 1536, 2048)
 PREFIX = T - PASS
 BANK_OF = {"slope_ps": 6, "pos_ps0": 0, "pos_ps1": 1, "wide_ps0": 4, "wide_ps1": 5, "vs_ps0": 0, "vs_ps1": 1,
@@ -45,15 +46,16 @@ def tile_attend_soft_alibi_gate_srtq256n1024t2048_kernel(tc, qT, k_words, k_scal
 
         offsets = kept("offsets", [P, N // 16], U16)
         ident = kept("ident", [P, P], F32)
-        warm = placed("warm", [P, 4 * KB], F32, 0)
-        v0_hi = placed("v0_hi", [P, T // 2], F32, 0)
+        warm = placed("warm", [P, 65 * 64], F32, 0)
+        v0_raw = [kept("v0_raw0", [P, 1024], F32), placed("v0_raw1", [P, 512], F32, 16), placed("v0_raw2", [P, 512], F32, 0)]
         pos_col = [placed(f"pos_col{g}", [P, 4], F32, g / 16) for g in range(2)]
         slope_col = placed("slope_col", [P, 2], F32, 2 / 16)
+        slope_rows = placed("slope_rows", [P, P], F32, 3.5)
         kw_win = placed("kw_win", [P, T], I32, 4)
         q_raw = placed("q_raw", [P, 4, NQ], F32, 12)
         ks_win = placed("ks_win", [P, T], U8, 49.5)
         pos_win = placed("pos_win", [P, T], F32, 20)
-        v1_raw = [placed("v1_raw0", [P, 768], F32, 18), placed("v1_raw1", [P, 768], F32, 21), placed("v1_raw2", [P, 512], F32, 48)]
+        v1_raw = [placed("v1_raw0", [P, 768], F32, 20), placed("v1_raw1", [P, 768], F32, 23), placed("v1_raw2", [P, 512], F32, 48)]
         og_sb = placed("og_sb", [P, 2, DV], F32, 4)
         pos_g = [placed("pos_g0", [P, PASS], F32, 30), kept("pos_g1", [P, PASS], F32)]
         ks_g = [kept("ks_g0", [P, PASS], U8), placed("ks_g1", [P, PASS], U8, 30)]
@@ -63,8 +65,6 @@ def tile_attend_soft_alibi_gate_srtq256n1024t2048_kernel(tc, qT, k_words, k_scal
         v_bf = [placed(f"v_bf{g}", [P, DV, 4], BF16, 36 + 2 * g) for g in range(2)]
         gate_tanh = placed("gate_tanh", [P, 2, DV], F32, 42)
         p_sb = {(h, g): placed(f"p_sb{h}{g}", [P, 4, P], F32, 47 + 2 * g) for h in range(2) for g in range(2)}
-        v0_lo = kept("v0_lo", [P, T // 2], F32)
-        slope_rows = kept("slope_rows", [P, P], F32)
         vs_win = placed("vs_win", [P, T], F32, 51)
         v_cast0 = kept("v_cast0", [P, T], BF16)
         v_cast1 = kept("v_cast1", [P, T], BF16)
@@ -181,12 +181,19 @@ def tile_attend_soft_alibi_gate_srtq256n1024t2048_kernel(tc, qT, k_words, k_scal
         def deal_vs(g):
             nc.sync.dma_start(out=vs_col[g][:], in_=vs_g[g][0:1, :])
 
-        def cast_v0(half):
-            nc.scalar.activation(out=v_cast0[:, tokens(half)], in_=(v0_lo, v0_hi)[half][:], func=ACT.Copy)
+        def cast_v0(part):
+            a, b = V0_CUTS[part], V0_CUTS[part + 1]
+            nc.scalar.activation(out=v_cast0[:, a:b], in_=v0_raw[part][:], func=ACT.Copy)
+
+        def load_v0(part):
+            nc.sync.dma_start(out=v0_raw[part][:], in_=vT[0:P, V0_CUTS[part] : V0_CUTS[part + 1]])
 
         def cast_v1(part):
             a, b = V1_CUTS[part], V1_CUTS[part + 1]
             nc.scalar.activation(out=v_cast1[:, a:b], in_=v1_raw[part][:], func=ACT.Copy)
+
+        def gather_first_v():
+            nc.scalar.activation(out=v_g00[:].rearrange("p (u s e) -> p s u e", u=2, e=2), in_=v_cast0[:, 0:PREFIX].indirect(half_list(0)), func=ACT.Copy)
 
         def gather_v(f, g):
             nc.scalar.activation(out=v_g[f, g][:], in_=(v_cast0, v_cast1)[f][:].indirect(half_list(g)), func=ACT.Copy)
@@ -195,7 +202,7 @@ def tile_attend_soft_alibi_gate_srtq256n1024t2048_kernel(tc, qT, k_words, k_scal
             pairs = v_g[f, g][:].bitcast(F32)
             ps = bank[f"vt_ps{g}"] if f else new_bank(f"vt_ps{g}", [P, 2, 2, P])
             for u in range(2):
-                nc.tensor.transpose(ps[:, f, u, :], pairs[:, u : 2 * P : 2], ident[:])
+                nc.tensor.transpose(ps[:, f, u, :], pairs[:, u : 2 * P : 2] if f + g else pairs[:, u * P : (u + 1) * P], ident[:])
 
         def store_v(g):
             nc.scalar.copy(out=v_bf[g][:].rearrange("p c t -> p (c t)").bitcast(F32).rearrange("p (f c u) -> p f c u", f=2, u=2), in_=bank[f"vt_ps{g}"][:].rearrange("p f u c -> p f c u"))
@@ -239,19 +246,20 @@ def tile_attend_soft_alibi_gate_srtq256n1024t2048_kernel(tc, qT, k_words, k_scal
             nc.sync.dma_start(out=out[0, h * P : (h + 1) * P, :], in_=res[h][:])
 
         nc.vector.memset(ks_win[:].bitcast(I32), 0)
-        nc.vector.memset(slope_rows[:], 0.0)
         nc.vector.memset(pos_win[:], 0.0)
         make_identity(nc, ident[:])
 
         nc.sync.dma_start(offsets[:], offs)
-        nc.sync.dma_start(out=v0_lo[:], in_=vT[0:P, tokens(0)])
+        load_v0(0)
         load_scales()
-        nc.sync.dma_start(out=slope_rows[0:2, :], in_=slope[0].rearrange("(h p) o -> h (p o)", p=P))
         nc.scalar.activation(out=warm[32:64, 0:1], in_=pos_win[32:64, 0:1], func=ACT.Exp)
         nc.sync.dma_start(out=pos_win[0:1, :], in_=pos[0:1, :])
-        nc.sync.dma_start(out=v0_hi[:], in_=vT[0:P, tokens(1)])
-        nc.sync.dma_start(out=q_raw[:], in_=qT[0].rearrange("(p j) w -> p j w", j=4))
         kw_hbm = k_words[0].rearrange("p t r -> p (t r)").bitcast(I32)
+        load_v0(1)
+        nc.vector.memset(slope_rows[:], 0.0)
+        nc.sync.dma_start(out=q_raw[:], in_=qT[0].rearrange("(p j) w -> p j w", j=4))
+        nc.sync.dma_start(out=slope_rows[0:2, :], in_=slope[0].rearrange("(h p) o -> h (p o)", p=P))
+        load_v0(2)
         nc.sync.dma_start(out=kw_win[:, 0:PREFIX], in_=kw_hbm[:, 0:PREFIX])
         nc.sync.dma_start(out=kw_win[:, PREFIX:T], in_=kw_hbm[:, PREFIX:T])
         gather_scales(0)
@@ -271,14 +279,15 @@ def tile_attend_soft_alibi_gate_srtq256n1024t2048_kernel(tc, qT, k_words, k_scal
         gather_keys(1)
         load_og()
         cast_v0(1)
-        gather_v(0, 0)
+        gather_first_v()
+        cast_v0(2)
         pick_pos(0)
-        pick_slope()
         turn_pos_only(1)
-        pick_pos(1)
         spread_pos(0)
-        spread_pos(1)
         gather_v(0, 1)
+        pick_pos(1)
+        pick_slope()
+        spread_pos(1)
         store_pos(0)
         store_pos(1)
         scores(0, 0)

@@ -25,7 +25,7 @@ V1_CUTS = (0, 768, 1536, 2048)
 PREFIX = T - PASS
 BANK_OF = {"slope_ps": 6, "pos_ps0": 0, "pos_ps1": 1, "wide_ps0": 4, "wide_ps1": 5, "vs_ps0": 0, "vs_ps1": 1,
            "a_ps00": 2, "a_ps01": 3, "a_ps10": 6, "a_ps11": 7, "vt_ps0": 2, "vt_ps1": 3,
-           "pt_ps00": 4, "pt_ps01": 5, "pt_ps10": 6, "pt_ps11": 7, "y_ps0": 0, "y_ps1": 1}
+           "pt_ps00": 4, "pt_ps01": 5, "pt_ps10": 6, "pt_ps11": 7, "y_ps0": 0, "y_ps1": 1, "y_ps2": 2}
 
 
 def tile_attend_soft_alibi_gate_srtq256n1024t2048_kernel(tc, qT, k_words, k_scales, vT, vs, pos, slope, og, offs, out):
@@ -53,21 +53,21 @@ def tile_attend_soft_alibi_gate_srtq256n1024t2048_kernel(tc, qT, k_words, k_scal
         slope_rows = placed("slope_rows", [P, P], F32, 3.5)
         kw_win = placed("kw_win", [P, T], I32, 4)
         q_raw = placed("q_raw", [P, 4, NQ], F32, 12)
-        ks_win = placed("ks_win", [P, T], U8, 49.5)
+        ks_win = placed("ks_win", [P, T], U8, 63)
         pos_win = placed("pos_win", [P, T], F32, 20)
-        v1_raw = [placed("v1_raw0", [P, 768], F32, 20), placed("v1_raw1", [P, 768], F32, 23), placed("v1_raw2", [P, 512], F32, 48)]
+        v1_raw = [placed("v1_raw0", [P, 768], F32, 20), placed("v1_raw1", [P, 768], F32, 23), placed("v1_raw2", [P, 1536], F32, 64)]
         og_sb = placed("og_sb", [P, 2, DV], F32, 4)
         pos_g = [placed("pos_g0", [P, PASS], F32, 30), kept("pos_g1", [P, PASS], F32)]
         ks_g = [kept("ks_g0", [P, PASS], U8), placed("ks_g1", [P, PASS], U8, 30)]
         pos_wide = [placed("pos_wide0", [P, PASS], F32, 32), placed("pos_wide1", [P, PASS], F32, 34)]
         vs_g = [placed("vs_g0", [P, PASS], F32, 32), placed("vs_g1", [P, PASS], F32, 34)]
         s_sb = [placed(f"s_sb{h}", [P, N], F32, 36 + 4 * h) for h in range(2)]
-        v_bf = [placed(f"v_bf{g}", [P, DV, 4], BF16, 36 + 2 * g) for g in range(2)]
+        v_cast1 = placed("v_cast1", [P, T], BF16, 72)
+        v_bf = [placed(f"v_bf{g}", [P, DV, 4], BF16, 72 + 2 * g) for g in range(2)]
         gate_tanh = placed("gate_tanh", [P, 2, DV], F32, 42)
-        p_sb = {(h, g): placed(f"p_sb{h}{g}", [P, 4, P], F32, 47 + 2 * g) for h in range(2) for g in range(2)}
-        vs_win = placed("vs_win", [P, T], F32, 51)
+        p_sb = {(h, g): placed(f"p_sb{h}{g}", [P, 4, P], F32, 66 + 2 * g) for h in range(2) for g in range(2)}
+        vs_win = placed("vs_win", [P, T], F32, 55.5)
         v_cast0 = kept("v_cast0", [P, T], BF16)
-        v_cast1 = kept("v_cast1", [P, T], BF16)
         v_g00 = kept("v_g00", [P, PASS], BF16)
         v_g01 = kept("v_g01", [P, PASS], BF16)
         v_g10 = kept("v_g10", [P, PASS], BF16)
@@ -77,7 +77,7 @@ def tile_attend_soft_alibi_gate_srtq256n1024t2048_kernel(tc, qT, k_words, k_scal
         q_bf = kept("q_bf", [P, NQ, 4], BF16)
         q_codes = kept("q_codes", [P, NQ], U32)
         q_scales = kept("q_scales", [P, NQ], U8)
-        neg_max = [kept("neg_max0", [P, 1], F32), placed("neg_max1", [P, 1], F32, 58)]
+        neg_max = [kept(f"neg_max{h}", [P, 1], F32) for h in range(2)]
         v_codes = [placed(f"v_codes{g}", [P, DV], U32, 32 + 2 * g) for g in range(2)]
         v_scales = [kept(f"v_scales{g}", [P, DV], U8) for g in range(2)]
         gate = kept("gate", [P, 2, DV], F32)
@@ -87,7 +87,9 @@ def tile_attend_soft_alibi_gate_srtq256n1024t2048_kernel(tc, qT, k_words, k_scal
         half_sum = kept("half_sum", [P, 2, 2], F32)
         total = kept("total", [P, 2], F32)
         inv = kept("inv", [P, 2], F32)
-        res = [kept(f"res{h}", [P, DV], F32) for h in range(2)]
+        res = [kept("res0", [P, DV], F32), kept("res1", [P, P], F32), kept("res2", [P, P], F32)]
+        a_sb = {1: placed("a_sb", [P, PASS], F32, 64)}
+        bias_sb = {1: kept("bias_sb", [P, PASS], F32)}
         v_g = {(0, 0): v_g00, (0, 1): v_g01, (1, 0): v_g10, (1, 1): v_g11}
         bank = {}
 
@@ -107,7 +109,7 @@ def tile_attend_soft_alibi_gate_srtq256n1024t2048_kernel(tc, qT, k_words, k_scal
                 nc.sync.dma_start(out=ks_win[32 * quad : 32 * quad + 4, :].bitcast(I32), in_=ks_hbm[4 * quad : 4 * quad + 4, :])
 
         def load_v1(part):
-            nc.sync.dma_start(out=v1_raw[part][:], in_=vT[P : 2 * P, V1_CUTS[part] : V1_CUTS[part + 1]])
+            nc.sync.dma_start(out=v1_raw[part][:, 0 : V1_CUTS[part + 1] - V1_CUTS[part]], in_=vT[P : 2 * P, V1_CUTS[part] : V1_CUTS[part + 1]])
 
         def load_vs():
             nc.sync.dma_start(out=vs_win[:, 0:PREFIX], in_=vs[:, 0:PREFIX])
@@ -152,6 +154,9 @@ def tile_attend_soft_alibi_gate_srtq256n1024t2048_kernel(tc, qT, k_words, k_scal
         def store_pos(g):
             nc.scalar.copy(out=pos_wide[g][:], in_=bank[f"wide_ps{g}"][:].rearrange("p j s -> p (j s)"))
 
+        def make_bias(g):
+            nc.gpsimd.tensor_scalar(bias_sb[g][:], pos_wide[g][:], slope_col[:, 1:2], 0.0, ALU.mult, ALU.add)
+
         def cast_q():
             nc.gpsimd.tensor_scalar(q_bf[:], q_raw[:].rearrange("p j w -> p w j"), 1.0, 0.0, ALU.mult, ALU.add)
 
@@ -167,6 +172,12 @@ def tile_attend_soft_alibi_gate_srtq256n1024t2048_kernel(tc, qT, k_words, k_scal
         def add_bias(h, g):
             nc.vector.scalar_tensor_tensor(out=s_sb[h][:, slots(g)], in0=pos_wide[g][:], scalar=slope_col[:, h : h + 1],
                                            in1=bank[f"a_ps{h}{g}"][:], op0=ALU.mult, op1=ALU.add)
+
+        def empty_scores(g):
+            nc.scalar.copy(out=a_sb[g][:], in_=bank[f"a_ps1{g}"][:])
+
+        def add_bias_aside(g):
+            nc.gpsimd.tensor_tensor(s_sb[1][:, slots(g)], a_sb[g][:], bias_sb[g][:], ALU.add)
 
         def row_max(h):
             nc.vector.tensor_reduce(out=neg_max[h][:], in_=s_sb[h][:], axis=AX.X, op=ALU.max, negate=True)
@@ -190,10 +201,11 @@ def tile_attend_soft_alibi_gate_srtq256n1024t2048_kernel(tc, qT, k_words, k_scal
 
         def cast_v1(part):
             a, b = V1_CUTS[part], V1_CUTS[part + 1]
-            nc.scalar.activation(out=v_cast1[:, a:b], in_=v1_raw[part][:], func=ACT.Copy)
+            nc.scalar.activation(out=v_cast1[:, a:b], in_=v1_raw[part][:, 0 : b - a], func=ACT.Copy)
 
-        def gather_first_v():
-            nc.scalar.activation(out=v_g00[:].rearrange("p (u s e) -> p s u e", u=2, e=2), in_=v_cast0[:, 0:PREFIX].indirect(half_list(0)), func=ACT.Copy)
+        def gather_first_v(f):
+            window = (v_cast0, v_cast1)[f][:, 0:PREFIX]
+            nc.scalar.activation(out=v_g[f, 0][:].rearrange("p (u s e) -> p s u e", u=2, e=2), in_=window.indirect(half_list(0)), func=ACT.Copy)
 
         def gather_v(f, g):
             nc.scalar.activation(out=v_g[f, g][:], in_=(v_cast0, v_cast1)[f][:].indirect(half_list(g)), func=ACT.Copy)
@@ -202,7 +214,7 @@ def tile_attend_soft_alibi_gate_srtq256n1024t2048_kernel(tc, qT, k_words, k_scal
             pairs = v_g[f, g][:].bitcast(F32)
             ps = bank[f"vt_ps{g}"] if f else new_bank(f"vt_ps{g}", [P, 2, 2, P])
             for u in range(2):
-                nc.tensor.transpose(ps[:, f, u, :], pairs[:, u : 2 * P : 2] if f + g else pairs[:, u * P : (u + 1) * P], ident[:])
+                nc.tensor.transpose(ps[:, f, u, :], pairs[:, u : 2 * P : 2] if g else pairs[:, u * P : (u + 1) * P], ident[:])
 
         def store_v(g):
             nc.scalar.copy(out=v_bf[g][:].rearrange("p c t -> p (c t)").bitcast(F32).rearrange("p (f c u) -> p f c u", f=2, u=2), in_=bank[f"vt_ps{g}"][:].rearrange("p f u c -> p f c u"))
@@ -235,15 +247,14 @@ def tile_attend_soft_alibi_gate_srtq256n1024t2048_kernel(tc, qT, k_words, k_scal
         def invert():
             nc.vector.reciprocal(inv[:], total[:])
 
-        def product(h):
-            ps = new_bank(f"y_ps{h}", [P, DV])
-            for g in range(2):
-                nc.tensor.matmul_mx(out=ps[:], lhsT=w_codes[h][:, g, :].bitcast(FP8X4), lhsT_scale=w_scales[h][:, g, :],
-                                    rhs=v_codes[g][:].bitcast(FP8X4), rhs_scale=v_scales[g][:], start=(g == 0), stop=(g == 1))
+        def product(h, piece, features, g):
+            ps = bank[f"y_ps{piece}"] if g else new_bank(f"y_ps{piece}", [P, features.stop - features.start])
+            nc.tensor.matmul_mx(out=ps[:], lhsT=w_codes[h][:, g, :].bitcast(FP8X4), lhsT_scale=w_scales[h][:, g, :],
+                                rhs=v_codes[g][:, features].bitcast(FP8X4), rhs_scale=v_scales[g][:, features], start=(g == 0), stop=(g == 1))
 
-        def finish(h):
-            nc.vector.scalar_tensor_tensor(out=res[h][:], in0=bank[f"y_ps{h}"][:], scalar=inv[:, h : h + 1], in1=gate[:, h, :], op0=ALU.mult, op1=ALU.mult)
-            nc.sync.dma_start(out=out[0, h * P : (h + 1) * P, :], in_=res[h][:])
+        def finish(h, piece, features):
+            nc.vector.scalar_tensor_tensor(out=res[piece][:], in0=bank[f"y_ps{piece}"][:], scalar=inv[:, h : h + 1], in1=gate[:, h, features], op0=ALU.mult, op1=ALU.mult)
+            nc.sync.dma_start(out=out[0, h * P : (h + 1) * P, features], in_=res[piece][:])
 
         nc.vector.memset(ks_win[:].bitcast(I32), 0)
         nc.vector.memset(pos_win[:], 0.0)
@@ -279,7 +290,7 @@ def tile_attend_soft_alibi_gate_srtq256n1024t2048_kernel(tc, qT, k_words, k_scal
         gather_keys(1)
         load_og()
         cast_v0(1)
-        gather_first_v()
+        gather_first_v(0)
         cast_v0(2)
         pick_pos(0)
         turn_pos_only(1)
@@ -294,15 +305,17 @@ def tile_attend_soft_alibi_gate_srtq256n1024t2048_kernel(tc, qT, k_words, k_scal
         scores(1, 0)
         scores(0, 1)
         scores(1, 1)
+        make_bias(1)
         cast_v1(0)
         cast_v1(1)
         cast_v1(2)
-        gather_v(1, 0)
+        gather_first_v(1)
+        empty_scores(1)
+        add_bias_aside(1)
         gather_v(1, 1)
         add_bias(0, 0)
         add_bias(1, 0)
         add_bias(0, 1)
-        add_bias(1, 1)
         row_max(0)
         gather_vs(0)
         deal_vs(0)
@@ -335,9 +348,14 @@ def tile_attend_soft_alibi_gate_srtq256n1024t2048_kernel(tc, qT, k_words, k_scal
         weigh(1, 0)
         weigh(1, 1)
         invert()
-        product(0)
+        product(0, 0, slice(0, DV), 0)
+        product(0, 0, slice(0, DV), 1)
         quantize_w(1, 0, 0)
+        product(1, 1, slice(0, P), 0)
+        product(1, 2, slice(P, DV), 0)
         quantize_w(1, 1, 1)
-        product(1)
-        finish(0)
-        finish(1)
+        product(1, 1, slice(0, P), 1)
+        product(1, 2, slice(P, DV), 1)
+        finish(0, 0, slice(0, DV))
+        finish(1, 1, slice(0, P))
+        finish(1, 2, slice(P, DV))

@@ -20,12 +20,12 @@ AX = mybir.AxisListType
 P = 128
 PASS = 512
 KB = 1024
-V0_CUTS = (0, 1024, 1536, 2048)
+V0_CUTS = (0, 768, 1536, 2048)
 V1_CUTS = (0, 768, 1536, 2048)
 PREFIX = T - PASS
 BANK_OF = {"slope_ps": 6, "pos_ps0": 0, "pos_ps1": 1, "wide_ps0": 4, "wide_ps1": 5, "vs_ps0": 0, "vs_ps1": 1,
-           "a_ps00": 2, "a_ps01": 3, "a_ps10": 6, "a_ps11": 7, "vt_ps0": 2, "vt_ps1": 3,
-           "pt_ps00": 4, "pt_ps01": 5, "pt_ps10": 6, "pt_ps11": 7, "y_ps0": 0, "y_ps1": 1, "y_ps2": 2}
+           "a_ps00": 2, "a_ps01": 3, "a_ps10": 6, "a_ps11": 7, "vt_ps0": 3, "vt_ps1": 6,
+           "pt_ps00": 4, "pt_ps01": 5, "pt_ps10": 2, "pt_ps11": 7, "y_ps0": 0, "y_ps1": 1, "y_ps2": 3}
 
 
 def tile_attend_soft_alibi_gate_srtq256n1024t2048_kernel(tc, qT, k_words, k_scales, vT, vs, pos, slope, og, offs, out):
@@ -46,11 +46,11 @@ def tile_attend_soft_alibi_gate_srtq256n1024t2048_kernel(tc, qT, k_words, k_scal
 
         offsets = kept("offsets", [P, N // 16], U16)
         ident = kept("ident", [P, P], F32)
-        warm = placed("warm", [P, 65 * 64], F32, 0)
-        v0_raw = [kept("v0_raw0", [P, 1024], F32), placed("v0_raw1", [P, 512], F32, 16), placed("v0_raw2", [P, 512], F32, 0)]
-        pos_col = [placed(f"pos_col{g}", [P, 4], F32, g / 16) for g in range(2)]
-        slope_col = placed("slope_col", [P, 2], F32, 2 / 16)
-        slope_rows = placed("slope_rows", [P, P], F32, 3.5)
+        warm = placed("warm", [P, 1], F32, 80)
+        v0_raw = [kept("v0_raw0", [P, 768], F32), placed("v0_raw1", [P, 768], F32, 16), placed("v0_raw2", [P, 512], F32, 33)]
+        pos_col = [kept(f"pos_col{g}", [P, 4], F32) for g in range(2)]
+        slope_col = kept("slope_col", [P, 2], F32)
+        slope_rows = kept("slope_rows", [P, P], F32)
         kw_win = placed("kw_win", [P, T], I32, 4)
         q_raw = placed("q_raw", [P, 4, NQ], F32, 12)
         ks_win = placed("ks_win", [P, T], U8, 63)
@@ -58,22 +58,22 @@ def tile_attend_soft_alibi_gate_srtq256n1024t2048_kernel(tc, qT, k_words, k_scal
         v1_raw = [placed("v1_raw0", [P, 768], F32, 20), placed("v1_raw1", [P, 768], F32, 23), placed("v1_raw2", [P, 1536], F32, 64)]
         og_sb = placed("og_sb", [P, 2, DV], F32, 4)
         pos_g = [placed("pos_g0", [P, PASS], F32, 30), kept("pos_g1", [P, PASS], F32)]
-        ks_g = [kept("ks_g0", [P, PASS], U8), placed("ks_g1", [P, PASS], U8, 30)]
+        ks_g = [kept("ks_g0", [P, PASS], U8), kept("ks_g1", [P, PASS], U8)]
         pos_wide = [placed("pos_wide0", [P, PASS], F32, 32), placed("pos_wide1", [P, PASS], F32, 34)]
-        vs_g = [placed("vs_g0", [P, PASS], F32, 32), placed("vs_g1", [P, PASS], F32, 34)]
+        vs_g = [kept("vs_g0", [P, PASS], F32), placed("vs_g1", [P, PASS], F32, 34)]
         s_sb = [placed(f"s_sb{h}", [P, N], F32, 36 + 4 * h) for h in range(2)]
         v_cast1 = placed("v_cast1", [P, T], BF16, 72)
         v_bf = [placed(f"v_bf{g}", [P, DV, 4], BF16, 72 + 2 * g) for g in range(2)]
         gate_tanh = placed("gate_tanh", [P, 2, DV], F32, 42)
         p_sb = {(h, g): placed(f"p_sb{h}{g}", [P, 4, P], F32, 66 + 2 * g) for h in range(2) for g in range(2)}
-        vs_win = placed("vs_win", [P, T], F32, 55.5)
+        vs_win = placed("vs_win", [P, T], F32, 80)
         v_cast0 = kept("v_cast0", [P, T], BF16)
         v_g00 = kept("v_g00", [P, PASS], BF16)
         v_g01 = kept("v_g01", [P, PASS], BF16)
         v_g10 = kept("v_g10", [P, PASS], BF16)
         v_g11 = kept("v_g11", [P, PASS], BF16)
         kw_g = kept("kw_g", [P, N], U32)
-        vs_col = [kept(f"vs_col{g}", [P, 4], F32) for g in range(2)]
+        vs_col = [kept("vs_col0", [P, 4], F32), placed("vs_col1", [P, 4], F32, 90)]
         q_bf = kept("q_bf", [P, NQ, 4], BF16)
         q_codes = kept("q_codes", [P, NQ], U32)
         q_scales = kept("q_scales", [P, NQ], U8)
@@ -86,8 +86,8 @@ def tile_attend_soft_alibi_gate_srtq256n1024t2048_kernel(tc, qT, k_words, k_scal
         w_scales = [kept(f"w_scales{h}", [P, 2, P], U8) for h in range(2)]
         half_sum = kept("half_sum", [P, 2, 2], F32)
         total = kept("total", [P, 2], F32)
-        inv = kept("inv", [P, 2], F32)
-        res = [kept("res0", [P, DV], F32), kept("res1", [P, P], F32), kept("res2", [P, P], F32)]
+        inv = placed("inv", [P, 2], F32, 66)
+        res = [placed("res0", [P, DV], F32, 90), kept("res1", [P, P], F32), kept("res2", [P, P], F32)]
         a_sb = {1: placed("a_sb", [P, PASS], F32, 64)}
         bias_sb = {1: kept("bias_sb", [P, PASS], F32)}
         v_g = {(0, 0): v_g00, (0, 1): v_g01, (1, 0): v_g10, (1, 1): v_g11}
@@ -112,8 +112,8 @@ def tile_attend_soft_alibi_gate_srtq256n1024t2048_kernel(tc, qT, k_words, k_scal
             nc.sync.dma_start(out=v1_raw[part][:, 0 : V1_CUTS[part + 1] - V1_CUTS[part]], in_=vT[P : 2 * P, V1_CUTS[part] : V1_CUTS[part + 1]])
 
         def load_vs():
-            nc.sync.dma_start(out=vs_win[:, 0:PREFIX], in_=vs[:, 0:PREFIX])
-            nc.sync.dma_start(out=vs_win[:, PREFIX:T], in_=vs[:, PREFIX:T])
+            nc.gpsimd.memset(vs_win[0 : P - 1, :], 0.0)
+            nc.sync.dma_start(out=vs_win[P - 1 : P, :], in_=vs[0:1, :])
 
         def load_og():
             nc.sync.dma_start(out=og_sb[:], in_=og[0].rearrange("(h p) e -> p h e", p=P))
@@ -125,7 +125,7 @@ def tile_attend_soft_alibi_gate_srtq256n1024t2048_kernel(tc, qT, k_words, k_scal
             nc.vector.tensor_copy(pos_g[g][:], pos_win[:].indirect(half_list(g)))
 
         def gather_vs(g):
-            nc.vector.tensor_copy(vs_g[g][:], vs_win[:, 0 : (PREFIX, T)[g]].indirect(half_list(g)))
+            nc.vector.tensor_copy(vs_g[g][:], vs_win[:].indirect(half_list(g)))
 
         def gather_keys(g):
             window = kw_win[:, 0 : (PREFIX, T)[g]]
@@ -136,7 +136,7 @@ def tile_attend_soft_alibi_gate_srtq256n1024t2048_kernel(tc, qT, k_words, k_scal
             nc.tensor.transpose(ps[:], slope_rows[:], ident[:])
 
         def pick_slope():
-            nc.scalar.copy(out=slope_col[:], in_=bank["slope_ps"][:, 0:2])
+            nc.scalar.copy(out=slope_col[:], in_=bank["slope_ps"][:, P - 2 : P])
 
         def turn_pos_only(g):
             ps = new_bank(f"pos_ps{g}", [P, 4, P])
@@ -144,7 +144,7 @@ def tile_attend_soft_alibi_gate_srtq256n1024t2048_kernel(tc, qT, k_words, k_scal
                 nc.tensor.transpose(ps[:, j, :], pos_g[g][:, j * P : (j + 1) * P], ident[:])
 
         def pick_pos(g):
-            nc.scalar.copy(out=pos_col[g][:], in_=bank[f"pos_ps{g}"][:, :, 0])
+            nc.scalar.copy(out=pos_col[g][:], in_=bank[f"pos_ps{g}"][:, :, P - 1])
 
         def spread_pos(g):
             ps = new_bank(f"wide_ps{g}", [P, 4, P])
@@ -190,7 +190,7 @@ def tile_attend_soft_alibi_gate_srtq256n1024t2048_kernel(tc, qT, k_words, k_scal
             nc.scalar.activation(out=total[:, h : h + 1], in_=half_sum[:, h, 0:1], func=ACT.Identity, bias=half_sum[:, h, 1:2])
 
         def deal_vs(g):
-            nc.sync.dma_start(out=vs_col[g][:], in_=vs_g[g][0:1, :])
+            nc.sync.dma_start(out=vs_col[g][:], in_=vs_g[g][P - 1 : P, :])
 
         def cast_v0(part):
             a, b = V0_CUTS[part], V0_CUTS[part + 1]
@@ -227,7 +227,7 @@ def tile_attend_soft_alibi_gate_srtq256n1024t2048_kernel(tc, qT, k_words, k_scal
             nc.scalar.activation(out=gate_tanh[:], in_=og_sb[:], func=ACT.Tanh, scale=0.5)
 
         def make_gate():
-            nc.scalar.activation(out=gate[:], in_=gate_tanh[:], func=ACT.Copy, scale=0.5, bias=0.5)
+            nc.gpsimd.tensor_scalar(gate[:], gate_tanh[:], 0.5, 0.5, ALU.mult, ALU.add)
 
         def turn_p(h, g):
             ps = new_bank(f"pt_ps{h}{g}", [P, 4, P])
@@ -257,55 +257,59 @@ def tile_attend_soft_alibi_gate_srtq256n1024t2048_kernel(tc, qT, k_words, k_scal
             nc.sync.dma_start(out=out[0, h * P : (h + 1) * P, features], in_=res[piece][:])
 
         nc.vector.memset(ks_win[:].bitcast(I32), 0)
-        nc.vector.memset(pos_win[:], 0.0)
+        nc.vector.memset(slope_rows[0 : P - 2, :], 0.0)
+        nc.vector.memset(pos_win[0 : P - 1, :], 0.0)
         make_identity(nc, ident[:])
 
-        nc.sync.dma_start(offsets[:], offs)
-        load_v0(0)
-        load_scales()
-        nc.scalar.activation(out=warm[32:64, 0:1], in_=pos_win[32:64, 0:1], func=ACT.Exp)
-        nc.sync.dma_start(out=pos_win[0:1, :], in_=pos[0:1, :])
         kw_hbm = k_words[0].rearrange("p t r -> p (t r)").bitcast(I32)
+        nc.sync.dma_start(offsets[:], offs)
+        nc.sync.dma_start(out=pos_win[P - 1 : P, :], in_=pos[0:1, :])
+        nc.scalar.activation(out=warm[32:64, :], in_=pos_win[32:64, 0:1], func=ACT.Exp)
+        load_v0(0)
         load_v0(1)
-        nc.vector.memset(slope_rows[:], 0.0)
+        load_scales()
+        load_vs()
         nc.sync.dma_start(out=q_raw[:], in_=qT[0].rearrange("(p j) w -> p j w", j=4))
-        nc.sync.dma_start(out=slope_rows[0:2, :], in_=slope[0].rearrange("(h p) o -> h (p o)", p=P))
         load_v0(2)
+        nc.sync.dma_start(out=slope_rows[P - 2 : P, :], in_=slope[0].rearrange("(h p) o -> h (p o)", p=P))
         nc.sync.dma_start(out=kw_win[:, 0:PREFIX], in_=kw_hbm[:, 0:PREFIX])
-        nc.sync.dma_start(out=kw_win[:, PREFIX:T], in_=kw_hbm[:, PREFIX:T])
-        gather_scales(0)
         gather_pos(0)
         gather_pos(1)
+        nc.sync.dma_start(out=kw_win[:, PREFIX:T], in_=kw_hbm[:, PREFIX:T])
         load_v1(0)
         load_v1(1)
-        cast_v0(0)
-        turn_slope()
-        turn_pos_only(0)
+        gather_scales(0)
         gather_scales(1)
         load_v1(2)
-        load_vs()
+        cast_v0(0)
+        turn_pos_only(0)
+        turn_pos_only(1)
+        gather_vs(0)
         cast_q()
         quantize_q()
         gather_keys(0)
         gather_keys(1)
         load_og()
+        deal_vs(0)
         cast_v0(1)
-        gather_first_v(0)
-        cast_v0(2)
         pick_pos(0)
-        turn_pos_only(1)
         spread_pos(0)
-        gather_v(0, 1)
+        gather_first_v(0)
         pick_pos(1)
-        pick_slope()
         spread_pos(1)
+        cast_v0(2)
+        turn_slope()
+        gather_v(0, 1)
+        pick_slope()
         store_pos(0)
         store_pos(1)
+        make_bias(1)
         scores(0, 0)
         scores(1, 0)
         scores(0, 1)
         scores(1, 1)
-        make_bias(1)
+        turn_v(0, 0)
+        turn_v(0, 1)
         cast_v1(0)
         cast_v1(1)
         cast_v1(2)
@@ -317,13 +321,9 @@ def tile_attend_soft_alibi_gate_srtq256n1024t2048_kernel(tc, qT, k_words, k_scal
         add_bias(1, 0)
         add_bias(0, 1)
         row_max(0)
-        gather_vs(0)
-        deal_vs(0)
         gather_vs(1)
         deal_vs(1)
         row_max(1)
-        turn_v(0, 0)
-        turn_v(0, 1)
         turn_v(1, 0)
         turn_v(1, 1)
         exp_half(0, 0)
@@ -346,8 +346,8 @@ def tile_attend_soft_alibi_gate_srtq256n1024t2048_kernel(tc, qT, k_words, k_scal
         quantize_v(1)
         quantize_w(0, 0, 1)
         weigh(1, 0)
-        weigh(1, 1)
         invert()
+        weigh(1, 1)
         product(0, 0, slice(0, DV), 0)
         product(0, 0, slice(0, DV), 1)
         quantize_w(1, 0, 0)

@@ -24,8 +24,8 @@ V0_CUTS = (0, 768, 1536, 2048)
 V1_CUTS = (0, 768, 1536, 2048)
 PREFIX = T - PASS
 BANK_OF = {"slope_ps": 6, "pos_ps0": 0, "pos_ps1": 1, "wide_ps0": 4, "wide_ps1": 5, "vs_ps0": 0, "vs_ps1": 1,
-           "a_ps00": 2, "a_ps01": 3, "a_ps10": 6, "a_ps11": 7, "vt_ps0": 3, "vt_ps1": 6,
-           "pt_ps00": 4, "pt_ps01": 5, "pt_ps10": 2, "pt_ps11": 7, "y_ps0": 0, "y_ps1": 1, "y_ps2": 3}
+           "a_ps00": 2, "a_ps01": 3, "a_ps10": 6, "a_ps11": 7, "vt_ps0": 0, "vt_ps1": 1,
+           "pt_ps00": 4, "pt_ps01": 5, "pt_ps10": 6, "pt_ps11": 7, "y_ps0": 2, "y_ps1": 3, "y_ps2": 0}
 
 
 def tile_attend_soft_alibi_gate_srtq256n1024t2048_kernel(tc, qT, k_words, k_scales, vT, vs, pos, slope, og, offs, out):
@@ -48,24 +48,23 @@ def tile_attend_soft_alibi_gate_srtq256n1024t2048_kernel(tc, qT, k_words, k_scal
         ident = kept("ident", [P, P], F32)
         warm = placed("warm", [P, 1], F32, 80)
         v0_raw = [kept("v0_raw0", [P, 768], F32), placed("v0_raw1", [P, 768], F32, 16), placed("v0_raw2", [P, 512], F32, 33)]
-        pos_col = [kept(f"pos_col{g}", [P, 4], F32) for g in range(2)]
+        pos_col = [kept("pos_col0", [P, 4], F32), placed("pos_col1", [P, 4], F32, 16)]
         slope_col = kept("slope_col", [P, 2], F32)
-        slope_rows = kept("slope_rows", [P, P], F32)
         kw_win = placed("kw_win", [P, T], I32, 4)
         q_raw = placed("q_raw", [P, 4, NQ], F32, 12)
         ks_win = placed("ks_win", [P, T], U8, 63)
         pos_win = placed("pos_win", [P, T], F32, 20)
-        v1_raw = [placed("v1_raw0", [P, 768], F32, 20), placed("v1_raw1", [P, 768], F32, 23), placed("v1_raw2", [P, 1536], F32, 64)]
+        v1_raw = kept("v1_raw", [P, T], F32)
         og_sb = placed("og_sb", [P, 2, DV], F32, 4)
         pos_g = [placed("pos_g0", [P, PASS], F32, 30), kept("pos_g1", [P, PASS], F32)]
-        ks_g = [kept("ks_g0", [P, PASS], U8), kept("ks_g1", [P, PASS], U8)]
+        ks_g = kept("ks_g", [P, N], U8)
         pos_wide = [placed("pos_wide0", [P, PASS], F32, 32), placed("pos_wide1", [P, PASS], F32, 34)]
-        vs_g = [kept("vs_g0", [P, PASS], F32), placed("vs_g1", [P, PASS], F32, 34)]
+        vs_g = kept("vs_g", [P, N], F32)
         s_sb = [placed(f"s_sb{h}", [P, N], F32, 36 + 4 * h) for h in range(2)]
-        v_cast1 = placed("v_cast1", [P, T], BF16, 72)
-        v_bf = [placed(f"v_bf{g}", [P, DV, 4], BF16, 72 + 2 * g) for g in range(2)]
+        v_cast1 = kept("v_cast1", [P, PREFIX], BF16)
+        v_bf = [kept(f"v_bf{f}", [P, 2, P, 4], BF16) for f in range(2)]
         gate_tanh = placed("gate_tanh", [P, 2, DV], F32, 42)
-        p_sb = {(h, g): placed(f"p_sb{h}{g}", [P, 4, P], F32, 66 + 2 * g) for h in range(2) for g in range(2)}
+        p_sb = {(h, g): placed(f"p_sb{h}{g}", [P, 4, P], F32, 64 + 4 * h + 2 * g) for h in range(2) for g in range(2)}
         vs_win = placed("vs_win", [P, T], F32, 80)
         v_cast0 = kept("v_cast0", [P, T], BF16)
         v_g00 = kept("v_g00", [P, PASS], BF16)
@@ -78,18 +77,18 @@ def tile_attend_soft_alibi_gate_srtq256n1024t2048_kernel(tc, qT, k_words, k_scal
         q_codes = kept("q_codes", [P, NQ], U32)
         q_scales = kept("q_scales", [P, NQ], U8)
         neg_max = [kept(f"neg_max{h}", [P, 1], F32) for h in range(2)]
-        v_codes = [placed(f"v_codes{g}", [P, DV], U32, 32 + 2 * g) for g in range(2)]
-        v_scales = [kept(f"v_scales{g}", [P, DV], U8) for g in range(2)]
+        v_codes = [placed("v_codes0", [P, 2, P], U32, 24), kept("v_codes1", [P, 2, P], U32)]
+        v_scales = [kept(f"v_scales{f}", [P, 2, P], U8) for f in range(2)]
         gate = kept("gate", [P, 2, DV], F32)
         w_bf = [kept(f"w_bf{h}", [P, 2, P, 4], BF16) for h in range(2)]
         w_codes = [kept(f"w_codes{h}", [P, 2, P], U32) for h in range(2)]
         w_scales = [kept(f"w_scales{h}", [P, 2, P], U8) for h in range(2)]
         half_sum = kept("half_sum", [P, 2, 2], F32)
         total = kept("total", [P, 2], F32)
-        inv = placed("inv", [P, 2], F32, 66)
+        inv = placed("inv", [P, 2], F32, 68)
         res = [placed("res0", [P, DV], F32, 90), kept("res1", [P, P], F32), kept("res2", [P, P], F32)]
-        a_sb = {1: placed("a_sb", [P, PASS], F32, 64)}
-        bias_sb = {1: kept("bias_sb", [P, PASS], F32)}
+        a_sb = {1: placed("a_sb", [P, PASS], F32, 34)}
+        bias_sb = {1: placed("bias_sb", [P, PASS], F32, 24)}
         v_g = {(0, 0): v_g00, (0, 1): v_g01, (1, 0): v_g10, (1, 1): v_g11}
         bank = {}
 
@@ -109,23 +108,36 @@ def tile_attend_soft_alibi_gate_srtq256n1024t2048_kernel(tc, qT, k_words, k_scal
                 nc.sync.dma_start(out=ks_win[32 * quad : 32 * quad + 4, :].bitcast(I32), in_=ks_hbm[4 * quad : 4 * quad + 4, :])
 
         def load_v1(part):
-            nc.sync.dma_start(out=v1_raw[part][:, 0 : V1_CUTS[part + 1] - V1_CUTS[part]], in_=vT[P : 2 * P, V1_CUTS[part] : V1_CUTS[part + 1]])
+            nc.sync.dma_start(out=v1_raw[:, V1_CUTS[part] : V1_CUTS[part + 1]], in_=vT[P : 2 * P, V1_CUTS[part] : V1_CUTS[part + 1]])
 
         def load_vs():
             nc.gpsimd.memset(vs_win[0 : P - 1, :], 0.0)
             nc.sync.dma_start(out=vs_win[P - 1 : P, :], in_=vs[0:1, :])
 
+        def load_keys(part):
+            cut = (0, PREFIX, T)
+            nc.sync.dma_start(out=kw_win[:, cut[part] : cut[part + 1]], in_=k_words[0].rearrange("p t r -> p (t r)").bitcast(I32)[:, cut[part] : cut[part + 1]])
+
+        def load_q():
+            nc.sync.dma_start(out=q_raw[:], in_=qT[0].rearrange("(p j) w -> p j w", j=4))
+
+        def load_slope():
+            nc.sync.dma_start(out=pos_g[0][P - 2 : P, 0:P], in_=slope[0].rearrange("(h p) o -> h (p o)", p=P))
+
+        def load_pos():
+            nc.sync.dma_start(out=pos_win[P - 1 : P, :], in_=pos[0:1, :])
+
         def load_og():
             nc.sync.dma_start(out=og_sb[:], in_=og[0].rearrange("(h p) e -> p h e", p=P))
 
-        def gather_scales(g):
-            nc.vector.tensor_copy(ks_g[g][:], ks_win[:].indirect(half_list(g)))
+        def gather_scales():
+            nc.vector.tensor_copy(ks_g[:], ks_win[:].indirect(offsets[:]))
 
         def gather_pos(g):
             nc.vector.tensor_copy(pos_g[g][:], pos_win[:].indirect(half_list(g)))
 
-        def gather_vs(g):
-            nc.vector.tensor_copy(vs_g[g][:], vs_win[:].indirect(half_list(g)))
+        def gather_vs():
+            nc.vector.tensor_copy(vs_g[:], vs_win[:].indirect(offsets[:]))
 
         def gather_keys(g):
             window = kw_win[:, 0 : (PREFIX, T)[g]]
@@ -133,7 +145,7 @@ def tile_attend_soft_alibi_gate_srtq256n1024t2048_kernel(tc, qT, k_words, k_scal
 
         def turn_slope():
             ps = new_bank("slope_ps", [P, P])
-            nc.tensor.transpose(ps[:], slope_rows[:], ident[:])
+            nc.tensor.transpose(ps[:], pos_g[0][:, 0:P], ident[:])
 
         def pick_slope():
             nc.scalar.copy(out=slope_col[:], in_=bank["slope_ps"][:, P - 2 : P])
@@ -167,7 +179,7 @@ def tile_attend_soft_alibi_gate_srtq256n1024t2048_kernel(tc, qT, k_words, k_scal
             qs = slice(h * P, (h + 1) * P)
             ps = new_bank(f"a_ps{h}{g}", [P, PASS])
             nc.tensor.matmul_mx(out=ps[:], lhsT=q_codes[:, qs].bitcast(FP8X4), lhsT_scale=q_scales[:, qs],
-                                rhs=kw_g[:, slots(g)].bitcast(FP8X4), rhs_scale=ks_g[g][:], start=True, stop=True)
+                                rhs=kw_g[:, slots(g)].bitcast(FP8X4), rhs_scale=ks_g[:, slots(g)], start=True, stop=True)
 
         def add_bias(h, g):
             nc.vector.scalar_tensor_tensor(out=s_sb[h][:, slots(g)], in0=pos_wide[g][:], scalar=slope_col[:, h : h + 1],
@@ -190,7 +202,7 @@ def tile_attend_soft_alibi_gate_srtq256n1024t2048_kernel(tc, qT, k_words, k_scal
             nc.scalar.activation(out=total[:, h : h + 1], in_=half_sum[:, h, 0:1], func=ACT.Identity, bias=half_sum[:, h, 1:2])
 
         def deal_vs(g):
-            nc.sync.dma_start(out=vs_col[g][:], in_=vs_g[g][P - 1 : P, :])
+            nc.sync.dma_start(out=vs_col[g][:], in_=vs_g[P - 1 : P, slots(g)])
 
         def cast_v0(part):
             a, b = V0_CUTS[part], V0_CUTS[part + 1]
@@ -201,27 +213,31 @@ def tile_attend_soft_alibi_gate_srtq256n1024t2048_kernel(tc, qT, k_words, k_scal
 
         def cast_v1(part):
             a, b = V1_CUTS[part], V1_CUTS[part + 1]
-            nc.scalar.activation(out=v_cast1[:, a:b], in_=v1_raw[part][:, 0 : b - a], func=ACT.Copy)
+            nc.scalar.activation(out=v_cast1[:, a:b], in_=v1_raw[:, a:b], func=ACT.Copy)
 
         def gather_first_v(f):
             window = (v_cast0, v_cast1)[f][:, 0:PREFIX]
             nc.scalar.activation(out=v_g[f, 0][:].rearrange("p (u s e) -> p s u e", u=2, e=2), in_=window.indirect(half_list(0)), func=ACT.Copy)
 
-        def gather_v(f, g):
-            nc.scalar.activation(out=v_g[f, g][:], in_=(v_cast0, v_cast1)[f][:].indirect(half_list(g)), func=ACT.Copy)
+        def gather_v01():
+            nc.scalar.activation(out=v_g[0, 1][:], in_=v_cast0[:].indirect(half_list(1)), func=ACT.Copy)
+
+        def gather_v11():
+            nc.vector.tensor_copy(v_g[1, 1][:], v1_raw[:].indirect(half_list(1)))
 
         def turn_v(f, g):
             pairs = v_g[f, g][:].bitcast(F32)
-            ps = bank[f"vt_ps{g}"] if f else new_bank(f"vt_ps{g}", [P, 2, 2, P])
+            ps = bank[f"vt_ps{f}"] if g else new_bank(f"vt_ps{f}", [P, 2, 2, P])
             for u in range(2):
-                nc.tensor.transpose(ps[:, f, u, :], pairs[:, u : 2 * P : 2] if g else pairs[:, u * P : (u + 1) * P], ident[:])
+                nc.tensor.transpose(ps[:, g, u, :], pairs[:, u : 2 * P : 2] if g else pairs[:, u * P : (u + 1) * P], ident[:])
 
-        def store_v(g):
-            nc.scalar.copy(out=v_bf[g][:].rearrange("p c t -> p (c t)").bitcast(F32).rearrange("p (f c u) -> p f c u", f=2, u=2), in_=bank[f"vt_ps{g}"][:].rearrange("p f u c -> p f c u"))
+        def store_v(f):
+            nc.scalar.copy(out=v_bf[f][:].rearrange("p g c t -> p (g c t)").bitcast(F32).rearrange("p (g c u) -> p g c u", g=2, u=2),
+                           in_=bank[f"vt_ps{f}"][:].rearrange("p g u c -> p g c u"))
 
-        def quantize_v(g):
-            nc.vector.quantize_mx(out=v_codes[g][:].bitcast(FP8X4), scales=v_scales[g][:],
-                                  in_=v_bf[g][:].rearrange("p c t -> p (c t)"))
+        def quantize_v(f):
+            nc.vector.quantize_mx(out=v_codes[f][:].rearrange("p g c -> p (g c)").bitcast(FP8X4), scales=v_scales[f][:].rearrange("p g c -> p (g c)"),
+                                  in_=v_bf[f][:].rearrange("p g c t -> p (g c t)"))
 
         def make_tanh():
             nc.scalar.activation(out=gate_tanh[:], in_=og_sb[:], func=ACT.Tanh, scale=0.5)
@@ -247,50 +263,46 @@ def tile_attend_soft_alibi_gate_srtq256n1024t2048_kernel(tc, qT, k_words, k_scal
         def invert():
             nc.vector.reciprocal(inv[:], total[:])
 
-        def product(h, piece, features, g):
-            ps = bank[f"y_ps{piece}"] if g else new_bank(f"y_ps{piece}", [P, features.stop - features.start])
-            nc.tensor.matmul_mx(out=ps[:], lhsT=w_codes[h][:, g, :].bitcast(FP8X4), lhsT_scale=w_scales[h][:, g, :],
-                                rhs=v_codes[g][:, features].bitcast(FP8X4), rhs_scale=v_scales[g][:, features], start=(g == 0), stop=(g == 1))
+        def product(piece, h, f, g, columns):
+            nc.tensor.matmul_mx(out=bank[f"y_ps{piece}"][:, columns], lhsT=w_codes[h][:, g, :].bitcast(FP8X4), lhsT_scale=w_scales[h][:, g, :],
+                                rhs=v_codes[f][:, g, :].bitcast(FP8X4), rhs_scale=v_scales[f][:, g, :], start=(g == 0), stop=(g == 1))
 
         def finish(h, piece, features):
             nc.vector.scalar_tensor_tensor(out=res[piece][:], in0=bank[f"y_ps{piece}"][:], scalar=inv[:, h : h + 1], in1=gate[:, h, features], op0=ALU.mult, op1=ALU.mult)
             nc.sync.dma_start(out=out[0, h * P : (h + 1) * P, features], in_=res[piece][:])
 
         nc.vector.memset(ks_win[:].bitcast(I32), 0)
-        nc.vector.memset(slope_rows[0 : P - 2, :], 0.0)
         nc.vector.memset(pos_win[0 : P - 1, :], 0.0)
         make_identity(nc, ident[:])
-
-        kw_hbm = k_words[0].rearrange("p t r -> p (t r)").bitcast(I32)
         nc.sync.dma_start(offsets[:], offs)
-        nc.sync.dma_start(out=pos_win[P - 1 : P, :], in_=pos[0:1, :])
+        load_pos()
         nc.scalar.activation(out=warm[32:64, :], in_=pos_win[32:64, 0:1], func=ACT.Exp)
         load_v0(0)
         load_v0(1)
         load_scales()
         load_vs()
-        nc.sync.dma_start(out=q_raw[:], in_=qT[0].rearrange("(p j) w -> p j w", j=4))
+        load_q()
         load_v0(2)
-        nc.sync.dma_start(out=slope_rows[P - 2 : P, :], in_=slope[0].rearrange("(h p) o -> h (p o)", p=P))
-        nc.sync.dma_start(out=kw_win[:, 0:PREFIX], in_=kw_hbm[:, 0:PREFIX])
         gather_pos(0)
         gather_pos(1)
-        nc.sync.dma_start(out=kw_win[:, PREFIX:T], in_=kw_hbm[:, PREFIX:T])
-        load_v1(0)
-        load_v1(1)
-        gather_scales(0)
-        gather_scales(1)
-        load_v1(2)
-        cast_v0(0)
         turn_pos_only(0)
         turn_pos_only(1)
-        gather_vs(0)
+        load_slope()
+        load_keys(0)
+        load_keys(1)
+        load_v1(0)
+        load_v1(1)
+        load_v1(2)
+        gather_scales()
+        gather_vs()
+        cast_v0(0)
         cast_q()
         quantize_q()
         gather_keys(0)
         gather_keys(1)
         load_og()
         deal_vs(0)
+        deal_vs(1)
         cast_v0(1)
         pick_pos(0)
         spread_pos(0)
@@ -299,38 +311,36 @@ def tile_attend_soft_alibi_gate_srtq256n1024t2048_kernel(tc, qT, k_words, k_scal
         spread_pos(1)
         cast_v0(2)
         turn_slope()
-        gather_v(0, 1)
+        gather_v01()
         pick_slope()
         store_pos(0)
         store_pos(1)
         make_bias(1)
+        turn_v(0, 0)
+        turn_v(0, 1)
+        store_v(0)
         scores(0, 0)
         scores(1, 0)
         scores(0, 1)
         scores(1, 1)
-        turn_v(0, 0)
-        turn_v(0, 1)
-        cast_v1(0)
-        cast_v1(1)
-        cast_v1(2)
-        gather_first_v(1)
-        empty_scores(1)
-        add_bias_aside(1)
-        gather_v(1, 1)
         add_bias(0, 0)
         add_bias(1, 0)
         add_bias(0, 1)
         row_max(0)
-        gather_vs(1)
-        deal_vs(1)
+        gather_v11()
+        cast_v1(0)
+        cast_v1(1)
+        empty_scores(1)
+        add_bias_aside(1)
+        gather_first_v(1)
         row_max(1)
+        quantize_v(0)
         turn_v(1, 0)
         turn_v(1, 1)
         exp_half(0, 0)
         turn_p(0, 0)
         exp_half(0, 1)
         turn_p(0, 1)
-        store_v(0)
         store_v(1)
         exp_half(1, 0)
         turn_p(1, 0)
@@ -341,21 +351,24 @@ def tile_attend_soft_alibi_gate_srtq256n1024t2048_kernel(tc, qT, k_words, k_scal
         make_tanh()
         make_gate()
         weigh(0, 0)
-        quantize_v(0)
         weigh(0, 1)
         quantize_v(1)
         quantize_w(0, 0, 1)
         weigh(1, 0)
         invert()
         weigh(1, 1)
-        product(0, 0, slice(0, DV), 0)
-        product(0, 0, slice(0, DV), 1)
+        new_bank("y_ps0", [P, DV])
+        for f in range(2):
+            for g in range(2):
+                product(0, 0, f, g, slice(f * P, (f + 1) * P))
         quantize_w(1, 0, 0)
-        product(1, 1, slice(0, P), 0)
-        product(1, 2, slice(P, DV), 0)
+        new_bank("y_ps1", [P, P])
+        new_bank("y_ps2", [P, P])
+        product(1, 1, 0, 0, slice(0, P))
+        product(2, 1, 1, 0, slice(0, P))
         quantize_w(1, 1, 1)
-        product(1, 1, slice(0, P), 1)
-        product(1, 2, slice(P, DV), 1)
+        product(1, 1, 0, 1, slice(0, P))
+        product(2, 1, 1, 1, slice(0, P))
         finish(0, 0, slice(0, DV))
         finish(1, 1, slice(0, P))
         finish(1, 2, slice(P, DV))

@@ -22,6 +22,8 @@ PASS = 512
 KB = 1024
 V0_CUTS = (0, 768, 1536, 2048)
 V1_CUTS = (0, 768, 1536, 2048)
+SHARE = 128
+LATE = T - SHARE
 PREFIX = T - PASS
 BANK_OF = {"slope_ps": 6, "pos_ps0": 0, "pos_ps1": 1, "wide_ps0": 4, "wide_ps1": 5, "vs_ps0": 0, "vs_ps1": 1,
            "a_ps00": 2, "a_ps01": 3, "a_ps10": 6, "a_ps11": 7, "vt_ps0": 0, "vt_ps1": 1,
@@ -61,7 +63,7 @@ def tile_attend_soft_alibi_gate_srtq256n1024t2048_kernel(tc, qT, k_words, k_scal
         pos_wide = [placed("pos_wide0", [P, PASS], F32, 32), placed("pos_wide1", [P, PASS], F32, 34)]
         vs_g = kept("vs_g", [P, N], F32)
         s_sb = [placed(f"s_sb{h}", [P, N], F32, 36 + 4 * h) for h in range(2)]
-        v_cast1 = kept("v_cast1", [P, PREFIX], BF16)
+        v_cast1 = kept("v_cast1", [P, LATE], BF16)
         v_bf = [kept(f"v_bf{f}", [P, 2, P, 4], BF16) for f in range(2)]
         gate_tanh = placed("gate_tanh", [P, 2, DV], F32, 42)
         p_sb = {(h, g): placed(f"p_sb{h}{g}", [P, 4, P], F32, 64 + 4 * h + 2 * g) for h in range(2) for g in range(2)}
@@ -77,7 +79,7 @@ def tile_attend_soft_alibi_gate_srtq256n1024t2048_kernel(tc, qT, k_words, k_scal
         q_codes = kept("q_codes", [P, NQ], U32)
         q_scales = kept("q_scales", [P, NQ], U8)
         neg_max = [kept(f"neg_max{h}", [P, 1], F32) for h in range(2)]
-        v_codes = [placed("v_codes0", [P, 2, P], U32, 24), kept("v_codes1", [P, 2, P], U32)]
+        v_codes = [placed("v_codes0", [P, 2, P], U32, 34), placed("v_codes1", [P, 2, P], U32, 66)]
         v_scales = [kept(f"v_scales{f}", [P, 2, P], U8) for f in range(2)]
         gate = kept("gate", [P, 2, DV], F32)
         w_bf = [kept(f"w_bf{h}", [P, 2, P, 4], BF16) for h in range(2)]
@@ -87,8 +89,6 @@ def tile_attend_soft_alibi_gate_srtq256n1024t2048_kernel(tc, qT, k_words, k_scal
         total = kept("total", [P, 2], F32)
         inv = placed("inv", [P, 2], F32, 68)
         res = [placed("res0", [P, DV], F32, 90), kept("res1", [P, P], F32), kept("res2", [P, P], F32)]
-        a_sb = {1: placed("a_sb", [P, PASS], F32, 34)}
-        bias_sb = {1: placed("bias_sb", [P, PASS], F32, 24)}
         v_g = {(0, 0): v_g00, (0, 1): v_g01, (1, 0): v_g10, (1, 1): v_g11}
         bank = {}
 
@@ -166,11 +166,11 @@ def tile_attend_soft_alibi_gate_srtq256n1024t2048_kernel(tc, qT, k_words, k_scal
         def store_pos(g):
             nc.scalar.copy(out=pos_wide[g][:], in_=bank[f"wide_ps{g}"][:].rearrange("p j s -> p (j s)"))
 
-        def make_bias(g):
-            nc.gpsimd.tensor_scalar(bias_sb[g][:], pos_wide[g][:], slope_col[:, 1:2], 0.0, ALU.mult, ALU.add)
-
         def cast_q():
-            nc.gpsimd.tensor_scalar(q_bf[:], q_raw[:].rearrange("p j w -> p w j"), 1.0, 0.0, ALU.mult, ALU.add)
+            nc.gpsimd.tensor_scalar(q_bf[:, 0:P, :], q_raw[:, :, 0:P].rearrange("p j w -> p w j"), 1.0, 0.0, ALU.mult, ALU.add)
+
+        def cast_q_rest():
+            nc.scalar.activation(out=q_bf[:, P:NQ, :], in_=q_raw[:, :, P:NQ].rearrange("p j w -> p w j"), func=ACT.Copy)
 
         def quantize_q():
             nc.vector.quantize_mx(out=q_codes[:].bitcast(FP8X4), scales=q_scales[:], in_=q_bf[:].rearrange("p w j -> p (w j)"))
@@ -184,12 +184,6 @@ def tile_attend_soft_alibi_gate_srtq256n1024t2048_kernel(tc, qT, k_words, k_scal
         def add_bias(h, g):
             nc.vector.scalar_tensor_tensor(out=s_sb[h][:, slots(g)], in0=pos_wide[g][:], scalar=slope_col[:, h : h + 1],
                                            in1=bank[f"a_ps{h}{g}"][:], op0=ALU.mult, op1=ALU.add)
-
-        def empty_scores(g):
-            nc.scalar.copy(out=a_sb[g][:], in_=bank[f"a_ps1{g}"][:])
-
-        def add_bias_aside(g):
-            nc.gpsimd.tensor_tensor(s_sb[1][:, slots(g)], a_sb[g][:], bias_sb[g][:], ALU.add)
 
         def row_max(h):
             nc.vector.tensor_reduce(out=neg_max[h][:], in_=s_sb[h][:], axis=AX.X, op=ALU.max, negate=True)
@@ -222,8 +216,14 @@ def tile_attend_soft_alibi_gate_srtq256n1024t2048_kernel(tc, qT, k_words, k_scal
         def gather_v01():
             nc.scalar.activation(out=v_g[0, 1][:], in_=v_cast0[:].indirect(half_list(1)), func=ACT.Copy)
 
-        def gather_v11():
-            nc.vector.tensor_copy(v_g[1, 1][:], v1_raw[:].indirect(half_list(1)))
+        def cast_v1_end():
+            nc.scalar.activation(out=v_cast1[:, PREFIX:LATE], in_=v1_raw[:, PREFIX:LATE], func=ACT.Copy)
+
+        def gather_v11_first():
+            nc.scalar.activation(out=v_g[1, 1][:, 0 : PASS - SHARE], in_=v_cast1[:].indirect(offsets[:, 32 : 64 - SHARE // 16]), func=ACT.Copy)
+
+        def gather_v11_last():
+            nc.vector.tensor_copy(v_g[1, 1][:, PASS - SHARE : PASS], v1_raw[:].indirect(offsets[:, 64 - SHARE // 16 : 64]))
 
         def turn_v(f, g):
             pairs = v_g[f, g][:].bitcast(F32)
@@ -243,7 +243,7 @@ def tile_attend_soft_alibi_gate_srtq256n1024t2048_kernel(tc, qT, k_words, k_scal
             nc.scalar.activation(out=gate_tanh[:], in_=og_sb[:], func=ACT.Tanh, scale=0.5)
 
         def make_gate():
-            nc.gpsimd.tensor_scalar(gate[:], gate_tanh[:], 0.5, 0.5, ALU.mult, ALU.add)
+            nc.scalar.activation(out=gate[:], in_=gate_tanh[:], func=ACT.Copy, scale=0.5, bias=0.5)
 
         def turn_p(h, g):
             ps = new_bank(f"pt_ps{h}{g}", [P, 4, P])
@@ -279,8 +279,8 @@ def tile_attend_soft_alibi_gate_srtq256n1024t2048_kernel(tc, qT, k_words, k_scal
         nc.scalar.activation(out=warm[32:64, :], in_=pos_win[32:64, 0:1], func=ACT.Exp)
         load_v0(0)
         load_v0(1)
-        load_scales()
         load_vs()
+        load_scales()
         load_q()
         load_v0(2)
         gather_pos(0)
@@ -293,29 +293,29 @@ def tile_attend_soft_alibi_gate_srtq256n1024t2048_kernel(tc, qT, k_words, k_scal
         load_v1(0)
         load_v1(1)
         load_v1(2)
-        gather_scales()
         gather_vs()
+        gather_scales()
         cast_v0(0)
         cast_q()
+        cast_v0(1)
+        gather_first_v(0)
+        pick_pos(0)
+        spread_pos(0)
+        pick_pos(1)
+        spread_pos(1)
+        cast_q_rest()
         quantize_q()
         gather_keys(0)
         gather_keys(1)
-        load_og()
         deal_vs(0)
+        load_og()
         deal_vs(1)
-        cast_v0(1)
-        pick_pos(0)
-        spread_pos(0)
-        gather_first_v(0)
-        pick_pos(1)
-        spread_pos(1)
         cast_v0(2)
         turn_slope()
         gather_v01()
         pick_slope()
         store_pos(0)
         store_pos(1)
-        make_bias(1)
         turn_v(0, 0)
         turn_v(0, 1)
         store_v(0)
@@ -326,13 +326,14 @@ def tile_attend_soft_alibi_gate_srtq256n1024t2048_kernel(tc, qT, k_words, k_scal
         add_bias(0, 0)
         add_bias(1, 0)
         add_bias(0, 1)
+        add_bias(1, 1)
         row_max(0)
-        gather_v11()
+        gather_v11_last()
         cast_v1(0)
         cast_v1(1)
-        empty_scores(1)
-        add_bias_aside(1)
+        cast_v1_end()
         gather_first_v(1)
+        gather_v11_first()
         row_max(1)
         quantize_v(0)
         turn_v(1, 0)

@@ -51,16 +51,17 @@ def tile_attend_soft_alibi_gate_srtq256n1024t2048_kernel(tc, qT, k_words, k_scal
         warm = placed("warm", [P, 1], F32, 80)
         v0_raw = [kept("v0_raw0", [P, 768], F32), placed("v0_raw1", [P, 768], F32, 16), placed("v0_raw2", [P, 512], F32, 33)]
         pos_col = [kept("pos_col0", [P, 4], F32), placed("pos_col1", [P, 4], F32, 16)]
-        slope_col = kept("slope_col", [P, 2], F32)
+        slope_rows = kept("slope_rows", [P, P], F32)
+        slope_col = placed("slope_col", [P, 2], F32, 33.5)
         kw_win = placed("kw_win", [P, T], I32, 4)
         q_raw = placed("q_raw", [P, 4, NQ], F32, 12)
         ks_win = placed("ks_win", [P, T], U8, 63)
         pos_win = placed("pos_win", [P, T], F32, 20)
         v1_raw = kept("v1_raw", [P, T], F32)
         og_sb = placed("og_sb", [P, 2, DV], F32, 4)
-        pos_g = [placed("pos_g0", [P, PASS], F32, 30), kept("pos_g1", [P, PASS], F32)]
+        pos_g = [kept("pos_g0", [P, PASS], F32), kept("pos_g1", [P, PASS], F32)]
         ks_g = kept("ks_g", [P, N], U8)
-        pos_wide = [placed("pos_wide0", [P, PASS], F32, 32), placed("pos_wide1", [P, PASS], F32, 34)]
+        pos_wide = [placed("pos_wide0", [P, PASS], F32, 31.5), placed("pos_wide1", [P, PASS], F32, 34)]
         vs_g = kept("vs_g", [P, N], F32)
         s_sb = [placed(f"s_sb{h}", [P, N], F32, 36 + 4 * h) for h in range(2)]
         v_cast1 = kept("v_cast1", [P, LATE], BF16)
@@ -105,7 +106,7 @@ def tile_attend_soft_alibi_gate_srtq256n1024t2048_kernel(tc, qT, k_words, k_scal
         def load_scales():
             ks_hbm = k_scales[0].bitcast(I32)
             for quad in range(4):
-                nc.sync.dma_start(out=ks_win[32 * quad : 32 * quad + 4, :].bitcast(I32), in_=ks_hbm[4 * quad : 4 * quad + 4, :])
+                nc.scalar.dma_start(out=ks_win[32 * quad : 32 * quad + 4, :].bitcast(I32), in_=ks_hbm[4 * quad : 4 * quad + 4, :])
 
         def load_v1(part):
             nc.sync.dma_start(out=v1_raw[:, V1_CUTS[part] : V1_CUTS[part + 1]], in_=vT[P : 2 * P, V1_CUTS[part] : V1_CUTS[part + 1]])
@@ -122,7 +123,7 @@ def tile_attend_soft_alibi_gate_srtq256n1024t2048_kernel(tc, qT, k_words, k_scal
             nc.sync.dma_start(out=q_raw[:], in_=qT[0].rearrange("(p j) w -> p j w", j=4))
 
         def load_slope():
-            nc.sync.dma_start(out=pos_g[0][P - 2 : P, 0:P], in_=slope[0].rearrange("(h p) o -> h (p o)", p=P))
+            nc.sync.dma_start(out=slope_rows[P - 2 : P, :], in_=slope[0].rearrange("(h p) o -> h (p o)", p=P))
 
         def load_pos():
             nc.sync.dma_start(out=pos_win[P - 1 : P, :], in_=pos[0:1, :])
@@ -145,7 +146,7 @@ def tile_attend_soft_alibi_gate_srtq256n1024t2048_kernel(tc, qT, k_words, k_scal
 
         def turn_slope():
             ps = new_bank("slope_ps", [P, P])
-            nc.tensor.transpose(ps[:], pos_g[0][:, 0:P], ident[:])
+            nc.tensor.transpose(ps[:], slope_rows[:], ident[:])
 
         def pick_slope():
             nc.scalar.copy(out=slope_col[:], in_=bank["slope_ps"][:, P - 2 : P])
@@ -273,28 +274,29 @@ def tile_attend_soft_alibi_gate_srtq256n1024t2048_kernel(tc, qT, k_words, k_scal
 
         nc.vector.memset(ks_win[:].bitcast(I32), 0)
         nc.vector.memset(pos_win[0 : P - 1, :], 0.0)
+        nc.vector.memset(slope_rows[0 : P - 2, :], 0.0)
         make_identity(nc, ident[:])
         nc.sync.dma_start(offsets[:], offs)
         load_pos()
+        load_scales()
         nc.scalar.activation(out=warm[32:64, :], in_=pos_win[32:64, 0:1], func=ACT.Exp)
         load_v0(0)
         load_v0(1)
-        load_vs()
-        load_scales()
         load_q()
+        load_vs()
+        load_slope()
         load_v0(2)
         gather_pos(0)
         gather_pos(1)
         turn_pos_only(0)
         turn_pos_only(1)
-        load_slope()
         load_keys(0)
         load_keys(1)
         load_v1(0)
         load_v1(1)
         load_v1(2)
-        gather_vs()
         gather_scales()
+        gather_vs()
         cast_v0(0)
         cast_q()
         cast_v0(1)

@@ -19,167 +19,133 @@ AX = mybir.AxisListType
 
 P = 128
 PASS = 512
+WORD = 4
+LANES = 16
 KB = 1024
-V0_CUTS = (0, 768, 1536, 2048)
-V1_CUTS = (0, 768, 1536, 2048)
+PREFIX = T - PASS
+CUTS = (0, PREFIX // 2, PREFIX, T)
 SHARE = 128
 LATE = T - SHARE
-PREFIX = T - PASS
-BANK_OF = {"slope_ps": 6, "pos_ps0": 0, "pos_ps1": 1, "wide_ps0": 4, "wide_ps1": 5, "vs_ps0": 0, "vs_ps1": 1,
-           "a_ps00": 2, "a_ps01": 3, "a_ps10": 6, "a_ps11": 7, "vt_ps0": 0, "vt_ps1": 1,
-           "pt_ps00": 4, "pt_ps01": 5, "pt_ps10": 6, "pt_ps11": 7, "y_ps0": 2, "y_ps1": 3, "y_ps2": 0}
+BANK_OF = {"pos_ps0": 0, "vt_ps0": 0, "y_ps2": 0,
+           "pos_ps1": 1, "vt_ps1": 1,
+           "a_ps00": 2, "y_ps0": 2,
+           "a_ps01": 3, "y_ps1": 3,
+           "wide_ps0": 4, "pt_ps00": 4,
+           "wide_ps1": 5, "pt_ps01": 5,
+           "slope_ps": 6, "a_ps10": 6, "pt_ps10": 6,
+           "a_ps11": 7, "pt_ps11": 7}
 
 
 def tile_attend_soft_alibi_gate_srtq256n1024t2048_kernel(tc, qT, k_words, k_scales, vT, vs, pos, slope, og, offs, out):
     nc = tc.nc
     with ExitStack() as ctx:
         keep = ctx.enter_context(tc.tile_pool(name="keep", bufs=1))
-        late = ctx.enter_context(tc.tile_pool(name="late", bufs=1))
+        shared = ctx.enter_context(tc.tile_pool(name="shared", bufs=1))
         psum = ctx.enter_context(tc.psum_pool(name="psum", bufs=1))
-
-        def slots(g):
-            return slice(g * PASS, (g + 1) * PASS)
 
         def kept(name, shape, dtype):
             return keep.tile(shape, dtype, name=name, align_bytes=64)
 
         def placed(name, shape, dtype, kib):
-            return late.tile(shape, dtype, name=name, align_bytes=64, offset=int(kib * KB))
+            return shared.tile(shape, dtype, name=name, align_bytes=64, offset=int(kib * KB))
 
-        offsets = kept("offsets", [P, N // 16], U16)
+        kw_win = placed("kw_win", [P, T], I32, 0)
+        og_sb = placed("og_sb", [P, 2, DV], F32, 0)
+        v0_raw = [kept("v0_raw0", [P, CUTS[1]], F32), placed("v0_raw1", [P, CUTS[1]], F32, 8), placed("v0_raw2", [P, PASS], F32, 13.5)]
+        pos_col = [kept("pos_col0", [P, WORD], F32), placed("pos_col1", [P, WORD], F32, 8)]
+        pos_wide = [placed("pos_wide0", [P, PASS], F32, 12), placed("pos_wide1", [P, PASS], F32, 14.5)]
+        slope_col = placed("slope_col", [P, 2], F32, 14)
+        s_sb = [kept("s_sb0", [P, N], F32), placed("s_sb1", [P, N], F32, 18)]
+        gate_tanh = placed("gate_tanh", [P, 2, DV], F32, 20)
+        p_sb = {(h, g): placed(f"p_sb{h}{g}", [P, WORD, P], F32, 22 + 4 * h + 2 * g) for h in range(2) for g in range(2)}
+        v_codes = [placed("v_codes0", [P, 2, P], U32, 14.5), placed("v_codes1", [P, 2, P], U32, 24)]
+        inv = placed("inv", [P, 2], F32, 26)
+        vs_col = [kept("vs_col0", [P, WORD], F32), placed("vs_col1", [P, WORD], F32, 30)]
+        res = [placed("res0", [P, DV], F32, 30), kept("res1", [P, P], F32), kept("res2", [P, P], F32)]
+
+        offsets = kept("offsets", [P, N // LANES], U16)
         ident = kept("ident", [P, P], F32)
-        warm = placed("warm", [P, 1], F32, 80)
-        v0_raw = [kept("v0_raw0", [P, 768], F32), placed("v0_raw1", [P, 768], F32, 16), placed("v0_raw2", [P, 512], F32, 33)]
-        pos_col = [kept("pos_col0", [P, 4], F32), placed("pos_col1", [P, 4], F32, 16)]
         slope_rows = kept("slope_rows", [P, P], F32)
-        slope_col = placed("slope_col", [P, 2], F32, 33.5)
-        kw_win = placed("kw_win", [P, T], I32, 4)
-        q_raw = placed("q_raw", [P, 4, NQ], F32, 12)
-        ks_win = placed("ks_win", [P, T], U8, 63)
-        pos_win = placed("pos_win", [P, T], F32, 20)
+        q_raw = kept("q_raw", [P, WORD, NQ], F32)
+        ks_win = kept("ks_win", [P, T], U8)
+        pos_win = kept("pos_win", [P, T], F32)
+        vs_win = kept("vs_win", [P, T], F32)
         v1_raw = kept("v1_raw", [P, T], F32)
-        og_sb = placed("og_sb", [P, 2, DV], F32, 4)
-        pos_g = [kept("pos_g0", [P, PASS], F32), kept("pos_g1", [P, PASS], F32)]
+        v_cast = [kept("v_cast0", [P, T], BF16), kept("v_cast1", [P, LATE], BF16)]
+        pos_g = [kept(f"pos_g{g}", [P, PASS], F32) for g in range(2)]
         ks_g = kept("ks_g", [P, N], U8)
-        pos_wide = [placed("pos_wide0", [P, PASS], F32, 31.5), placed("pos_wide1", [P, PASS], F32, 34)]
         vs_g = kept("vs_g", [P, N], F32)
-        s_sb = [placed(f"s_sb{h}", [P, N], F32, 36 + 4 * h) for h in range(2)]
-        v_cast1 = kept("v_cast1", [P, LATE], BF16)
-        v_bf = [kept(f"v_bf{f}", [P, 2, P, 4], BF16) for f in range(2)]
-        gate_tanh = placed("gate_tanh", [P, 2, DV], F32, 42)
-        p_sb = {(h, g): placed(f"p_sb{h}{g}", [P, 4, P], F32, 64 + 4 * h + 2 * g) for h in range(2) for g in range(2)}
-        vs_win = placed("vs_win", [P, T], F32, 80)
-        v_cast0 = kept("v_cast0", [P, T], BF16)
-        v_g00 = kept("v_g00", [P, PASS], BF16)
-        v_g01 = kept("v_g01", [P, PASS], BF16)
-        v_g10 = kept("v_g10", [P, PASS], BF16)
-        v_g11 = kept("v_g11", [P, PASS], BF16)
         kw_g = kept("kw_g", [P, N], U32)
-        vs_col = [kept("vs_col0", [P, 4], F32), placed("vs_col1", [P, 4], F32, 90)]
-        q_bf = kept("q_bf", [P, NQ, 4], BF16)
+        v_g = {(f, g): kept(f"v_g{f}{g}", [P, PASS], BF16) for f in range(2) for g in range(2)}
+        v_bf = [kept(f"v_bf{f}", [P, 2, P, WORD], BF16) for f in range(2)]
+        v_scales = [kept(f"v_scales{f}", [P, 2, P], U8) for f in range(2)]
+        q_bf = kept("q_bf", [P, NQ, WORD], BF16)
         q_codes = kept("q_codes", [P, NQ], U32)
         q_scales = kept("q_scales", [P, NQ], U8)
         neg_max = [kept(f"neg_max{h}", [P, 1], F32) for h in range(2)]
-        v_codes = [placed("v_codes0", [P, 2, P], U32, 34), placed("v_codes1", [P, 2, P], U32, 66)]
-        v_scales = [kept(f"v_scales{f}", [P, 2, P], U8) for f in range(2)]
-        gate = kept("gate", [P, 2, DV], F32)
-        w_bf = [kept(f"w_bf{h}", [P, 2, P, 4], BF16) for h in range(2)]
+        w_bf = [kept(f"w_bf{h}", [P, 2, P, WORD], BF16) for h in range(2)]
         w_codes = [kept(f"w_codes{h}", [P, 2, P], U32) for h in range(2)]
         w_scales = [kept(f"w_scales{h}", [P, 2, P], U8) for h in range(2)]
         half_sum = kept("half_sum", [P, 2, 2], F32)
         total = kept("total", [P, 2], F32)
-        inv = placed("inv", [P, 2], F32, 68)
-        res = [placed("res0", [P, DV], F32, 90), kept("res1", [P, P], F32), kept("res2", [P, P], F32)]
-        v_g = {(0, 0): v_g00, (0, 1): v_g01, (1, 0): v_g10, (1, 1): v_g11}
+        gate = kept("gate", [P, 2, DV], F32)
         bank = {}
 
         def new_bank(key, shape):
             bank[key] = psum.tile(shape, F32, name=key, tag=f"bank{BANK_OF[key]}")
             return bank[key]
 
-        def half_list(g):
-            return offsets[:, 32 * g : 32 * (g + 1)]
+        def block(index):
+            return slice(index * P, (index + 1) * P)
 
-        def tokens(half):
-            return slice(half * T // 2, (half + 1) * T // 2)
+        def slots(g):
+            return slice(g * PASS, (g + 1) * PASS)
+
+        def entries(first, end):
+            return offsets[:, first // LANES : end // LANES]
+
+        def half_list(g):
+            return entries(g * PASS, (g + 1) * PASS)
+
+        def piece(part):
+            return slice(CUTS[part], CUTS[part + 1])
 
         def load_scales():
             ks_hbm = k_scales[0].bitcast(I32)
             for quad in range(4):
-                nc.scalar.dma_start(out=ks_win[32 * quad : 32 * quad + 4, :].bitcast(I32), in_=ks_hbm[4 * quad : 4 * quad + 4, :])
+                nc.sync.dma_start(out=ks_win[32 * quad : 32 * quad + 4, :].bitcast(I32), in_=ks_hbm[4 * quad : 4 * quad + 4, :])
+
+        def load_keys(columns):
+            nc.sync.dma_start(out=kw_win[:, columns], in_=k_words[0].rearrange("p t r -> p (t r)").bitcast(I32)[:, columns])
+
+        def load_v0(part):
+            nc.sync.dma_start(out=v0_raw[part][:], in_=vT[block(0), piece(part)])
 
         def load_v1(part):
-            nc.sync.dma_start(out=v1_raw[:, V1_CUTS[part] : V1_CUTS[part + 1]], in_=vT[P : 2 * P, V1_CUTS[part] : V1_CUTS[part + 1]])
+            nc.sync.dma_start(out=v1_raw[:, piece(part)], in_=vT[block(1), piece(part)])
 
-        def load_vs():
-            nc.gpsimd.memset(vs_win[0 : P - 1, :], 0.0)
-            nc.sync.dma_start(out=vs_win[P - 1 : P, :], in_=vs[0:1, :])
-
-        def load_keys(part):
-            cut = (0, PREFIX, T)
-            nc.sync.dma_start(out=kw_win[:, cut[part] : cut[part + 1]], in_=k_words[0].rearrange("p t r -> p (t r)").bitcast(I32)[:, cut[part] : cut[part + 1]])
-
-        def load_q():
-            nc.sync.dma_start(out=q_raw[:], in_=qT[0].rearrange("(p j) w -> p j w", j=4))
-
-        def load_slope():
-            nc.sync.dma_start(out=slope_rows[P - 2 : P, :], in_=slope[0].rearrange("(h p) o -> h (p o)", p=P))
-
-        def load_pos():
-            nc.sync.dma_start(out=pos_win[P - 1 : P, :], in_=pos[0:1, :])
-
-        def load_og():
-            nc.sync.dma_start(out=og_sb[:], in_=og[0].rearrange("(h p) e -> p h e", p=P))
-
-        def gather_scales():
-            nc.vector.tensor_copy(ks_g[:], ks_win[:].indirect(offsets[:]))
+        def deal_vs(g):
+            nc.sync.dma_start(out=vs_col[g][:], in_=vs_g[P - 1 : P, slots(g)])
 
         def gather_pos(g):
             nc.vector.tensor_copy(pos_g[g][:], pos_win[:].indirect(half_list(g)))
 
-        def gather_vs():
-            nc.vector.tensor_copy(vs_g[:], vs_win[:].indirect(offsets[:]))
-
-        def gather_keys(g):
-            window = kw_win[:, 0 : (PREFIX, T)[g]]
-            nc.vector.tensor_copy(kw_g[:, slots(g)], window.bitcast(U32).indirect(half_list(g)))
-
-        def turn_slope():
-            ps = new_bank("slope_ps", [P, P])
-            nc.tensor.transpose(ps[:], slope_rows[:], ident[:])
-
-        def pick_slope():
-            nc.scalar.copy(out=slope_col[:], in_=bank["slope_ps"][:, P - 2 : P])
-
-        def turn_pos_only(g):
-            ps = new_bank(f"pos_ps{g}", [P, 4, P])
-            for j in range(4):
-                nc.tensor.transpose(ps[:, j, :], pos_g[g][:, j * P : (j + 1) * P], ident[:])
-
-        def pick_pos(g):
-            nc.scalar.copy(out=pos_col[g][:], in_=bank[f"pos_ps{g}"][:, :, P - 1])
+        def turn_pos(g):
+            ps = new_bank(f"pos_ps{g}", [P, WORD, P])
+            for j in range(WORD):
+                nc.tensor.transpose(ps[:, j, :], pos_g[g][:, block(j)], ident[:])
 
         def spread_pos(g):
-            ps = new_bank(f"wide_ps{g}", [P, 4, P])
-            for j in range(4):
+            nc.scalar.copy(out=pos_col[g][:], in_=bank[f"pos_ps{g}"][:, :, P - 1])
+            ps = new_bank(f"wide_ps{g}", [P, WORD, P])
+            for j in range(WORD):
                 nc.tensor.transpose(ps[:, j, :], pos_col[g][:, j : j + 1].to_broadcast([P, P]), ident[:])
 
         def store_pos(g):
             nc.scalar.copy(out=pos_wide[g][:], in_=bank[f"wide_ps{g}"][:].rearrange("p j s -> p (j s)"))
 
-        def cast_q():
-            nc.gpsimd.tensor_scalar(q_bf[:, 0:P, :], q_raw[:, :, 0:P].rearrange("p j w -> p w j"), 1.0, 0.0, ALU.mult, ALU.add)
-
-        def cast_q_rest():
-            nc.scalar.activation(out=q_bf[:, P:NQ, :], in_=q_raw[:, :, P:NQ].rearrange("p j w -> p w j"), func=ACT.Copy)
-
-        def quantize_q():
-            nc.vector.quantize_mx(out=q_codes[:].bitcast(FP8X4), scales=q_scales[:], in_=q_bf[:].rearrange("p w j -> p (w j)"))
-
         def scores(h, g):
-            qs = slice(h * P, (h + 1) * P)
-            ps = new_bank(f"a_ps{h}{g}", [P, PASS])
-            nc.tensor.matmul_mx(out=ps[:], lhsT=q_codes[:, qs].bitcast(FP8X4), lhsT_scale=q_scales[:, qs],
+            nc.tensor.matmul_mx(out=new_bank(f"a_ps{h}{g}", [P, PASS])[:], lhsT=q_codes[:, block(h)].bitcast(FP8X4), lhsT_scale=q_scales[:, block(h)],
                                 rhs=kw_g[:, slots(g)].bitcast(FP8X4), rhs_scale=ks_g[:, slots(g)], start=True, stop=True)
 
         def add_bias(h, g):
@@ -189,48 +155,38 @@ def tile_attend_soft_alibi_gate_srtq256n1024t2048_kernel(tc, qT, k_words, k_scal
         def row_max(h):
             nc.vector.tensor_reduce(out=neg_max[h][:], in_=s_sb[h][:], axis=AX.X, op=ALU.max, negate=True)
 
-        def exp_half(h, g):
-            nc.scalar.activation(out=p_sb[h, g][:].rearrange("p t s -> p s t"), in_=s_sb[h][:, slots(g)].rearrange("p (s t) -> p s t", t=4),
+        def exp_and_turn(h, g):
+            nc.scalar.activation(out=p_sb[h, g][:].rearrange("p t s -> p s t"), in_=s_sb[h][:, slots(g)].rearrange("p (s t) -> p s t", t=WORD),
                                  func=ACT.Exp, bias=neg_max[h][:], accum_out=half_sum[:, h, g : g + 1])
+            ps = new_bank(f"pt_ps{h}{g}", [P, WORD, P])
+            for t in range(WORD):
+                nc.tensor.transpose(ps[:, t, :], p_sb[h, g][:, t, :], ident[:])
 
-        def join_sums(h):
-            nc.scalar.activation(out=total[:, h : h + 1], in_=half_sum[:, h, 0:1], func=ACT.Identity, bias=half_sum[:, h, 1:2])
+        def weigh(h, g):
+            nc.vector.tensor_tensor(w_bf[h][:, g, :, :], bank[f"pt_ps{h}{g}"][:].rearrange("p t q -> p q t"),
+                                    vs_col[g][:].unsqueeze(1).to_broadcast([P, P, WORD]), ALU.mult)
 
-        def deal_vs(g):
-            nc.sync.dma_start(out=vs_col[g][:], in_=vs_g[P - 1 : P, slots(g)])
+        def quantize_w(h, halves):
+            nc.vector.quantize_mx(out=w_codes[h][:, halves, :].rearrange("p g q -> p (g q)").bitcast(FP8X4),
+                                  scales=w_scales[h][:, halves, :].rearrange("p g q -> p (g q)"),
+                                  in_=w_bf[h][:, halves, :, :].rearrange("p g q t -> p (g q t)"))
 
         def cast_v0(part):
-            a, b = V0_CUTS[part], V0_CUTS[part + 1]
-            nc.scalar.activation(out=v_cast0[:, a:b], in_=v0_raw[part][:], func=ACT.Copy)
+            nc.scalar.activation(out=v_cast[0][:, piece(part)], in_=v0_raw[part][:], func=ACT.Copy)
 
-        def load_v0(part):
-            nc.sync.dma_start(out=v0_raw[part][:], in_=vT[0:P, V0_CUTS[part] : V0_CUTS[part + 1]])
+        def cast_v1(columns):
+            nc.scalar.activation(out=v_cast[1][:, columns], in_=v1_raw[:, columns], func=ACT.Copy)
 
-        def cast_v1(part):
-            a, b = V1_CUTS[part], V1_CUTS[part + 1]
-            nc.scalar.activation(out=v_cast1[:, a:b], in_=v1_raw[:, a:b], func=ACT.Copy)
+        def gather_first_half(f):
+            nc.scalar.activation(out=v_g[f, 0][:].rearrange("p (u s e) -> p s u e", u=2, e=2),
+                                 in_=v_cast[f][:, 0:PREFIX].indirect(half_list(0)), func=ACT.Copy)
 
-        def gather_first_v(f):
-            window = (v_cast0, v_cast1)[f][:, 0:PREFIX]
-            nc.scalar.activation(out=v_g[f, 0][:].rearrange("p (u s e) -> p s u e", u=2, e=2), in_=window.indirect(half_list(0)), func=ACT.Copy)
-
-        def gather_v01():
-            nc.scalar.activation(out=v_g[0, 1][:], in_=v_cast0[:].indirect(half_list(1)), func=ACT.Copy)
-
-        def cast_v1_end():
-            nc.scalar.activation(out=v_cast1[:, PREFIX:LATE], in_=v1_raw[:, PREFIX:LATE], func=ACT.Copy)
-
-        def gather_v11_first():
-            nc.scalar.activation(out=v_g[1, 1][:, 0 : PASS - SHARE], in_=v_cast1[:].indirect(offsets[:, 32 : 64 - SHARE // 16]), func=ACT.Copy)
-
-        def gather_v11_last():
-            nc.vector.tensor_copy(v_g[1, 1][:, PASS - SHARE : PASS], v1_raw[:].indirect(offsets[:, 64 - SHARE // 16 : 64]))
-
-        def turn_v(f, g):
-            pairs = v_g[f, g][:].bitcast(F32)
-            ps = bank[f"vt_ps{f}"] if g else new_bank(f"vt_ps{f}", [P, 2, 2, P])
-            for u in range(2):
-                nc.tensor.transpose(ps[:, g, u, :], pairs[:, u : 2 * P : 2] if g else pairs[:, u * P : (u + 1) * P], ident[:])
+        def turn_v(f):
+            ps = new_bank(f"vt_ps{f}", [P, 2, 2, P])
+            for g in range(2):
+                pairs = v_g[f, g][:].bitcast(F32)
+                for u in range(2):
+                    nc.tensor.transpose(ps[:, g, u, :], pairs[:, u : 2 * P : 2] if g else pairs[:, block(u)], ident[:])
 
         def store_v(f):
             nc.scalar.copy(out=v_bf[f][:].rearrange("p g c t -> p (g c t)").bitcast(F32).rearrange("p (g c u) -> p g c u", g=2, u=2),
@@ -240,138 +196,103 @@ def tile_attend_soft_alibi_gate_srtq256n1024t2048_kernel(tc, qT, k_words, k_scal
             nc.vector.quantize_mx(out=v_codes[f][:].rearrange("p g c -> p (g c)").bitcast(FP8X4), scales=v_scales[f][:].rearrange("p g c -> p (g c)"),
                                   in_=v_bf[f][:].rearrange("p g c t -> p (g c t)"))
 
-        def make_tanh():
-            nc.scalar.activation(out=gate_tanh[:], in_=og_sb[:], func=ACT.Tanh, scale=0.5)
-
-        def make_gate():
-            nc.scalar.activation(out=gate[:], in_=gate_tanh[:], func=ACT.Copy, scale=0.5, bias=0.5)
-
-        def turn_p(h, g):
-            ps = new_bank(f"pt_ps{h}{g}", [P, 4, P])
-            for t in range(4):
-                nc.tensor.transpose(ps[:, t, :], p_sb[h, g][:, t, :], ident[:])
-
-        def weigh(h, g):
-            nc.vector.tensor_tensor(w_bf[h][:, g, :, :], bank[f"pt_ps{h}{g}"][:].rearrange("p t q -> p q t"),
-                                    vs_col[g][:].unsqueeze(1).to_broadcast([P, P, 4]), ALU.mult)
-
-        def quantize_w(h, first, last):
-            passes = slice(first, last + 1)
-            nc.vector.quantize_mx(out=w_codes[h][:, passes, :].rearrange("p g q -> p (g q)").bitcast(FP8X4),
-                                  scales=w_scales[h][:, passes, :].rearrange("p g q -> p (g q)"),
-                                  in_=w_bf[h][:, passes, :, :].rearrange("p g q t -> p (g q t)"))
-
-        def invert():
-            nc.vector.reciprocal(inv[:], total[:])
-
-        def product(piece, h, f, g, columns):
-            nc.tensor.matmul_mx(out=bank[f"y_ps{piece}"][:, columns], lhsT=w_codes[h][:, g, :].bitcast(FP8X4), lhsT_scale=w_scales[h][:, g, :],
+        def product(y_ps, h, f, g):
+            nc.tensor.matmul_mx(out=y_ps, lhsT=w_codes[h][:, g, :].bitcast(FP8X4), lhsT_scale=w_scales[h][:, g, :],
                                 rhs=v_codes[f][:, g, :].bitcast(FP8X4), rhs_scale=v_scales[f][:, g, :], start=(g == 0), stop=(g == 1))
 
-        def finish(h, piece, features):
-            nc.vector.scalar_tensor_tensor(out=res[piece][:], in0=bank[f"y_ps{piece}"][:], scalar=inv[:, h : h + 1], in1=gate[:, h, features], op0=ALU.mult, op1=ALU.mult)
-            nc.sync.dma_start(out=out[0, h * P : (h + 1) * P, features], in_=res[piece][:])
+        def finish(y_ps, result, h, features):
+            nc.vector.scalar_tensor_tensor(out=result[:], in0=y_ps[:], scalar=inv[:, h : h + 1], in1=gate[:, h, features], op0=ALU.mult, op1=ALU.mult)
+            nc.sync.dma_start(out=out[0, block(h), features], in_=result[:])
 
-        nc.vector.memset(ks_win[:].bitcast(I32), 0)
         nc.vector.memset(pos_win[0 : P - 1, :], 0.0)
         nc.vector.memset(slope_rows[0 : P - 2, :], 0.0)
         make_identity(nc, ident[:])
+        nc.gpsimd.memset(ks_win[:].bitcast(I32), 0)
+        nc.gpsimd.memset(vs_win[0 : P - 1, :], 0.0)
+
         nc.sync.dma_start(offsets[:], offs)
-        load_pos()
-        load_scales()
-        nc.scalar.activation(out=warm[32:64, :], in_=pos_win[32:64, 0:1], func=ACT.Exp)
+        nc.sync.dma_start(out=pos_win[P - 1 : P, :], in_=pos[0:1, :])
         load_v0(0)
         load_v0(1)
-        load_q()
-        load_vs()
-        load_slope()
+        load_scales()
+        nc.sync.dma_start(out=vs_win[P - 1 : P, :], in_=vs[0:1, :])
+        nc.sync.dma_start(out=q_raw[:], in_=qT[0].rearrange("(p j) w -> p j w", j=WORD))
         load_v0(2)
-        gather_pos(0)
-        gather_pos(1)
-        turn_pos_only(0)
-        turn_pos_only(1)
-        load_keys(0)
-        load_keys(1)
-        load_v1(0)
-        load_v1(1)
-        load_v1(2)
-        gather_scales()
-        gather_vs()
+        nc.sync.dma_start(out=slope_rows[P - 2 : P, :], in_=slope[0].rearrange("(h p) o -> h (p o)", p=P))
+        load_keys(slice(0, PREFIX))
+        load_keys(slice(PREFIX, T))
+        for part in range(3):
+            load_v1(part)
+
+        for g in range(2):
+            gather_pos(g)
+        for g in range(2):
+            turn_pos(g)
+        nc.vector.tensor_copy(ks_g[:], ks_win[:].indirect(offsets[:]))
+        nc.vector.tensor_copy(vs_g[:], vs_win[:].indirect(offsets[:]))
         cast_v0(0)
-        cast_q()
+        nc.gpsimd.tensor_scalar(q_bf[:, block(0), :], q_raw[:, :, block(0)].rearrange("p j w -> p w j"), 1.0, 0.0, ALU.mult, ALU.add)
         cast_v0(1)
-        gather_first_v(0)
-        pick_pos(0)
-        spread_pos(0)
-        pick_pos(1)
-        spread_pos(1)
-        cast_q_rest()
-        quantize_q()
-        gather_keys(0)
-        gather_keys(1)
+        gather_first_half(0)
+        for g in range(2):
+            spread_pos(g)
+        nc.scalar.activation(out=q_bf[:, block(1), :], in_=q_raw[:, :, block(1)].rearrange("p j w -> p w j"), func=ACT.Copy)
+        nc.vector.quantize_mx(out=q_codes[:].bitcast(FP8X4), scales=q_scales[:], in_=q_bf[:].rearrange("p w j -> p (w j)"))
+        for g, end in enumerate((PREFIX, T)):
+            nc.vector.tensor_copy(kw_g[:, slots(g)], kw_win[:, 0:end].bitcast(U32).indirect(half_list(g)))
         deal_vs(0)
-        load_og()
+        nc.sync.dma_start(out=og_sb[:], in_=og[0].rearrange("(h p) e -> p h e", p=P))
         deal_vs(1)
         cast_v0(2)
-        turn_slope()
-        gather_v01()
-        pick_slope()
-        store_pos(0)
-        store_pos(1)
-        turn_v(0, 0)
-        turn_v(0, 1)
+        nc.tensor.transpose(new_bank("slope_ps", [P, P])[:], slope_rows[:], ident[:])
+        nc.scalar.activation(out=v_g[0, 1][:], in_=v_cast[0][:].indirect(half_list(1)), func=ACT.Copy)
+        nc.scalar.copy(out=slope_col[:], in_=bank["slope_ps"][:, P - 2 : P])
+        for g in range(2):
+            store_pos(g)
+        turn_v(0)
         store_v(0)
-        scores(0, 0)
-        scores(1, 0)
-        scores(0, 1)
-        scores(1, 1)
-        add_bias(0, 0)
-        add_bias(1, 0)
-        add_bias(0, 1)
-        add_bias(1, 1)
+
+        for g in range(2):
+            for h in range(2):
+                scores(h, g)
+        for g in range(2):
+            for h in range(2):
+                add_bias(h, g)
         row_max(0)
-        gather_v11_last()
-        cast_v1(0)
-        cast_v1(1)
-        cast_v1_end()
-        gather_first_v(1)
-        gather_v11_first()
+        nc.vector.tensor_copy(v_g[1, 1][:, PASS - SHARE : PASS], v1_raw[:].indirect(entries(N - SHARE, N)))
+        for columns in (piece(0), piece(1), slice(PREFIX, LATE)):
+            cast_v1(columns)
+        gather_first_half(1)
+        nc.scalar.activation(out=v_g[1, 1][:, 0 : PASS - SHARE], in_=v_cast[1][:].indirect(entries(PASS, N - SHARE)), func=ACT.Copy)
         row_max(1)
         quantize_v(0)
-        turn_v(1, 0)
-        turn_v(1, 1)
-        exp_half(0, 0)
-        turn_p(0, 0)
-        exp_half(0, 1)
-        turn_p(0, 1)
+        turn_v(1)
+        exp_and_turn(0, 0)
+        exp_and_turn(0, 1)
         store_v(1)
-        exp_half(1, 0)
-        turn_p(1, 0)
-        exp_half(1, 1)
-        turn_p(1, 1)
-        join_sums(0)
-        join_sums(1)
-        make_tanh()
-        make_gate()
+        exp_and_turn(1, 0)
+        exp_and_turn(1, 1)
+        for h in range(2):
+            nc.scalar.activation(out=total[:, h : h + 1], in_=half_sum[:, h, 0:1], func=ACT.Identity, bias=half_sum[:, h, 1:2])
+        nc.scalar.activation(out=gate_tanh[:], in_=og_sb[:], func=ACT.Tanh, scale=0.5)
+        nc.scalar.activation(out=gate[:], in_=gate_tanh[:], func=ACT.Copy, scale=0.5, bias=0.5)
+
         weigh(0, 0)
         weigh(0, 1)
         quantize_v(1)
-        quantize_w(0, 0, 1)
+        quantize_w(0, slice(0, 2))
         weigh(1, 0)
-        invert()
+        nc.vector.reciprocal(inv[:], total[:])
         weigh(1, 1)
-        new_bank("y_ps0", [P, DV])
+        y_first = new_bank("y_ps0", [P, DV])
         for f in range(2):
             for g in range(2):
-                product(0, 0, f, g, slice(f * P, (f + 1) * P))
-        quantize_w(1, 0, 0)
-        new_bank("y_ps1", [P, P])
-        new_bank("y_ps2", [P, P])
-        product(1, 1, 0, 0, slice(0, P))
-        product(2, 1, 1, 0, slice(0, P))
-        quantize_w(1, 1, 1)
-        product(1, 1, 0, 1, slice(0, P))
-        product(2, 1, 1, 1, slice(0, P))
-        finish(0, 0, slice(0, DV))
-        finish(1, 1, slice(0, P))
-        finish(1, 2, slice(P, DV))
+                product(y_first[:, block(f)], 0, f, g)
+        y_last = [new_bank(f"y_ps{1 + f}", [P, P]) for f in range(2)]
+        for g in range(2):
+            quantize_w(1, slice(g, g + 1))
+            for f in range(2):
+                product(y_last[f][:], 1, f, g)
+        finish(y_first, res[0], 0, slice(0, DV))
+        for f in range(2):
+            finish(y_last[f], res[1 + f], 1, block(f))

@@ -23,17 +23,15 @@ WORD = 4
 LANES = 16
 KB = 1024
 PREFIX = T - PASS
-CUTS = (0, PREFIX // 2, PREFIX, T)
-SHARE = 128
-LATE = T - SHARE
-BANK_OF = {"pos_ps0": 0, "vt_ps0": 0, "y_ps2": 0,
-           "pos_ps1": 1, "vt_ps1": 1,
-           "a_ps00": 2, "y_ps0": 2,
-           "a_ps01": 3, "y_ps1": 3,
-           "wide_ps0": 4, "pt_ps00": 4,
-           "wide_ps1": 5, "pt_ps01": 5,
-           "slope_ps": 6, "a_ps10": 6, "pt_ps10": 6,
-           "a_ps11": 7, "pt_ps11": 7}
+QUARTER = N // 4
+BANK_OF = {"pos_ps0": 0, "pt_ps00": 0, "y_ps2": 0,
+           "pos_ps1": 1, "pt_ps01": 1,
+           "a_ps00": 2, "vt_ps0": 2,
+           "a_ps01": 3, "y_ps0": 3,
+           "wide_ps0": 4, "pt_ps10": 4,
+           "wide_ps1": 5, "pt_ps11": 5,
+           "slope_ps": 6, "a_ps10": 6, "vt_ps1": 6,
+           "a_ps11": 7, "y_ps1": 7}
 
 
 def tile_attend_soft_alibi_gate_srtq256n1024t2048_kernel(tc, qT, k_words, k_scales, vT, vs, pos, slope, og, offs, out):
@@ -51,35 +49,35 @@ def tile_attend_soft_alibi_gate_srtq256n1024t2048_kernel(tc, qT, k_words, k_scal
 
         kw_win = placed("kw_win", [P, T], I32, 0)
         og_sb = placed("og_sb", [P, 2, DV], F32, 0)
-        v0_raw = [kept("v0_raw0", [P, CUTS[1]], F32), placed("v0_raw1", [P, CUTS[1]], F32, 8), placed("v0_raw2", [P, PASS], F32, 13.5)]
-        pos_col = [kept("pos_col0", [P, WORD], F32), placed("pos_col1", [P, WORD], F32, 8)]
-        pos_wide = [placed("pos_wide0", [P, PASS], F32, 12), placed("pos_wide1", [P, PASS], F32, 14.5)]
-        slope_col = placed("slope_col", [P, 2], F32, 14)
-        s_sb = [kept("s_sb0", [P, N], F32), placed("s_sb1", [P, N], F32, 18)]
-        gate_tanh = placed("gate_tanh", [P, 2, DV], F32, 20)
+        q_raw = placed("q_raw", [P, WORD, NQ], F32, 8)
+        kw_g = [kept("kw_g0", [P, PASS], U32), placed("kw_g1", [P, PASS], U32, 8)]
+        pos_g = [kept("pos_g0", [P, PASS], F32), placed("pos_g1", [P, PASS], F32, 12)]
+        vs_g = [kept("vs_g0", [P, PASS], F32), placed("vs_g1", [P, PASS], F32, 12)]
+        q_bf = kept("q_bf", [P, NQ, WORD], BF16)
+        pos_col = [placed(f"pos_col{g}", [P, WORD], F32, 16 + 2 * g) for g in range(2)]
+        pos_wide = [kept("pos_wide0", [P, PASS], F32), placed("pos_wide1", [P, PASS], F32, 14)]
         p_sb = {(h, g): placed(f"p_sb{h}{g}", [P, WORD, P], F32, 22 + 4 * h + 2 * g) for h in range(2) for g in range(2)}
-        v_codes = [placed("v_codes0", [P, 2, P], U32, 14.5), placed("v_codes1", [P, 2, P], U32, 24)]
-        inv = placed("inv", [P, 2], F32, 26)
-        vs_col = [kept("vs_col0", [P, WORD], F32), placed("vs_col1", [P, WORD], F32, 30)]
-        res = [placed("res0", [P, DV], F32, 30), kept("res1", [P, P], F32), kept("res2", [P, P], F32)]
+        v_first = placed("v_first", [P, 2, PASS], BF16, 18)
+        v_g = {(0, 0): v_first[:, 0, :], (0, 1): v_first[:, 1, :],
+               (1, 0): placed("v_g10", [P, PASS], BF16, 14)[:], (1, 1): placed("v_g11", [P, PASS], BF16, 15)[:]}
+        v_bf = [placed("v_bf0", [P, 2, P, WORD], BF16, 22), placed("v_bf1", [P, 2, P, WORD], BF16, 26)]
+        gate_tanh = placed("gate_tanh", [P, 2, DV], F32, 28)
+        vs_col = [placed(f"vs_col{g}", [P, WORD], F32, 4 + g) for g in range(2)]
+        res = [placed("res0", [P, DV], F32, 5), kept("res1", [P, P], F32), kept("res2", [P, P], F32)]
 
+        v_raw = [kept(f"v_raw{f}", [P, T], F32) for f in range(2)]
+        s_sb = [kept(f"s_sb{h}", [P, N], F32) for h in range(2)]
+        inv = kept("inv", [P, 2], F32)
         offsets = kept("offsets", [P, N // LANES], U16)
         ident = kept("ident", [P, P], F32)
         slope_rows = kept("slope_rows", [P, P], F32)
-        q_raw = kept("q_raw", [P, WORD, NQ], F32)
         ks_win = kept("ks_win", [P, T], U8)
         pos_win = kept("pos_win", [P, T], F32)
         vs_win = kept("vs_win", [P, T], F32)
-        v1_raw = kept("v1_raw", [P, T], F32)
-        v_cast = [kept("v_cast0", [P, T], BF16), kept("v_cast1", [P, LATE], BF16)]
-        pos_g = [kept(f"pos_g{g}", [P, PASS], F32) for g in range(2)]
+        slope_col = kept("slope_col", [P, 2], F32)
+        v_codes = [kept(f"v_codes{f}", [P, 2, P], U32) for f in range(2)]
         ks_g = kept("ks_g", [P, N], U8)
-        vs_g = kept("vs_g", [P, N], F32)
-        kw_g = kept("kw_g", [P, N], U32)
-        v_g = {(f, g): kept(f"v_g{f}{g}", [P, PASS], BF16) for f in range(2) for g in range(2)}
-        v_bf = [kept(f"v_bf{f}", [P, 2, P, WORD], BF16) for f in range(2)]
         v_scales = [kept(f"v_scales{f}", [P, 2, P], U8) for f in range(2)]
-        q_bf = kept("q_bf", [P, NQ, WORD], BF16)
         q_codes = kept("q_codes", [P, NQ], U32)
         q_scales = kept("q_scales", [P, NQ], U8)
         neg_max = [kept(f"neg_max{h}", [P, 1], F32) for h in range(2)]
@@ -107,28 +105,29 @@ def tile_attend_soft_alibi_gate_srtq256n1024t2048_kernel(tc, qT, k_words, k_scal
         def half_list(g):
             return entries(g * PASS, (g + 1) * PASS)
 
-        def piece(part):
-            return slice(CUTS[part], CUTS[part + 1])
-
         def load_scales():
             ks_hbm = k_scales[0].bitcast(I32)
             for quad in range(4):
-                nc.sync.dma_start(out=ks_win[32 * quad : 32 * quad + 4, :].bitcast(I32), in_=ks_hbm[4 * quad : 4 * quad + 4, :])
+                nc.scalar.dma_start(out=ks_win[32 * quad : 32 * quad + 4, :].bitcast(I32), in_=ks_hbm[4 * quad : 4 * quad + 4, :])
 
         def load_keys(columns):
             nc.sync.dma_start(out=kw_win[:, columns], in_=k_words[0].rearrange("p t r -> p (t r)").bitcast(I32)[:, columns])
 
-        def load_v0(part):
-            nc.sync.dma_start(out=v0_raw[part][:], in_=vT[block(0), piece(part)])
+        def gather_keys(g, end):
+            nc.vector.tensor_copy(kw_g[g][:], kw_win[:, 0:end].bitcast(U32).indirect(half_list(g)))
 
-        def load_v1(part):
-            nc.sync.dma_start(out=v1_raw[:, piece(part)], in_=vT[block(1), piece(part)])
+        def gather_vs(quarter):
+            g, first = divmod(quarter * QUARTER, PASS)
+            nc.scalar.activation(out=vs_g[g][:, first : first + QUARTER], in_=vs_win[:].indirect(entries(quarter * QUARTER, (quarter + 1) * QUARTER)), func=ACT.Copy)
+
+        def load_v(f):
+            nc.sync.dma_start(out=v_raw[f][:], in_=vT[block(f), :])
 
         def deal_vs(g):
-            nc.sync.dma_start(out=vs_col[g][:], in_=vs_g[P - 1 : P, slots(g)])
+            nc.sync.dma_start(out=vs_col[g][:], in_=vs_g[g][P - 1 : P, :])
 
         def gather_pos(g):
-            nc.vector.tensor_copy(pos_g[g][:], pos_win[:].indirect(half_list(g)))
+            nc.scalar.activation(out=pos_g[g][:], in_=pos_win[:].indirect(half_list(g)), func=ACT.Copy)
 
         def turn_pos(g):
             ps = new_bank(f"pos_ps{g}", [P, WORD, P])
@@ -146,7 +145,7 @@ def tile_attend_soft_alibi_gate_srtq256n1024t2048_kernel(tc, qT, k_words, k_scal
 
         def scores(h, g):
             nc.tensor.matmul_mx(out=new_bank(f"a_ps{h}{g}", [P, PASS])[:], lhsT=q_codes[:, block(h)].bitcast(FP8X4), lhsT_scale=q_scales[:, block(h)],
-                                rhs=kw_g[:, slots(g)].bitcast(FP8X4), rhs_scale=ks_g[:, slots(g)], start=True, stop=True)
+                                rhs=kw_g[g][:].bitcast(FP8X4), rhs_scale=ks_g[:, slots(g)], start=True, stop=True)
 
         def add_bias(h, g):
             nc.vector.scalar_tensor_tensor(out=s_sb[h][:, slots(g)], in0=pos_wide[g][:], scalar=slope_col[:, h : h + 1],
@@ -171,22 +170,15 @@ def tile_attend_soft_alibi_gate_srtq256n1024t2048_kernel(tc, qT, k_words, k_scal
                                   scales=w_scales[h][:, halves, :].rearrange("p g q -> p (g q)"),
                                   in_=w_bf[h][:, halves, :, :].rearrange("p g q t -> p (g q t)"))
 
-        def cast_v0(part):
-            nc.scalar.activation(out=v_cast[0][:, piece(part)], in_=v0_raw[part][:], func=ACT.Copy)
+        def gather_v(f, g, first):
+            nc.scalar.activation(out=v_g[f, g][:, first:PASS], in_=v_raw[f][:].indirect(entries(g * PASS + first, (g + 1) * PASS)), func=ACT.Copy)
 
-        def cast_v1(columns):
-            nc.scalar.activation(out=v_cast[1][:, columns], in_=v1_raw[:, columns], func=ACT.Copy)
-
-        def gather_first_half(f):
-            nc.scalar.activation(out=v_g[f, 0][:].rearrange("p (u s e) -> p s u e", u=2, e=2),
-                                 in_=v_cast[f][:, 0:PREFIX].indirect(half_list(0)), func=ACT.Copy)
-
-        def turn_v(f):
-            ps = new_bank(f"vt_ps{f}", [P, 2, 2, P])
-            for g in range(2):
-                pairs = v_g[f, g][:].bitcast(F32)
-                for u in range(2):
-                    nc.tensor.transpose(ps[:, g, u, :], pairs[:, u : 2 * P : 2] if g else pairs[:, block(u)], ident[:])
+        def turn_v(f, g):
+            if g == 0:
+                new_bank(f"vt_ps{f}", [P, 2, 2, P])
+            pairs = v_g[f, g].bitcast(F32)
+            for u in range(2):
+                nc.tensor.transpose(bank[f"vt_ps{f}"][:, g, u, :], pairs[:, u : 2 * P : 2], ident[:])
 
         def store_v(f):
             nc.scalar.copy(out=v_bf[f][:].rearrange("p g c t -> p (g c t)").bitcast(F32).rearrange("p (g c u) -> p g c u", g=2, u=2),
@@ -205,73 +197,69 @@ def tile_attend_soft_alibi_gate_srtq256n1024t2048_kernel(tc, qT, k_words, k_scal
             nc.sync.dma_start(out=out[0, block(h), features], in_=result[:])
 
         nc.vector.memset(pos_win[0 : P - 1, :], 0.0)
-        nc.vector.memset(slope_rows[0 : P - 2, :], 0.0)
-        make_identity(nc, ident[:])
         nc.gpsimd.memset(ks_win[:].bitcast(I32), 0)
+        nc.gpsimd.memset(ident[:], 0.0)
+        nc.scalar.activation(out=slope_rows[0 : P - 2, :], in_=ident[0 : P - 2, :], func=ACT.Copy)
         nc.gpsimd.memset(vs_win[0 : P - 1, :], 0.0)
+        make_identity(nc, ident[:], nomemset=True)
 
         nc.sync.dma_start(offsets[:], offs)
         nc.sync.dma_start(out=pos_win[P - 1 : P, :], in_=pos[0:1, :])
-        load_v0(0)
-        load_v0(1)
         load_scales()
         nc.sync.dma_start(out=vs_win[P - 1 : P, :], in_=vs[0:1, :])
         nc.sync.dma_start(out=q_raw[:], in_=qT[0].rearrange("(p j) w -> p j w", j=WORD))
-        load_v0(2)
         nc.sync.dma_start(out=slope_rows[P - 2 : P, :], in_=slope[0].rearrange("(h p) o -> h (p o)", p=P))
         load_keys(slice(0, PREFIX))
         load_keys(slice(PREFIX, T))
-        for part in range(3):
-            load_v1(part)
+        load_v(0)
+        load_v(1)
 
-        for g in range(2):
-            gather_pos(g)
+        nc.vector.tensor_copy(pos_g[0][:], pos_win[:].indirect(half_list(0)))
+        gather_pos(1)
+        nc.vector.tensor_copy(ks_g[:], ks_win[:].indirect(offsets[:]))
+        gather_vs(0)
+        gather_vs(1)
         for g in range(2):
             turn_pos(g)
-        nc.vector.tensor_copy(ks_g[:], ks_win[:].indirect(offsets[:]))
-        nc.vector.tensor_copy(vs_g[:], vs_win[:].indirect(offsets[:]))
-        cast_v0(0)
-        nc.gpsimd.tensor_scalar(q_bf[:, block(0), :], q_raw[:, :, block(0)].rearrange("p j w -> p w j"), 1.0, 0.0, ALU.mult, ALU.add)
-        cast_v0(1)
-        gather_first_half(0)
-        for g in range(2):
-            spread_pos(g)
-        nc.scalar.activation(out=q_bf[:, block(1), :], in_=q_raw[:, :, block(1)].rearrange("p j w -> p w j"), func=ACT.Copy)
-        nc.vector.quantize_mx(out=q_codes[:].bitcast(FP8X4), scales=q_scales[:], in_=q_bf[:].rearrange("p w j -> p (w j)"))
-        for g, end in enumerate((PREFIX, T)):
-            nc.vector.tensor_copy(kw_g[:, slots(g)], kw_win[:, 0:end].bitcast(U32).indirect(half_list(g)))
-        deal_vs(0)
-        nc.sync.dma_start(out=og_sb[:], in_=og[0].rearrange("(h p) e -> p h e", p=P))
-        deal_vs(1)
-        cast_v0(2)
         nc.tensor.transpose(new_bank("slope_ps", [P, P])[:], slope_rows[:], ident[:])
-        nc.scalar.activation(out=v_g[0, 1][:], in_=v_cast[0][:].indirect(half_list(1)), func=ACT.Copy)
+        gather_keys(0, PREFIX)
+        spread_pos(0)
+        spread_pos(1)
         nc.scalar.copy(out=slope_col[:], in_=bank["slope_ps"][:, P - 2 : P])
+        for h in range(2):
+            nc.gpsimd.tensor_scalar(q_bf[:, block(h), :], q_raw[:, :, block(h)].rearrange("p j w -> p w j"), 1.0, 0.0, ALU.mult, ALU.add)
+        nc.vector.quantize_mx(out=q_codes[:].bitcast(FP8X4), scales=q_scales[:], in_=q_bf[:].rearrange("p w j -> p (w j)"))
+        gather_keys(1, T)
+        gather_vs(2)
+        gather_vs(3)
+        store_pos(0)
+        store_pos(1)
         for g in range(2):
-            store_pos(g)
-        turn_v(0)
-        store_v(0)
+            deal_vs(g)
+        nc.sync.dma_start(out=og_sb[:], in_=og[0].rearrange("(h p) e -> p h e", p=P))
 
         for g in range(2):
             for h in range(2):
                 scores(h, g)
         for g in range(2):
-            for h in range(2):
-                add_bias(h, g)
+            gather_v(0, g, 0)
+            turn_v(0, g)
+        add_bias(0, 0)
+        add_bias(1, 0)
+        add_bias(0, 1)
         row_max(0)
-        nc.vector.tensor_copy(v_g[1, 1][:, PASS - SHARE : PASS], v1_raw[:].indirect(entries(N - SHARE, N)))
-        for columns in (piece(0), piece(1), slice(PREFIX, LATE)):
-            cast_v1(columns)
-        gather_first_half(1)
-        nc.scalar.activation(out=v_g[1, 1][:, 0 : PASS - SHARE], in_=v_cast[1][:].indirect(entries(PASS, N - SHARE)), func=ACT.Copy)
+        add_bias(1, 1)
         row_max(1)
-        quantize_v(0)
-        turn_v(1)
+        for g in range(2):
+            nc.vector.tensor_copy(v_g[1, g], v_raw[1][:].indirect(half_list(g)))
         exp_and_turn(0, 0)
         exp_and_turn(0, 1)
-        store_v(1)
+        store_v(0)
+        turn_v(1, 0)
         exp_and_turn(1, 0)
+        turn_v(1, 1)
         exp_and_turn(1, 1)
+        store_v(1)
         for h in range(2):
             nc.scalar.activation(out=total[:, h : h + 1], in_=half_sum[:, h, 0:1], func=ACT.Identity, bias=half_sum[:, h, 1:2])
         nc.scalar.activation(out=gate_tanh[:], in_=og_sb[:], func=ACT.Tanh, scale=0.5)
@@ -279,11 +267,12 @@ def tile_attend_soft_alibi_gate_srtq256n1024t2048_kernel(tc, qT, k_words, k_scal
 
         weigh(0, 0)
         weigh(0, 1)
-        quantize_v(1)
+        quantize_v(0)
         quantize_w(0, slice(0, 2))
         weigh(1, 0)
-        nc.vector.reciprocal(inv[:], total[:])
+        quantize_v(1)
         weigh(1, 1)
+        nc.vector.reciprocal(inv[:], total[:])
         y_first = new_bank("y_ps0", [P, DV])
         for f in range(2):
             for g in range(2):
@@ -294,5 +283,5 @@ def tile_attend_soft_alibi_gate_srtq256n1024t2048_kernel(tc, qT, k_words, k_scal
             for f in range(2):
                 product(y_last[f][:], 1, f, g)
         finish(y_first, res[0], 0, slice(0, DV))
-        for f in range(2):
-            finish(y_last[f], res[1 + f], 1, block(f))
+        finish(y_last[0], res[1], 1, block(0))
+        finish(y_last[1], res[2], 1, block(1))

@@ -51,17 +51,19 @@ def tile_attend_soft_alibi_gate_srtq256n1024t2048_kernel(tc, qT, k_words, k_scal
         og_sb = placed("og_sb", [P, 2, DV], F32, 0)
         q_raw = placed("q_raw", [P, WORD, NQ], F32, 8)
         kw_g = [kept("kw_g0", [P, PASS], U32), placed("kw_g1", [P, PASS], U32, 8)]
-        pos_g = [kept("pos_g0", [P, PASS], F32), placed("pos_g1", [P, PASS], F32, 12)]
-        vs_g = [kept("vs_g0", [P, PASS], F32), placed("vs_g1", [P, PASS], F32, 12)]
+        pos_g = [kept(f"pos_g{g}", [P, PASS], F32) for g in range(2)]
         q_bf = kept("q_bf", [P, NQ, WORD], BF16)
         pos_col = [placed(f"pos_col{g}", [P, WORD], F32, 16 + 2 * g) for g in range(2)]
-        pos_wide = [kept("pos_wide0", [P, PASS], F32), placed("pos_wide1", [P, PASS], F32, 14)]
+        vs_g = [kept("vs_g0", [P, PASS], F32), placed("vs_g1", [P, PASS], F32, 18)]
+        a_sb = kept("a_sb", [P, PASS], F32)
+        bias_sb = kept("bias_sb", [P, PASS], F32)
+        pos_wide = [kept("pos_wide0", [P, PASS], F32), placed("pos_wide1", [P, PASS], F32, 34)]
+        v_g = {(0, 0): placed("v_g00", [P, PASS], BF16, 22)[:], (0, 1): kept("v_g01", [P, PASS], BF16)[:],
+               (1, 0): placed("v_g10", [P, PASS], BF16, 34)[:], (1, 1): placed("v_g11", [P, PASS], BF16, 35)[:]}
         p_sb = {(h, g): placed(f"p_sb{h}{g}", [P, WORD, P], F32, 22 + 4 * h + 2 * g) for h in range(2) for g in range(2)}
-        v_first = placed("v_first", [P, 2, PASS], BF16, 18)
-        v_g = {(0, 0): v_first[:, 0, :], (0, 1): v_first[:, 1, :],
-               (1, 0): placed("v_g10", [P, PASS], BF16, 14)[:], (1, 1): placed("v_g11", [P, PASS], BF16, 15)[:]}
         v_bf = [placed("v_bf0", [P, 2, P, WORD], BF16, 22), placed("v_bf1", [P, 2, P, WORD], BF16, 26)]
         gate_tanh = placed("gate_tanh", [P, 2, DV], F32, 28)
+        total = placed("total", [P, 2], F32, 24)
         vs_col = [placed(f"vs_col{g}", [P, WORD], F32, 4 + g) for g in range(2)]
         res = [placed("res0", [P, DV], F32, 5), kept("res1", [P, P], F32), kept("res2", [P, P], F32)]
 
@@ -85,7 +87,6 @@ def tile_attend_soft_alibi_gate_srtq256n1024t2048_kernel(tc, qT, k_words, k_scal
         w_codes = [kept(f"w_codes{h}", [P, 2, P], U32) for h in range(2)]
         w_scales = [kept(f"w_scales{h}", [P, 2, P], U8) for h in range(2)]
         half_sum = kept("half_sum", [P, 2, 2], F32)
-        total = kept("total", [P, 2], F32)
         gate = kept("gate", [P, 2, DV], F32)
         bank = {}
 
@@ -230,25 +231,27 @@ def tile_attend_soft_alibi_gate_srtq256n1024t2048_kernel(tc, qT, k_words, k_scal
             nc.gpsimd.tensor_scalar(q_bf[:, block(h), :], q_raw[:, :, block(h)].rearrange("p j w -> p w j"), 1.0, 0.0, ALU.mult, ALU.add)
         nc.vector.quantize_mx(out=q_codes[:].bitcast(FP8X4), scales=q_scales[:], in_=q_bf[:].rearrange("p w j -> p (w j)"))
         gather_keys(1, T)
-        gather_vs(2)
-        gather_vs(3)
+        nc.vector.tensor_copy(vs_g[1][:, 0:QUARTER], vs_win[:].indirect(entries(PASS, PASS + QUARTER)))
         store_pos(0)
         store_pos(1)
-        for g in range(2):
-            deal_vs(g)
         nc.sync.dma_start(out=og_sb[:], in_=og[0].rearrange("(h p) e -> p h e", p=P))
 
         for g in range(2):
             for h in range(2):
                 scores(h, g)
+        nc.gpsimd.tensor_scalar(bias_sb[:], pos_wide[0][:], slope_col[:, 1:2], 0.0, ALU.mult, ALU.add)
+        nc.scalar.copy(out=a_sb[:], in_=bank["a_ps10"][:])
+        nc.gpsimd.tensor_tensor(s_sb[1][:, slots(0)], a_sb[:], bias_sb[:], ALU.add)
+        gather_vs(3)
+        for g in range(2):
+            deal_vs(g)
         for g in range(2):
             gather_v(0, g, 0)
             turn_v(0, g)
         add_bias(0, 0)
-        add_bias(1, 0)
         add_bias(0, 1)
-        row_max(0)
         add_bias(1, 1)
+        row_max(0)
         row_max(1)
         for g in range(2):
             nc.vector.tensor_copy(v_g[1, g], v_raw[1][:].indirect(half_list(g)))
@@ -260,8 +263,6 @@ def tile_attend_soft_alibi_gate_srtq256n1024t2048_kernel(tc, qT, k_words, k_scal
         turn_v(1, 1)
         exp_and_turn(1, 1)
         store_v(1)
-        for h in range(2):
-            nc.scalar.activation(out=total[:, h : h + 1], in_=half_sum[:, h, 0:1], func=ACT.Identity, bias=half_sum[:, h, 1:2])
         nc.scalar.activation(out=gate_tanh[:], in_=og_sb[:], func=ACT.Tanh, scale=0.5)
         nc.scalar.activation(out=gate[:], in_=gate_tanh[:], func=ACT.Copy, scale=0.5, bias=0.5)
 
@@ -271,6 +272,7 @@ def tile_attend_soft_alibi_gate_srtq256n1024t2048_kernel(tc, qT, k_words, k_scal
         quantize_w(0, slice(0, 2))
         weigh(1, 0)
         quantize_v(1)
+        nc.vector.tensor_tensor(total[:], half_sum[:, :, 0], half_sum[:, :, 1], ALU.add)
         weigh(1, 1)
         nc.vector.reciprocal(inv[:], total[:])
         y_first = new_bank("y_ps0", [P, DV])

@@ -24,6 +24,7 @@ LANES = 16
 KB = 1024
 PREFIX = T - PASS
 QUARTER = N // 4
+ZERO_CUT = 1280
 BANK_OF = {"pos_ps0": 0, "pt_ps00": 0, "y_ps2": 0,
            "pos_ps1": 1, "pt_ps01": 1,
            "a_ps00": 2, "vt_ps0": 2,
@@ -198,10 +199,11 @@ def tile_attend_soft_alibi_gate_srtq256n1024t2048_kernel(tc, qT, k_words, k_scal
             nc.sync.dma_start(out=out[0, block(h), features], in_=result[:])
 
         nc.vector.memset(pos_win[0 : P - 1, :], 0.0)
+        nc.vector.memset(vs_win[0 : P - 1, ZERO_CUT:T], 0.0)
         nc.gpsimd.memset(ks_win[:].bitcast(I32), 0)
         nc.gpsimd.memset(ident[:], 0.0)
         nc.scalar.activation(out=slope_rows[0 : P - 2, :], in_=ident[0 : P - 2, :], func=ACT.Copy)
-        nc.gpsimd.memset(vs_win[0 : P - 1, :], 0.0)
+        nc.gpsimd.memset(vs_win[0 : P - 1, 0:ZERO_CUT], 0.0)
         make_identity(nc, ident[:], nomemset=True)
 
         nc.sync.dma_start(offsets[:], offs)

@@ -24,7 +24,7 @@ LANES = 16
 KB = 1024
 PREFIX = T - PASS
 QUARTER = N // 4
-ZERO_CUT = 1280
+ZERO_CUT = 1024
 BANK_OF = {"pos_ps0": 0, "pt_ps00": 0, "y_ps2": 0,
            "pos_ps1": 1, "pt_ps01": 1,
            "a_ps00": 2, "vt_ps0": 2,
@@ -203,7 +203,8 @@ def tile_attend_soft_alibi_gate_srtq256n1024t2048_kernel(tc, qT, k_words, k_scal
         nc.gpsimd.memset(ks_win[:].bitcast(I32), 0)
         nc.gpsimd.memset(ident[:], 0.0)
         nc.scalar.activation(out=slope_rows[0 : P - 2, :], in_=ident[0 : P - 2, :], func=ACT.Copy)
-        nc.gpsimd.memset(vs_win[0 : P - 1, 0:ZERO_CUT], 0.0)
+        for half in range(2):
+            nc.gpsimd.memset(vs_win[0 : P - 1, half * ZERO_CUT // 2 : (half + 1) * ZERO_CUT // 2], 0.0)
         make_identity(nc, ident[:], nomemset=True)
 
         nc.sync.dma_start(offsets[:], offs)

from contextlib import ExitStack

import concourse.mybir as mybir
from concourse.masks import make_identity

N, T, D, DV, NQ = 1024, 2048, 512, 256, 256
FLOPS = 2 * NQ * N * D + 2 * NQ * N * DV

F32 = mybir.dt.float32
BF16 = mybir.dt.bfloat16
I32 = mybir.dt.int32
U32 = mybir.dt.uint32
U16 = mybir.dt.uint16
U8 = mybir.dt.uint8
FP8X4 = mybir.dt.float8_e4m3fn_x4
ALU = mybir.AluOpType
ACT = mybir.ActivationFunctionType
AX = mybir.AxisListType

P = 128
PASS = 512
WORD = 4
LANES = 16
KB = 1024
PREFIX = T - PASS
QUARTER = N // 4
ZERO_CUT = 1024
BANK_OF = {"pos_ps0": 0, "pt_ps00": 0, "y_ps2": 0,
           "pos_ps1": 1, "pt_ps01": 1,
           "a_ps00": 2, "vt_ps0": 2,
           "a_ps01": 3, "y_ps0": 3,
           "wide_ps0": 4, "pt_ps10": 4,
           "wide_ps1": 5, "pt_ps11": 5,
           "slope_ps": 6, "a_ps10": 6, "vt_ps1": 6,
           "a_ps11": 7, "y_ps1": 7}


def tile_attend_soft_alibi_gate_srtq256n1024t2048_kernel(tc, qT, k_words, k_scales, vT, vs, pos, slope, og, offs, out):
    nc = tc.nc
    with ExitStack() as ctx:
        keep = ctx.enter_context(tc.tile_pool(name="keep", bufs=1))
        shared = ctx.enter_context(tc.tile_pool(name="shared", bufs=1))
        psum = ctx.enter_context(tc.psum_pool(name="psum", bufs=1))

        def kept(name, shape, dtype):
            return keep.tile(shape, dtype, name=name, align_bytes=64)

        def placed(name, shape, dtype, kib):
            return shared.tile(shape, dtype, name=name, align_bytes=64, offset=int(kib * KB))

        kw_win = placed("kw_win", [P, T], I32, 0)
        og_sb = placed("og_sb", [P, 2, DV], F32, 0)
        q_raw = placed("q_raw", [P, WORD, NQ], F32, 8)
        kw_g = [kept("kw_g0", [P, PASS], U32), placed("kw_g1", [P, PASS], U32, 8)]
        pos_g = [kept(f"pos_g{g}", [P, PASS], F32) for g in range(2)]
        q_bf = kept("q_bf", [P, NQ, WORD], BF16)
        pos_col = [placed(f"pos_col{g}", [P, WORD], F32, 16 + 2 * g) for g in range(2)]
        vs_g = [kept("vs_g0", [P, PASS], F32), placed("vs_g1", [P, PASS], F32, 18)]
        a_sb = kept("a_sb", [P, PASS], F32)
        bias_sb = kept("bias_sb", [P, PASS], F32)
        pos_wide = [kept("pos_wide0", [P, PASS], F32), placed("pos_wide1", [P, PASS], F32, 34)]
        v_g = {(0, 0): placed("v_g00", [P, PASS], BF16, 22)[:], (0, 1): kept("v_g01", [P, PASS], BF16)[:],
               (1, 0): placed("v_g10", [P, PASS], BF16, 34)[:], (1, 1): placed("v_g11", [P, PASS], BF16, 35)[:]}
        p_sb = {(h, g): placed(f"p_sb{h}{g}", [P, WORD, P], F32, 22 + 4 * h + 2 * g) for h in range(2) for g in range(2)}
        v_bf = [placed("v_bf0", [P, 2, P, WORD], BF16, 22), placed("v_bf1", [P, 2, P, WORD], BF16, 26)]
        gate_tanh = placed("gate_tanh", [P, 2, DV], F32, 28)
        total = placed("total", [P, 2], F32, 24)
        vs_col = [placed(f"vs_col{g}", [P, WORD], F32, 4 + g) for g in range(2)]
        res = [placed("res0", [P, DV], F32, 5), kept("res1", [P, P], F32), kept("res2", [P, P], F32)]

        v_raw = [kept(f"v_raw{f}", [P, T], F32) for f in range(2)]
        s_sb = [kept(f"s_sb{h}", [P, N], F32) for h in range(2)]
        inv = kept("inv", [P, 2], F32)
        offsets = kept("offsets", [P, N // LANES], U16)
        ident = kept("ident", [P, P], F32)
        slope_rows = kept("slope_rows", [P, P], F32)
        ks_win = kept("ks_win", [P, T], U8)
        pos_win = kept("pos_win", [P, T], F32)
        vs_win = kept("vs_win", [P, T], F32)
        slope_col = kept("slope_col", [P, 2], F32)
        v_codes = [kept(f"v_codes{f}", [P, 2, P], U32) for f in range(2)]
        ks_g = kept("ks_g", [P, N], U8)
        v_scales = [kept(f"v_scales{f}", [P, 2, P], U8) for f in range(2)]
        q_codes = kept("q_codes", [P, NQ], U32)
        q_scales = kept("q_scales", [P, NQ], U8)
        neg_max = [kept(f"neg_max{h}", [P, 1], F32) for h in range(2)]
        w_bf = [kept(f"w_bf{h}", [P, 2, P, WORD], BF16) for h in range(2)]
        w_codes = [kept(f"w_codes{h}", [P, 2, P], U32) for h in range(2)]
        w_scales = [kept(f"w_scales{h}", [P, 2, P], U8) for h in range(2)]
        half_sum = kept("half_sum", [P, 2, 2], F32)
        gate = kept("gate", [P, 2, DV], F32)
        bank = {}

        def new_bank(key, shape):
            bank[key] = psum.tile(shape, F32, name=key, tag=f"bank{BANK_OF[key]}")
            return bank[key]

        def block(index):
            return slice(index * P, (index + 1) * P)

        def slots(g):
            return slice(g * PASS, (g + 1) * PASS)

        def entries(first, end):
            return offsets[:, first // LANES : end // LANES]

        def half_list(g):
            return entries(g * PASS, (g + 1) * PASS)

        def load_scales():
            ks_hbm = k_scales[0].bitcast(I32)
            for quad in range(4):
                nc.scalar.dma_start(out=ks_win[32 * quad : 32 * quad + 4, :].bitcast(I32), in_=ks_hbm[4 * quad : 4 * quad + 4, :])

        def load_keys(columns):
            nc.sync.dma_start(out=kw_win[:, columns], in_=k_words[0].rearrange("p t r -> p (t r)").bitcast(I32)[:, columns])

        def gather_keys(g, end):
            nc.vector.tensor_copy(kw_g[g][:], kw_win[:, 0:end].bitcast(U32).indirect(half_list(g)))

        def gather_vs(quarter):
            g, first = divmod(quarter * QUARTER, PASS)
            nc.scalar.activation(out=vs_g[g][:, first : first + QUARTER], in_=vs_win[:].indirect(entries(quarter * QUARTER, (quarter + 1) * QUARTER)), func=ACT.Copy)

        def load_v(f):
            nc.sync.dma_start(out=v_raw[f][:], in_=vT[block(f), :])

        def deal_vs(g):
            nc.sync.dma_start(out=vs_col[g][:], in_=vs_g[g][P - 1 : P, :])

        def gather_pos(g):
            nc.scalar.activation(out=pos_g[g][:], in_=pos_win[:].indirect(half_list(g)), func=ACT.Copy)

        def turn_pos(g):
            ps = new_bank(f"pos_ps{g}", [P, WORD, P])
            for j in range(WORD):
                nc.tensor.transpose(ps[:, j, :], pos_g[g][:, block(j)], ident[:])

        def spread_pos(g):
            nc.scalar.copy(out=pos_col[g][:], in_=bank[f"pos_ps{g}"][:, :, P - 1])
            ps = new_bank(f"wide_ps{g}", [P, WORD, P])
            for j in range(WORD):
                nc.tensor.transpose(ps[:, j, :], pos_col[g][:, j : j + 1].to_broadcast([P, P]), ident[:])

        def store_pos(g):
            nc.scalar.copy(out=pos_wide[g][:], in_=bank[f"wide_ps{g}"][:].rearrange("p j s -> p (j s)"))

        def scores(h, g):
            nc.tensor.matmul_mx(out=new_bank(f"a_ps{h}{g}", [P, PASS])[:], lhsT=q_codes[:, block(h)].bitcast(FP8X4), lhsT_scale=q_scales[:, block(h)],
                                rhs=kw_g[g][:].bitcast(FP8X4), rhs_scale=ks_g[:, slots(g)], start=True, stop=True)

        def add_bias(h, g):
            nc.vector.scalar_tensor_tensor(out=s_sb[h][:, slots(g)], in0=pos_wide[g][:], scalar=slope_col[:, h : h + 1],
                                           in1=bank[f"a_ps{h}{g}"][:], op0=ALU.mult, op1=ALU.add)

        def row_max(h):
            nc.vector.tensor_reduce(out=neg_max[h][:], in_=s_sb[h][:], axis=AX.X, op=ALU.max, negate=True)

        def exp_and_turn(h, g):
            nc.scalar.activation(out=p_sb[h, g][:].rearrange("p t s -> p s t"), in_=s_sb[h][:, slots(g)].rearrange("p (s t) -> p s t", t=WORD),
                                 func=ACT.Exp, bias=neg_max[h][:], accum_out=half_sum[:, h, g : g + 1])
            ps = new_bank(f"pt_ps{h}{g}", [P, WORD, P])
            for t in range(WORD):
                nc.tensor.transpose(ps[:, t, :], p_sb[h, g][:, t, :], ident[:])

        def weigh(h, g):
            nc.vector.tensor_tensor(w_bf[h][:, g, :, :], bank[f"pt_ps{h}{g}"][:].rearrange("p t q -> p q t"),
                                    vs_col[g][:].unsqueeze(1).to_broadcast([P, P, WORD]), ALU.mult)

        def quantize_w(h, halves):
            nc.vector.quantize_mx(out=w_codes[h][:, halves, :].rearrange("p g q -> p (g q)").bitcast(FP8X4),
                                  scales=w_scales[h][:, halves, :].rearrange("p g q -> p (g q)"),
                                  in_=w_bf[h][:, halves, :, :].rearrange("p g q t -> p (g q t)"))

        def gather_v(f, g, first):
            nc.scalar.activation(out=v_g[f, g][:, first:PASS], in_=v_raw[f][:].indirect(entries(g * PASS + first, (g + 1) * PASS)), func=ACT.Copy)

        def turn_v(f, g):
            if g == 0:
                new_bank(f"vt_ps{f}", [P, 2, 2, P])
            pairs = v_g[f, g].bitcast(F32)
            for u in range(2):
                nc.tensor.transpose(bank[f"vt_ps{f}"][:, g, u, :], pairs[:, u : 2 * P : 2], ident[:])

        def store_v(f):
            nc.scalar.copy(out=v_bf[f][:].rearrange("p g c t -> p (g c t)").bitcast(F32).rearrange("p (g c u) -> p g c u", g=2, u=2),
                           in_=bank[f"vt_ps{f}"][:].rearrange("p g u c -> p g c u"))

        def quantize_v(f):
            nc.vector.quantize_mx(out=v_codes[f][:].rearrange("p g c -> p (g c)").bitcast(FP8X4), scales=v_scales[f][:].rearrange("p g c -> p (g c)"),
                                  in_=v_bf[f][:].rearrange("p g c t -> p (g c t)"))

        def product(y_ps, h, f, g):
            nc.tensor.matmul_mx(out=y_ps, lhsT=w_codes[h][:, g, :].bitcast(FP8X4), lhsT_scale=w_scales[h][:, g, :],
                                rhs=v_codes[f][:, g, :].bitcast(FP8X4), rhs_scale=v_scales[f][:, g, :], start=(g == 0), stop=(g == 1))

        def finish(y_ps, result, h, features):
            nc.vector.scalar_tensor_tensor(out=result[:], in0=y_ps[:], scalar=inv[:, h : h + 1], in1=gate[:, h, features], op0=ALU.mult, op1=ALU.mult)
            nc.sync.dma_start(out=out[0, block(h), features], in_=result[:])

        nc.vector.memset(pos_win[0 : P - 1, :], 0.0)
        nc.vector.memset(vs_win[0 : P - 1, ZERO_CUT:T], 0.0)
        nc.gpsimd.memset(ks_win[:].bitcast(I32), 0)
        nc.gpsimd.memset(ident[:], 0.0)
        nc.scalar.activation(out=slope_rows[0 : P - 2, :], in_=ident[0 : P - 2, :], func=ACT.Copy)
        for half in range(2):
            nc.gpsimd.memset(vs_win[0 : P - 1, half * ZERO_CUT // 2 : (half + 1) * ZERO_CUT // 2], 0.0)
        make_identity(nc, ident[:], nomemset=True)

        nc.sync.dma_start(offsets[:], offs)
        nc.sync.dma_start(out=pos_win[P - 1 : P, :], in_=pos[0:1, :])
        load_scales()
        nc.sync.dma_start(out=vs_win[P - 1 : P, :], in_=vs[0:1, :])
        nc.sync.dma_start(out=q_raw[:], in_=qT[0].rearrange("(p j) w -> p j w", j=WORD))
        nc.sync.dma_start(out=slope_rows[P - 2 : P, :], in_=slope[0].rearrange("(h p) o -> h (p o)", p=P))
        load_keys(slice(0, PREFIX))
        load_keys(slice(PREFIX, T))
        load_v(0)
        load_v(1)

        nc.vector.tensor_copy(pos_g[0][:], pos_win[:].indirect(half_list(0)))
        gather_pos(1)
        nc.vector.tensor_copy(ks_g[:], ks_win[:].indirect(offsets[:]))
        gather_vs(0)
        gather_vs(1)
        for g in range(2):
            turn_pos(g)
        nc.tensor.transpose(new_bank("slope_ps", [P, P])[:], slope_rows[:], ident[:])
        gather_keys(0, PREFIX)
        spread_pos(0)
        spread_pos(1)
        nc.scalar.copy(out=slope_col[:], in_=bank["slope_ps"][:, P - 2 : P])
        for h in range(2):
            nc.gpsimd.tensor_scalar(q_bf[:, block(h), :], q_raw[:, :, block(h)].rearrange("p j w -> p w j"), 1.0, 0.0, ALU.mult, ALU.add)
        nc.vector.quantize_mx(out=q_codes[:].bitcast(FP8X4), scales=q_scales[:], in_=q_bf[:].rearrange("p w j -> p (w j)"))
        gather_keys(1, T)
        nc.vector.tensor_copy(vs_g[1][:, 0:QUARTER], vs_win[:].indirect(entries(PASS, PASS + QUARTER)))
        store_pos(0)
        store_pos(1)
        nc.sync.dma_start(out=og_sb[:], in_=og[0].rearrange("(h p) e -> p h e", p=P))

        for g in range(2):
            for h in range(2):
                scores(h, g)
        nc.gpsimd.tensor_scalar(bias_sb[:], pos_wide[0][:], slope_col[:, 1:2], 0.0, ALU.mult, ALU.add)
        nc.scalar.copy(out=a_sb[:], in_=bank["a_ps10"][:])
        nc.gpsimd.tensor_tensor(s_sb[1][:, slots(0)], a_sb[:], bias_sb[:], ALU.add)
        gather_vs(3)
        for g in range(2):
            deal_vs(g)
        for g in range(2):
            gather_v(0, g, 0)
            turn_v(0, g)
        add_bias(0, 0)
        add_bias(0, 1)
        add_bias(1, 1)
        row_max(0)
        row_max(1)
        for g in range(2):
            nc.vector.tensor_copy(v_g[1, g], v_raw[1][:].indirect(half_list(g)))
        exp_and_turn(0, 0)
        exp_and_turn(0, 1)
        store_v(0)
        turn_v(1, 0)
        exp_and_turn(1, 0)
        turn_v(1, 1)
        exp_and_turn(1, 1)
        store_v(1)
        nc.scalar.activation(out=gate_tanh[:], in_=og_sb[:], func=ACT.Tanh, scale=0.5)
        nc.scalar.activation(out=gate[:], in_=gate_tanh[:], func=ACT.Copy, scale=0.5, bias=0.5)

        weigh(0, 0)
        weigh(0, 1)
        quantize_v(0)
        quantize_w(0, slice(0, 2))
        weigh(1, 0)
        quantize_v(1)
        nc.vector.tensor_tensor(total[:], half_sum[:, :, 0], half_sum[:, :, 1], ALU.add)
        weigh(1, 1)
        nc.vector.reciprocal(inv[:], total[:])
        y_first = new_bank("y_ps0", [P, DV])
        for f in range(2):
            for g in range(2):
                product(y_first[:, block(f)], 0, f, g)
        y_last = [new_bank(f"y_ps{1 + f}", [P, P]) for f in range(2)]
        for g in range(2):
            quantize_w(1, slice(g, g + 1))
            for f in range(2):
                product(y_last[f][:], 1, f, g)
        finish(y_first, res[0], 0, slice(0, DV))
        finish(y_last[0], res[1], 1, block(0))
        finish(y_last[1], res[2], 1, block(1))
